import numpy as np
import ml_dtypes


def mxq(x, axis, fmt="e4m3"):
    dtype, down = {"e4m3": (ml_dtypes.float8_e4m3fn, 7), "e5m2": (ml_dtypes.float8_e5m2, 14)}[fmt]
    v = np.moveaxis(np.asarray(x, np.float32).astype(ml_dtypes.bfloat16).astype(np.float64), axis, -1)
    blocks = v.reshape(v.shape[:-1] + (-1, 32))
    amax = np.abs(blocks).max(-1, keepdims=True)
    byte = np.maximum(np.where(amax > 0, np.frexp(amax)[1] - 1 + 127, 0) - down, 1)
    scale = np.exp2(byte - 127.0)
    codes = (blocks / scale).astype(np.float32).astype(dtype).astype(np.float64)
    return np.moveaxis((codes * scale).reshape(v.shape), -1, axis)


WIDE = False


def mx_kscale(k):
    if not WIDE:
        return np.ones(k)
    levels = np.array([10, -10, 5, -5, 0])
    if k % 512:
        return np.exp2(np.random.permutation(np.resize(levels, k // 32))).repeat(32)
    a = np.empty((k // 512, 16))
    for p in range(k // 512):
        a[p, :8] = np.random.permutation(np.resize(levels, 8))
        for g in range(8):
            far = levels[np.abs(levels - a[p, g]) >= 10]
            a[p, g + 8] = far[np.random.randint(len(far))]
    return np.exp2(a.ravel()).repeat(32)


def f64(x):
    return np.asarray(x).astype(np.float64)


def striped(idx):
    return np.tile(np.asarray(idx).reshape(-1, 16).T, (8, 1)).astype(np.uint16)


def unstriped(offs):
    return offs[:16].T.reshape(-1).astype(np.int64)


B, N, T, D, DV, NQ = 1, 1024, 4096, 512, 256, 128


def setup_inputs():
    n = np.random.standard_normal
    idx = np.random.permutation(T)[:B * N]
    s = mx_kscale(D)[:, None]
    u = np.ones(T)
    u[idx] = mx_kscale(B * N)
    r = np.random.uniform(0.5, 2.0, T)
    rk = np.random.uniform(0.5, 2.0, T)
    k = n((D, T)) / s / rk
    v = n((DV, T)) / (u * r)
    return {
        "qT": (n((B, D, NQ)) * s * (0.80 / np.sqrt(D))).astype(np.float32),
        "kT": k.astype(np.float32),
        "vT": v.astype(np.float32),
        "ks": np.tile(rk, (128, 1)).astype(np.float32),
        "vs": np.tile(u * r, (128, 1)).astype(np.float32),
        "sink": (2.0 + 3.0 * n((B, NQ, 1))).astype(np.float32),
        "offs": striped(idx),
    }


def reference(qT, kT, vT, ks, vs, sink, offs):
    idx = unstriped(offs)
    k = f64(kT)
    v = f64(vT)
    pick = lambda x: x[:, idx].reshape(x.shape[0], B, N).transpose(1, 0, 2)
    q = f64(qT)
    score = mxq(q, 1, "e4m3").transpose(0, 2, 1) @ mxq(pick(k), 1, "e4m3")
    score = score * pick(f64(ks))[:, :1, :]
    m = np.maximum(score.max(-1, keepdims=True), f64(sink))
    p = np.exp(score - m)
    total = p.sum(-1, keepdims=True) + np.exp(f64(sink) - m)
    w = p * pick(f64(vs))[:, :1, :]
    y = mxq(w, 2, "e4m3") @ mxq(pick(v).transpose(0, 2, 1), 1, "e4m3")
    y = y / total
    return y

@@ -1,0 +1,177 @@
+from contextlib import ExitStack
+
+import concourse.mybir as mybir
+from concourse.masks import make_identity
+
+D, T, N, DV, NQ = 512, 4096, 1024, 256, 128
+P = 128
+PACK = 4
+HALF = 512
+
+F32 = mybir.dt.float32
+BF16 = mybir.dt.bfloat16
+U32 = mybir.dt.uint32
+U16 = mybir.dt.uint16
+U8 = mybir.dt.uint8
+FP8X4 = mybir.dt.float8_e4m3fn_x4
+MULT = mybir.AluOpType.mult
+MIN = mybir.AluOpType.min
+AX = mybir.AxisListType.X
+COPY = mybir.ActivationFunctionType.Copy
+EXP = mybir.ActivationFunctionType.Exp
+
+FLOPS = 2 * NQ * N * (D + DV)
+BYTES = 4 * (D * T + DV * T + D * NQ + 2 * T + NQ + NQ * DV) + 2 * 128 * 64
+
+
+def tile_attend_x_ks_sink_topk_kernel(tc, qT, kT, vT, ks, vs, sink, offs, out):
+    nc = tc.nc
+    with ExitStack() as ctx:
+        keep = ctx.enter_context(tc.tile_pool(name="keep", bufs=1))
+        psum = ctx.enter_context(tc.psum_pool(name="psum", bufs=2))
+
+        offsets = keep.tile([P, N // 16], U16, name="offsets")
+        nc.sync.dma_start(offsets[:], offs)
+
+        q_raw = keep.tile([P, PACK, NQ], F32, name="q_raw")
+        nc.sync.dma_start(q_raw[:], qT.rearrange("b (p t) q -> p (b t) q", t=PACK))
+        sink_col = keep.tile([P, 1], F32, name="sink_col")
+        nc.scalar.dma_start(sink_col[:], sink.rearrange("b q o -> (b q) o"))
+
+        ks_row = keep.tile([P, T], F32, name="ks_row")
+        vs_row = keep.tile([P, T], F32, name="vs_row")
+        k_rows = kT.rearrange("(p t) n -> p t n", t=PACK)
+        k_raw = [keep.tile([P, T], F32, name="k_raw%d" % t) for t in range(PACK)]
+        v_raw = [keep.tile([P, T], F32, name="v_raw%d" % j, tag="v_raw%d" % j, align_bytes=64) for j in range(DV // P)]
+        nc.sync.dma_start(k_raw[0][:], k_rows[:, 0, :])
+        nc.vector.memset(ks_row[:], 0.0)
+        nc.scalar.dma_start(ks_row[0:1, :], ks[0:1, :])
+        nc.vector.memset(k_raw[1][:, 0:256], 0.0)
+        nc.sync.dma_start(k_raw[1][:], k_rows[:, 1, :])
+        nc.vector.memset(vs_row[:], 0.0)
+        nc.scalar.dma_start(vs_row[0:1, :], vs[0:1, :])
+        for t in range(2, PACK):
+            nc.vector.memset(k_raw[t][:, 0:256], 0.0)
+            nc.sync.dma_start(k_raw[t][:], k_rows[:, t, :])
+        for j in range(DV // P):
+            nc.vector.memset(v_raw[j][:, 0:8], 0.0)
+            nc.sync.dma_start(v_raw[j][:], vT[j * P : (j + 1) * P, :])
+
+        ident = keep.tile([P, P], F32, name="ident")
+        make_identity(nc, ident[:])
+        warm = keep.tile([P, 1], F32, name="warm")
+        nc.scalar.activation(warm[:], ident[:, 0:1], EXP)
+
+        q_bf = keep.tile([P, NQ, PACK], BF16, name="q_bf", align_bytes=64)
+        nc.scalar.copy(q_bf[:], q_raw[:].rearrange("p t q -> p q t"))
+        q_codes = keep.tile([P, NQ], U32, name="q_codes", align_bytes=64)
+        q_scales = keep.tile([P, NQ], U8, name="q_scales", align_bytes=64)
+        nc.vector.quantize_mx(q_codes[:].bitcast(FP8X4), q_scales[:], q_bf[:].rearrange("p q t -> p (q t)"))
+
+        a_neg = keep.tile([P, N + 2], F32, name="a_neg")
+        nc.vector.tensor_scalar(a_neg[:, N : N + 1], sink_col[:], -1.0, None, MULT)
+
+        ks_got = keep.tile([P, N], F32, name="ks_got")
+        nc.vector.tensor_copy(ks_got[:], ks_row[:].indirect(offsets[:]))
+        vs_got = keep.tile([P, N], F32, name="vs_got")
+        nc.vector.tensor_copy(vs_got[:], vs_row[:].indirect(offsets[:]))
+
+        ks_col = keep.tile([P, 8], F32, name="ks_col")
+        ks_neg = keep.tile([P, N], F32, name="ks_neg")
+        for h in range(2):
+            turned = psum.tile([P, 4, P], F32, name="wt")
+            for c in range(4):
+                at = h * HALF + c * P
+                nc.tensor.transpose(turned[:, c, :], ks_got[:, at : at + P], ident[:])
+            nc.scalar.copy(ks_col[:, 4 * h : 4 * h + 4], turned[:, :, 0])
+        for h in range(2):
+            spread = psum.tile([P, 4, P], F32, name="sc")
+            for c in range(4):
+                nc.tensor.transpose(spread[:, c, :], ks_col[:, 4 * h + c : 4 * h + c + 1].to_broadcast([P, P]), ident[:])
+            nc.scalar.activation(ks_neg[:, h * HALF : (h + 1) * HALF], spread[:].rearrange("p c s -> p (c s)"), COPY, scale=-1.0)
+        vs_col = keep.tile([P, 8], F32, name="vs_col")
+        for g in range(2):
+            turned = psum.tile([P, 4, P], F32, name="wt")
+            for t in range(PACK):
+                nc.tensor.transpose(turned[:, t, :], vs_got[:, g * HALF + t : (g + 1) * HALF : PACK], ident[:])
+            nc.scalar.copy(vs_col[:, 4 * g : 4 * g + 4], turned[:, :, 0])
+
+        k_bf = keep.tile([P, N, PACK], BF16, name="k_bf", align_bytes=64)
+        k_codes = keep.tile([P, N], U32, name="k_codes", align_bytes=64)
+        k_scales = keep.tile([P, N], U8, name="k_scales", align_bytes=64)
+        k_got = keep.tile([P, 2, N], F32, name="k_got")
+        for t in range(2):
+            nc.vector.tensor_copy(k_got[:, t, :], k_raw[t][:].indirect(offsets[:]))
+        nc.scalar.copy(k_bf[:, :, 0:2], k_got[:].rearrange("p t n -> p n t"))
+        k_late = keep.tile([P, 2, HALF], F32, name="k_late")
+        for t in range(2, PACK):
+            nc.vector.tensor_copy(k_late[:, t - 2, :], k_raw[t][:].indirect(offsets[:, 32:64]))
+            nc.vector.tensor_copy(k_bf[:, 0:HALF, t], k_raw[t][:].indirect(offsets[:, 0:32]))
+        nc.scalar.copy(k_bf[:, HALF:N, 2:4], k_late[:].rearrange("p t n -> p n t"))
+        scores = []
+        for h in range(2):
+            s = slice(h * HALF, (h + 1) * HALF)
+            nc.vector.quantize_mx(k_codes[:, s].bitcast(FP8X4), k_scales[:, s], k_bf[:, s, :].rearrange("p n t -> p (n t)"))
+            sc = psum.tile([P, HALF], F32, name="sc")
+            nc.tensor.matmul_mx(sc[:], lhsT=q_codes[:].bitcast(FP8X4), lhsT_scale=q_scales[:],
+                                rhs=k_codes[:, s].bitcast(FP8X4), rhs_scale=k_scales[:, s], start=True, stop=True)
+            scores.append(sc)
+
+        v_got = [keep.tile([P, N], F32, name="v_got%d" % j) for j in range(DV // P)]
+        for j in range(DV // P):
+            for g in range(2):
+                nc.vector.tensor_copy(v_got[j][:, g * HALF : (g + 1) * HALF], v_raw[j][:].indirect(offsets[:, g * 32 : (g + 1) * 32]))
+
+        m_neg = keep.tile([P, 1], F32, name="m_neg")
+        for h in range(2):
+            s = slice(h * HALF, (h + 1) * HALF)
+            nc.vector.tensor_tensor(a_neg[:, s], scores[h][:], ks_neg[:, s], MULT)
+            if h == 0:
+                nc.vector.tensor_reduce(a_neg[:, N + 1 : N + 2], a_neg[:, s], AX, MIN)
+            else:
+                nc.vector.tensor_reduce(m_neg[:], a_neg[:, HALF : N + 2], AX, MIN)
+        p = keep.tile([P, 2, PACK, P], F32, name="p")
+        sums = keep.tile([P, 3], F32, name="sums")
+        for g in range(2):
+            nc.scalar.activation(p[:, g].rearrange("q t s -> q s t"),
+                                 a_neg[:, g * HALF : (g + 1) * HALF].rearrange("q (s t) -> q s t", t=PACK),
+                                 EXP, bias=m_neg[:], scale=-1.0, accum_out=sums[:, g : g + 1])
+        nc.scalar.activation(sums[:, 2:3], sink_col[:], EXP, bias=m_neg[:])
+
+        w_bf = keep.tile([P, 2, NQ, PACK], BF16, name="w_bf", tag="v_raw1", align_bytes=64)
+        w_codes = keep.tile([P, 2, NQ], U32, name="w_codes", align_bytes=64)
+        w_scales = keep.tile([P, 2, NQ], U8, name="w_scales", align_bytes=64)
+        for g in range(2):
+            turned = psum.tile([P, PACK, NQ], F32, name="wt")
+            for t in range(PACK):
+                nc.tensor.transpose(turned[:, t, :], p[:, g, t, :], ident[:])
+            nc.vector.tensor_tensor(w_bf[:, g], turned[:].rearrange("s t q -> s q t"),
+                                    vs_col[:, 4 * g : 4 * g + 4].unsqueeze(1).to_broadcast([P, NQ, PACK]), MULT)
+        nc.vector.quantize_mx(w_codes[:].rearrange("p g q -> p (g q)").bitcast(FP8X4), w_scales[:].rearrange("p g q -> p (g q)"),
+                              w_bf[:].rearrange("p g q t -> p (g q t)"))
+        total = keep.tile([P, 1], F32, name="total")
+        nc.vector.tensor_reduce(total[:], sums[:], AX, mybir.AluOpType.add)
+        inv = keep.tile([P, 1], F32, name="inv")
+        nc.vector.reciprocal(inv[:], total[:])
+
+        v_bf = [keep.tile([P, 2, P, PACK], BF16, name="v_bf%d" % j, align_bytes=64) for j in range(DV // P)]
+        v_codes = keep.tile([P, DV // P, 2, P], U32, name="v_codes", tag="v_raw1", align_bytes=64)
+        v_scales = [keep.tile([P, 2, P], U8, name="v_scales%d" % j, align_bytes=64) for j in range(DV // P)]
+        for j in range(DV // P):
+            for g in range(2):
+                turned = psum.tile([P, PACK, P], F32, name=("vt", "sc")[j])
+                for t in range(PACK):
+                    nc.tensor.transpose(turned[:, t, :], v_got[j][:, g * HALF + t : (g + 1) * HALF : PACK], ident[:])
+                nc.scalar.copy(v_bf[j][:, g], turned[:].rearrange("s t e -> s e t"))
+        for j in range(DV // P):
+            for g in range(2):
+                nc.vector.quantize_mx(v_codes[:, j, g].bitcast(FP8X4), v_scales[j][:, g], v_bf[j][:, g].rearrange("p e t -> p (e t)"))
+        y_out = out.rearrange("b q e -> (b q) e")
+        for j in range(DV // P):
+            acc = psum.tile([P, P], F32, name="acc")
+            for g in range(2):
+                nc.tensor.matmul_mx(acc[:], lhsT=w_codes[:, g].bitcast(FP8X4), lhsT_scale=w_scales[:, g],
+                                    rhs=v_codes[:, j, g].bitcast(FP8X4), rhs_scale=v_scales[j][:, g], start=(g == 0), stop=(g == 1))
+            y = keep.tile([P, P], F32, name="y%d" % j)
+            nc.scalar.activation(y[:], acc[:], COPY, scale=inv[:])
+            nc.sync.dma_start(y_out[:, j * P : (j + 1) * P], y[:])

@@ -7,6 +7,7 @@ D, T, N, DV, NQ = 512, 4096, 1024, 256, 128
 P = 128
 PACK = 4
 HALF = 512
+RUN = T // P
 
 F32 = mybir.dt.float32
 BF16 = mybir.dt.bfloat16
@@ -15,9 +16,10 @@ U16 = mybir.dt.uint16
 U8 = mybir.dt.uint8
 FP8X4 = mybir.dt.float8_e4m3fn_x4
 MULT = mybir.AluOpType.mult
-MIN = mybir.AluOpType.min
+MAX = mybir.AluOpType.max
 AX = mybir.AxisListType.X
 COPY = mybir.ActivationFunctionType.Copy
+IDENTITY = mybir.ActivationFunctionType.Identity
 EXP = mybir.ActivationFunctionType.Exp
 
 FLOPS = 2 * NQ * N * (D + DV)
@@ -28,33 +30,31 @@ def tile_attend_x_ks_sink_topk_kernel(tc, qT, kT, vT, ks, vs, sink, offs, out):
     nc = tc.nc
     with ExitStack() as ctx:
         keep = ctx.enter_context(tc.tile_pool(name="keep", bufs=1))
-        psum = ctx.enter_context(tc.psum_pool(name="psum", bufs=2))
+        psum = ctx.enter_context(tc.psum_pool(name="psum", bufs=1))
 
-        offsets = keep.tile([P, N // 16], U16, name="offsets")
-        nc.sync.dma_start(offsets[:], offs)
+        def bank(b, shape, name):
+            return psum.tile(shape, F32, name=name, tag="bank%d" % b)
 
+        def slot(shape, dtype, name, tag):
+            return keep.tile(shape, dtype, name=name, tag=tag, align_bytes=64)
+
+        k_rows = kT.rearrange("(p t) n -> p t n", t=PACK)
+        k_raw = [slot([P, T], F32, "k_raw%d" % t, "k_raw%d" % t) for t in range(PACK)]
+        v_raw = [slot([P, T], F32, "v_raw%d" % j, "v_raw%d" % j) for j in range(DV // P)]
+        ks_run = keep.tile([P, RUN], F32, name="ks_run")
+        nc.sync.dma_start(ks_run[:], ks[0:1, :].rearrange("o (p c) -> (o p) c", c=RUN))
         q_raw = keep.tile([P, PACK, NQ], F32, name="q_raw")
         nc.sync.dma_start(q_raw[:], qT.rearrange("b (p t) q -> p (b t) q", t=PACK))
+        vs_pool = keep.tile([P, T], F32, name="vs_pool")
+        nc.sync.dma_start(vs_pool[P - 1 : P, :], vs[0:1, :])
+        nc.vector.memset(vs_pool[0 : P - 1, :], 0.0)
+        offsets = keep.tile([P, N // 16], U16, name="offsets")
+        nc.sync.dma_start(offsets[:], offs)
         sink_col = keep.tile([P, 1], F32, name="sink_col")
-        nc.scalar.dma_start(sink_col[:], sink.rearrange("b q o -> (b q) o"))
-
-        ks_row = keep.tile([P, T], F32, name="ks_row")
-        vs_row = keep.tile([P, T], F32, name="vs_row")
-        k_rows = kT.rearrange("(p t) n -> p t n", t=PACK)
-        k_raw = [keep.tile([P, T], F32, name="k_raw%d" % t) for t in range(PACK)]
-        v_raw = [keep.tile([P, T], F32, name="v_raw%d" % j, tag="v_raw%d" % j, align_bytes=64) for j in range(DV // P)]
-        nc.sync.dma_start(k_raw[0][:], k_rows[:, 0, :])
-        nc.vector.memset(ks_row[:], 0.0)
-        nc.scalar.dma_start(ks_row[0:1, :], ks[0:1, :])
-        nc.vector.memset(k_raw[1][:, 0:256], 0.0)
-        nc.sync.dma_start(k_raw[1][:], k_rows[:, 1, :])
-        nc.vector.memset(vs_row[:], 0.0)
-        nc.scalar.dma_start(vs_row[0:1, :], vs[0:1, :])
-        for t in range(2, PACK):
-            nc.vector.memset(k_raw[t][:, 0:256], 0.0)
+        nc.sync.dma_start(sink_col[:], sink.rearrange("b q o -> (b q) o"))
+        for t in range(PACK):
             nc.sync.dma_start(k_raw[t][:], k_rows[:, t, :])
         for j in range(DV // P):
-            nc.vector.memset(v_raw[j][:, 0:8], 0.0)
             nc.sync.dma_start(v_raw[j][:], vT[j * P : (j + 1) * P, :])
 
         ident = keep.tile([P, P], F32, name="ident")
@@ -62,47 +62,40 @@ def tile_attend_x_ks_sink_topk_kernel(tc, qT, kT, vT, ks, vs, sink, offs, out):
         warm = keep.tile([P, 1], F32, name="warm")
         nc.scalar.activation(warm[:], ident[:, 0:1], EXP)
 
+        ks_pool = keep.tile([P, T], F32, name="ks_pool")
+        by_run = ks_pool[:].rearrange("r (p c) -> r p c", c=RUN)
+        for b in range(RUN // 4):
+            turned = bank(b % 4, [P, 4, P], "spread")
+            for c in range(4):
+                nc.tensor.transpose(turned[:, c, :], ks_run[:, 4 * b + c : 4 * b + c + 1].to_broadcast([P, P]), ident[:])
+            nc.scalar.activation(by_run[:, :, 4 * b : 4 * b + 4], turned[:].rearrange("r c p -> r p c"), COPY)
+
         q_bf = keep.tile([P, NQ, PACK], BF16, name="q_bf", align_bytes=64)
         nc.scalar.copy(q_bf[:], q_raw[:].rearrange("p t q -> p q t"))
         q_codes = keep.tile([P, NQ], U32, name="q_codes", align_bytes=64)
         q_scales = keep.tile([P, NQ], U8, name="q_scales", align_bytes=64)
         nc.vector.quantize_mx(q_codes[:].bitcast(FP8X4), q_scales[:], q_bf[:].rearrange("p q t -> p (q t)"))
-
-        a_neg = keep.tile([P, N + 2], F32, name="a_neg")
-        nc.vector.tensor_scalar(a_neg[:, N : N + 1], sink_col[:], -1.0, None, MULT)
-
-        ks_got = keep.tile([P, N], F32, name="ks_got")
-        nc.vector.tensor_copy(ks_got[:], ks_row[:].indirect(offsets[:]))
-        vs_got = keep.tile([P, N], F32, name="vs_got")
-        nc.vector.tensor_copy(vs_got[:], vs_row[:].indirect(offsets[:]))
-
-        ks_col = keep.tile([P, 8], F32, name="ks_col")
-        ks_neg = keep.tile([P, N], F32, name="ks_neg")
-        for h in range(2):
-            turned = psum.tile([P, 4, P], F32, name="wt")
-            for c in range(4):
-                at = h * HALF + c * P
-                nc.tensor.transpose(turned[:, c, :], ks_got[:, at : at + P], ident[:])
-            nc.scalar.copy(ks_col[:, 4 * h : 4 * h + 4], turned[:, :, 0])
-        for h in range(2):
-            spread = psum.tile([P, 4, P], F32, name="sc")
-            for c in range(4):
-                nc.tensor.transpose(spread[:, c, :], ks_col[:, 4 * h + c : 4 * h + c + 1].to_broadcast([P, P]), ident[:])
-            nc.scalar.activation(ks_neg[:, h * HALF : (h + 1) * HALF], spread[:].rearrange("p c s -> p (c s)"), COPY, scale=-1.0)
-        vs_col = keep.tile([P, 8], F32, name="vs_col")
-        for g in range(2):
-            turned = psum.tile([P, 4, P], F32, name="wt")
-            for t in range(PACK):
-                nc.tensor.transpose(turned[:, t, :], vs_got[:, g * HALF + t : (g + 1) * HALF : PACK], ident[:])
-            nc.scalar.copy(vs_col[:, 4 * g : 4 * g + 4], turned[:, :, 0])
+        logits = keep.tile([P, N + 1], F32, name="logits")
+        nc.vector.tensor_copy(logits[:, N : N + 1], sink_col[:])
 
         k_bf = keep.tile([P, N, PACK], BF16, name="k_bf", align_bytes=64)
         k_codes = keep.tile([P, N], U32, name="k_codes", align_bytes=64)
         k_scales = keep.tile([P, N], U8, name="k_scales", align_bytes=64)
         k_got = keep.tile([P, 2, N], F32, name="k_got")
+        vs_got = keep.tile([P, N], F32, name="vs_got")
+        nc.vector.tensor_copy(vs_got[:], vs_pool[:].indirect(offsets[:]))
         for t in range(2):
             nc.vector.tensor_copy(k_got[:, t, :], k_raw[t][:].indirect(offsets[:]))
+        ks_got = slot([P, N], F32, "ks_got", "k_raw1")
+        nc.vector.tensor_copy(ks_got[:], ks_pool[:].indirect(offsets[:]))
         nc.scalar.copy(k_bf[:, :, 0:2], k_got[:].rearrange("p t n -> p n t"))
+        vs_col = keep.tile([P, 2, PACK], F32, name="vs_col")
+        for g in range(2):
+            turned = bank(4 + g, [P, PACK, P], "vs_turned")
+            for t in range(PACK):
+                nc.tensor.transpose(turned[:, t, :], vs_got[:, g * HALF + t : (g + 1) * HALF : PACK], ident[:])
+            nc.scalar.copy(vs_col[:, g, :], turned[:, :, P - 1])
+
         k_late = keep.tile([P, 2, HALF], F32, name="k_late")
         for t in range(2, PACK):
             nc.vector.tensor_copy(k_late[:, t - 2, :], k_raw[t][:].indirect(offsets[:, 32:64]))
@@ -112,66 +105,68 @@ def tile_attend_x_ks_sink_topk_kernel(tc, qT, kT, vT, ks, vs, sink, offs, out):
         for h in range(2):
             s = slice(h * HALF, (h + 1) * HALF)
             nc.vector.quantize_mx(k_codes[:, s].bitcast(FP8X4), k_scales[:, s], k_bf[:, s, :].rearrange("p n t -> p (n t)"))
-            sc = psum.tile([P, HALF], F32, name="sc")
+            sc = bank(h, [P, HALF], "scores")
             nc.tensor.matmul_mx(sc[:], lhsT=q_codes[:].bitcast(FP8X4), lhsT_scale=q_scales[:],
                                 rhs=k_codes[:, s].bitcast(FP8X4), rhs_scale=k_scales[:, s], start=True, stop=True)
             scores.append(sc)
 
-        v_got = [keep.tile([P, N], F32, name="v_got%d" % j) for j in range(DV // P)]
-        for j in range(DV // P):
-            for g in range(2):
-                nc.vector.tensor_copy(v_got[j][:, g * HALF : (g + 1) * HALF], v_raw[j][:].indirect(offsets[:, g * 32 : (g + 1) * 32]))
-
-        m_neg = keep.tile([P, 1], F32, name="m_neg")
         for h in range(2):
             s = slice(h * HALF, (h + 1) * HALF)
-            nc.vector.tensor_tensor(a_neg[:, s], scores[h][:], ks_neg[:, s], MULT)
-            if h == 0:
-                nc.vector.tensor_reduce(a_neg[:, N + 1 : N + 2], a_neg[:, s], AX, MIN)
-            else:
-                nc.vector.tensor_reduce(m_neg[:], a_neg[:, HALF : N + 2], AX, MIN)
+            nc.vector.tensor_tensor(logits[:, s], scores[h][:], ks_got[:, s], MULT)
+        m_neg = keep.tile([P, 1], F32, name="m_neg")
+        nc.vector.tensor_reduce(m_neg[:], logits[:], AX, MAX, negate=True)
         p = keep.tile([P, 2, PACK, P], F32, name="p")
         sums = keep.tile([P, 3], F32, name="sums")
         for g in range(2):
             nc.scalar.activation(p[:, g].rearrange("q t s -> q s t"),
-                                 a_neg[:, g * HALF : (g + 1) * HALF].rearrange("q (s t) -> q s t", t=PACK),
-                                 EXP, bias=m_neg[:], scale=-1.0, accum_out=sums[:, g : g + 1])
+                                 logits[:, g * HALF : (g + 1) * HALF].rearrange("q (s t) -> q s t", t=PACK),
+                                 EXP, bias=m_neg[:], accum_out=sums[:, g : g + 1])
         nc.scalar.activation(sums[:, 2:3], sink_col[:], EXP, bias=m_neg[:])
+        terms = keep.tile([P, 3], F32, name="terms")
+        total = keep.tile([P, 1], F32, name="total")
+        nc.scalar.activation(terms[:], sums[:], IDENTITY, accum_out=total[:])
 
-        w_bf = keep.tile([P, 2, NQ, PACK], BF16, name="w_bf", tag="v_raw1", align_bytes=64)
-        w_codes = keep.tile([P, 2, NQ], U32, name="w_codes", align_bytes=64)
-        w_scales = keep.tile([P, 2, NQ], U8, name="w_scales", align_bytes=64)
+        v_got = [slot([P, N], BF16, "v_got%d" % j, "v_got%d" % j) for j in range(DV // P)]
+        for j in range(DV // P):
+            for g in range(2):
+                nc.vector.tensor_copy(v_got[j][:, g * HALF : (g + 1) * HALF], v_raw[j][:].indirect(offsets[:, g * 32 : (g + 1) * 32]))
+
+        first_bf = slot([P, 2, 2, P, PACK], BF16, "first_bf", "v_raw0")
+        first_codes = slot([P, 2, 2, P], U32, "first_codes", "v_raw1")
+        first_scales = keep.tile([P, 2, 2, P], U8, name="first_scales", align_bytes=64)
         for g in range(2):
-            turned = psum.tile([P, PACK, NQ], F32, name="wt")
+            turned = bank(2 + g, [P, PACK, NQ], "p_turned")
             for t in range(PACK):
                 nc.tensor.transpose(turned[:, t, :], p[:, g, t, :], ident[:])
-            nc.vector.tensor_tensor(w_bf[:, g], turned[:].rearrange("s t q -> s q t"),
-                                    vs_col[:, 4 * g : 4 * g + 4].unsqueeze(1).to_broadcast([P, NQ, PACK]), MULT)
-        nc.vector.quantize_mx(w_codes[:].rearrange("p g q -> p (g q)").bitcast(FP8X4), w_scales[:].rearrange("p g q -> p (g q)"),
-                              w_bf[:].rearrange("p g q t -> p (g q t)"))
-        total = keep.tile([P, 1], F32, name="total")
-        nc.vector.tensor_reduce(total[:], sums[:], AX, mybir.AluOpType.add)
-        inv = keep.tile([P, 1], F32, name="inv")
-        nc.vector.reciprocal(inv[:], total[:])
+            nc.vector.tensor_tensor(first_bf[:, 0, g], turned[:].rearrange("s t q -> s q t"),
+                                    vs_col[:, g, :].unsqueeze(1).to_broadcast([P, NQ, PACK]), MULT)
 
-        v_bf = [keep.tile([P, 2, P, PACK], BF16, name="v_bf%d" % j, align_bytes=64) for j in range(DV // P)]
-        v_codes = keep.tile([P, DV // P, 2, P], U32, name="v_codes", tag="v_raw1", align_bytes=64)
-        v_scales = [keep.tile([P, 2, P], U8, name="v_scales%d" % j, align_bytes=64) for j in range(DV // P)]
+        last_bf = keep.tile([P, 2, P, PACK], BF16, name="last_bf", align_bytes=64)
+        last_codes = keep.tile([P, 2, P], U32, name="last_codes", align_bytes=64)
+        last_scales = keep.tile([P, 2, P], U8, name="last_scales", align_bytes=64)
         for j in range(DV // P):
+            words = v_got[j][:].bitcast(F32)
             for g in range(2):
-                turned = psum.tile([P, PACK, P], F32, name=("vt", "sc")[j])
-                for t in range(PACK):
-                    nc.tensor.transpose(turned[:, t, :], v_got[j][:, g * HALF + t : (g + 1) * HALF : PACK], ident[:])
-                nc.scalar.copy(v_bf[j][:, g], turned[:].rearrange("s t e -> s e t"))
-        for j in range(DV // P):
-            for g in range(2):
-                nc.vector.quantize_mx(v_codes[:, j, g].bitcast(FP8X4), v_scales[j][:, g], v_bf[j][:, g].rearrange("p e t -> p (e t)"))
+                turned = bank(4 + (2 * j + g) % 3, [P, 2, P], "v_turned")
+                for u in range(2):
+                    nc.tensor.transpose(turned[:, u, :], words[:, g * 256 + u : (g + 1) * 256 : 2], ident[:])
+                dest = first_bf[:, 1, g] if j == 0 else last_bf[:, g]
+                nc.scalar.copy(dest.rearrange("s e t -> s (e t)").bitcast(F32).rearrange("s (e u) -> s e u", u=2),
+                               turned[:].rearrange("s u e -> s e u"))
+        nc.vector.quantize_mx(first_codes[:].rearrange("p a g q -> p (a g q)").bitcast(FP8X4),
+                              first_scales[:].rearrange("p a g q -> p (a g q)"),
+                              first_bf[:].rearrange("p a g q t -> p (a g q t)"))
+        for g in range(2):
+            nc.vector.quantize_mx(last_codes[:, g].bitcast(FP8X4), last_scales[:, g], last_bf[:, g].rearrange("p e t -> p (e t)"))
+        inv = slot([P, 1], F32, "inv", "v_got0")
+        nc.vector.reciprocal(inv[:], total[:])
         y_out = out.rearrange("b q e -> (b q) e")
         for j in range(DV // P):
-            acc = psum.tile([P, P], F32, name="acc")
+            acc = bank((7, 0)[j], [P, P], "acc")
             for g in range(2):
-                nc.tensor.matmul_mx(acc[:], lhsT=w_codes[:, g].bitcast(FP8X4), lhsT_scale=w_scales[:, g],
-                                    rhs=v_codes[:, j, g].bitcast(FP8X4), rhs_scale=v_scales[j][:, g], start=(g == 0), stop=(g == 1))
+                codes, scales = (first_codes[:, 1, g], first_scales[:, 1, g]) if j == 0 else (last_codes[:, g], last_scales[:, g])
+                nc.tensor.matmul_mx(acc[:], lhsT=first_codes[:, 0, g].bitcast(FP8X4), lhsT_scale=first_scales[:, 0, g],
+                                    rhs=codes.bitcast(FP8X4), rhs_scale=scales, start=(g == 0), stop=(g == 1))
             y = keep.tile([P, P], F32, name="y%d" % j)
             nc.scalar.activation(y[:], acc[:], COPY, scale=inv[:])
             nc.sync.dma_start(y_out[:, j * P : (j + 1) * P], y[:])

@@ -7,6 +7,7 @@ D, T, N, DV, NQ = 512, 4096, 1024, 256, 128
 P = 128
 PACK = 4
 HALF = 512
+QUARTER = 256
 RUN = T // P
 
 F32 = mybir.dt.float32
@@ -30,6 +31,7 @@ def tile_attend_x_ks_sink_topk_kernel(tc, qT, kT, vT, ks, vs, sink, offs, out):
     nc = tc.nc
     with ExitStack() as ctx:
         keep = ctx.enter_context(tc.tile_pool(name="keep", bufs=1))
+        reuse = ctx.enter_context(tc.tile_pool(name="reuse", bufs=1))
         psum = ctx.enter_context(tc.psum_pool(name="psum", bufs=1))
 
         def bank(b, shape, name):
@@ -40,7 +42,7 @@ def tile_attend_x_ks_sink_topk_kernel(tc, qT, kT, vT, ks, vs, sink, offs, out):
 
         k_rows = kT.rearrange("(p t) n -> p t n", t=PACK)
         k_raw = [slot([P, T], F32, "k_raw%d" % t, "k_raw%d" % t) for t in range(PACK)]
-        v_raw = [slot([P, T], F32, "v_raw%d" % j, "v_raw%d" % j) for j in range(DV // P)]
+        v_raw = [keep.tile([P, T], F32, name="v_raw0"), reuse.tile([P, T], F32, name="v_raw1", offset=0, align_bytes=64)]
         ks_run = keep.tile([P, RUN], F32, name="ks_run")
         nc.sync.dma_start(ks_run[:], ks[0:1, :].rearrange("o (p c) -> (o p) c", c=RUN))
         q_raw = keep.tile([P, PACK, NQ], F32, name="q_raw")
@@ -101,20 +103,22 @@ def tile_attend_x_ks_sink_topk_kernel(tc, qT, kT, vT, ks, vs, sink, offs, out):
             nc.vector.tensor_copy(k_late[:, t - 2, :], k_raw[t][:].indirect(offsets[:, 32:64]))
             nc.vector.tensor_copy(k_bf[:, 0:HALF, t], k_raw[t][:].indirect(offsets[:, 0:32]))
         nc.scalar.copy(k_bf[:, HALF:N, 2:4], k_late[:].rearrange("p t n -> p n t"))
-        scores = []
-        for h in range(2):
-            s = slice(h * HALF, (h + 1) * HALF)
+        scores = [bank(h, [P, HALF], "scores") for h in range(2)]
+        for c in range(4):
+            s = slice(c * QUARTER, (c + 1) * QUARTER)
             nc.vector.quantize_mx(k_codes[:, s].bitcast(FP8X4), k_scales[:, s], k_bf[:, s, :].rearrange("p n t -> p (n t)"))
-            sc = bank(h, [P, HALF], "scores")
-            nc.tensor.matmul_mx(sc[:], lhsT=q_codes[:].bitcast(FP8X4), lhsT_scale=q_scales[:],
+            nc.tensor.matmul_mx(scores[c // 2][:, (c % 2) * QUARTER : (c % 2 + 1) * QUARTER],
+                                lhsT=q_codes[:].bitcast(FP8X4), lhsT_scale=q_scales[:],
                                 rhs=k_codes[:, s].bitcast(FP8X4), rhs_scale=k_scales[:, s], start=True, stop=True)
-            scores.append(sc)
 
         for h in range(2):
             s = slice(h * HALF, (h + 1) * HALF)
             nc.vector.tensor_tensor(logits[:, s], scores[h][:], ks_got[:, s], MULT)
+        tops = keep.tile([P, 2], F32, name="tops")
+        nc.vector.tensor_reduce(tops[:, 0:1], logits[:, 0:HALF], AX, MAX)
+        nc.vector.tensor_reduce(tops[:, 1:2], logits[:, HALF : N + 1], AX, MAX)
         m_neg = keep.tile([P, 1], F32, name="m_neg")
-        nc.vector.tensor_reduce(m_neg[:], logits[:], AX, MAX, negate=True)
+        nc.gpsimd.tensor_scalar(m_neg[:], tops[:, 0:1], tops[:, 1:2], -1.0, MAX, MULT)
         p = keep.tile([P, 2, PACK, P], F32, name="p")
         sums = keep.tile([P, 3], F32, name="sums")
         for g in range(2):
@@ -126,47 +130,43 @@ def tile_attend_x_ks_sink_topk_kernel(tc, qT, kT, vT, ks, vs, sink, offs, out):
         total = keep.tile([P, 1], F32, name="total")
         nc.scalar.activation(terms[:], sums[:], IDENTITY, accum_out=total[:])
 
-        v_got = [slot([P, N], BF16, "v_got%d" % j, "v_got%d" % j) for j in range(DV // P)]
+        v_got = [keep.tile([P, N], BF16, name="v_got%d" % j) for j in range(DV // P)]
         for j in range(DV // P):
             for g in range(2):
                 nc.vector.tensor_copy(v_got[j][:, g * HALF : (g + 1) * HALF], v_raw[j][:].indirect(offsets[:, g * 32 : (g + 1) * 32]))
 
-        first_bf = slot([P, 2, 2, P, PACK], BF16, "first_bf", "v_raw0")
-        first_codes = slot([P, 2, 2, P], U32, "first_codes", "v_raw1")
-        first_scales = keep.tile([P, 2, 2, P], U8, name="first_scales", align_bytes=64)
+        v_bf = keep.tile([P, 2, DV, PACK], BF16, name="v_bf", align_bytes=64)
+        for j in range(DV // P):
+            words = v_got[j][:].bitcast(F32)
+            for g in range(2):
+                turned = bank(4 + 2 * j + g, [P, 2, P], "v_turned")
+                for u in range(2):
+                    nc.tensor.transpose(turned[:, u, :], words[:, g * 256 + u : (g + 1) * 256 : 2], ident[:])
+                dest = v_bf[:, g, j * P : (j + 1) * P, :].rearrange("s e t -> s (e t)").bitcast(F32)
+                nc.scalar.copy(dest.rearrange("s (e u) -> s e u", u=2), turned[:].rearrange("s u e -> s e u"))
+
+        w_bf = reuse.tile([P, 2, NQ, PACK], BF16, name="w_bf", offset=0, align_bytes=64)
+        w_codes = reuse.tile([P, 2, NQ], U32, name="w_codes", offset=2048, align_bytes=64)
+        v_codes = reuse.tile([P, 2, DV], U32, name="v_codes", offset=3072, align_bytes=64)
+        w_scales = keep.tile([P, 2, NQ], U8, name="w_scales", align_bytes=64)
+        v_scales = keep.tile([P, 2, DV], U8, name="v_scales", align_bytes=64)
         for g in range(2):
             turned = bank(2 + g, [P, PACK, NQ], "p_turned")
             for t in range(PACK):
                 nc.tensor.transpose(turned[:, t, :], p[:, g, t, :], ident[:])
-            nc.vector.tensor_tensor(first_bf[:, 0, g], turned[:].rearrange("s t q -> s q t"),
+            nc.vector.tensor_tensor(w_bf[:, g], turned[:].rearrange("s t q -> s q t"),
                                     vs_col[:, g, :].unsqueeze(1).to_broadcast([P, NQ, PACK]), MULT)
-
-        last_bf = keep.tile([P, 2, P, PACK], BF16, name="last_bf", align_bytes=64)
-        last_codes = keep.tile([P, 2, P], U32, name="last_codes", align_bytes=64)
-        last_scales = keep.tile([P, 2, P], U8, name="last_scales", align_bytes=64)
-        for j in range(DV // P):
-            words = v_got[j][:].bitcast(F32)
-            for g in range(2):
-                turned = bank(4 + (2 * j + g) % 3, [P, 2, P], "v_turned")
-                for u in range(2):
-                    nc.tensor.transpose(turned[:, u, :], words[:, g * 256 + u : (g + 1) * 256 : 2], ident[:])
-                dest = first_bf[:, 1, g] if j == 0 else last_bf[:, g]
-                nc.scalar.copy(dest.rearrange("s e t -> s (e t)").bitcast(F32).rearrange("s (e u) -> s e u", u=2),
-                               turned[:].rearrange("s u e -> s e u"))
-        nc.vector.quantize_mx(first_codes[:].rearrange("p a g q -> p (a g q)").bitcast(FP8X4),
-                              first_scales[:].rearrange("p a g q -> p (a g q)"),
-                              first_bf[:].rearrange("p a g q t -> p (a g q t)"))
-        for g in range(2):
-            nc.vector.quantize_mx(last_codes[:, g].bitcast(FP8X4), last_scales[:, g], last_bf[:, g].rearrange("p e t -> p (e t)"))
-        inv = slot([P, 1], F32, "inv", "v_got0")
+            if g == 0:
+                nc.vector.quantize_mx(v_codes[:, 0].bitcast(FP8X4), v_scales[:, 0], v_bf[:, 0].rearrange("p e t -> p (e t)"))
+        nc.vector.quantize_mx(w_codes[:, 0].bitcast(FP8X4), w_scales[:, 0], w_bf[:, 0].rearrange("p e t -> p (e t)"))
+        nc.vector.quantize_mx(v_codes[:, 1].bitcast(FP8X4), v_scales[:, 1], v_bf[:, 1].rearrange("p e t -> p (e t)"))
+        nc.vector.quantize_mx(w_codes[:, 1].bitcast(FP8X4), w_scales[:, 1], w_bf[:, 1].rearrange("p e t -> p (e t)"))
+        inv = reuse.tile([P, 1], F32, name="inv", offset=5120, align_bytes=64)
         nc.vector.reciprocal(inv[:], total[:])
-        y_out = out.rearrange("b q e -> (b q) e")
-        for j in range(DV // P):
-            acc = bank((7, 0)[j], [P, P], "acc")
-            for g in range(2):
-                codes, scales = (first_codes[:, 1, g], first_scales[:, 1, g]) if j == 0 else (last_codes[:, g], last_scales[:, g])
-                nc.tensor.matmul_mx(acc[:], lhsT=first_codes[:, 0, g].bitcast(FP8X4), lhsT_scale=first_scales[:, 0, g],
-                                    rhs=codes.bitcast(FP8X4), rhs_scale=scales, start=(g == 0), stop=(g == 1))
-            y = keep.tile([P, P], F32, name="y%d" % j)
-            nc.scalar.activation(y[:], acc[:], COPY, scale=inv[:])
-            nc.sync.dma_start(y_out[:, j * P : (j + 1) * P], y[:])
+        acc = bank(0, [P, DV], "acc")
+        for g in range(2):
+            nc.tensor.matmul_mx(acc[:], lhsT=w_codes[:, g].bitcast(FP8X4), lhsT_scale=w_scales[:, g],
+                                rhs=v_codes[:, g].bitcast(FP8X4), rhs_scale=v_scales[:, g], start=(g == 0), stop=(g == 1))
+        y = keep.tile([P, DV], F32, name="y")
+        nc.scalar.activation(y[:], acc[:], COPY, scale=inv[:])
+        nc.sync.dma_start(out.rearrange("b q e -> (b q) e"), y[:])

@@ -80,7 +80,7 @@ def tile_attend_x_ks_sink_topk_kernel(tc, qT, kT, vT, ks, vs, sink, offs, out):
         logits = keep.tile([P, N + 1], F32, name="logits")
         nc.vector.tensor_copy(logits[:, N : N + 1], sink_col[:])
 
-        k_bf = keep.tile([P, N, PACK], BF16, name="k_bf", align_bytes=64)
+        k_bf = [keep.tile([P, HALF, PACK], BF16, name="k_bf%d" % h, align_bytes=64) for h in range(2)]
         k_codes = keep.tile([P, N], U32, name="k_codes", align_bytes=64)
         k_scales = keep.tile([P, N], U8, name="k_scales", align_bytes=64)
         k_got = keep.tile([P, 2, N], F32, name="k_got")
@@ -90,7 +90,8 @@ def tile_attend_x_ks_sink_topk_kernel(tc, qT, kT, vT, ks, vs, sink, offs, out):
             nc.vector.tensor_copy(k_got[:, t, :], k_raw[t][:].indirect(offsets[:]))
         ks_got = slot([P, N], F32, "ks_got", "k_raw1")
         nc.vector.tensor_copy(ks_got[:], ks_pool[:].indirect(offsets[:]))
-        nc.scalar.copy(k_bf[:, :, 0:2], k_got[:].rearrange("p t n -> p n t"))
+        for h in range(2):
+            nc.scalar.copy(k_bf[h][:, :, 0:2], k_got[:, :, h * HALF : (h + 1) * HALF].rearrange("p t n -> p n t"))
         vs_col = keep.tile([P, 2, PACK], F32, name="vs_col")
         for g in range(2):
             turned = bank(4 + g, [P, PACK, P], "vs_turned")
@@ -98,31 +99,34 @@ def tile_attend_x_ks_sink_topk_kernel(tc, qT, kT, vT, ks, vs, sink, offs, out):
                 nc.tensor.transpose(turned[:, t, :], vs_got[:, g * HALF + t : (g + 1) * HALF : PACK], ident[:])
             nc.scalar.copy(vs_col[:, g, :], turned[:, :, P - 1])
 
-        k_late = keep.tile([P, 2, HALF], F32, name="k_late")
+        k_late = [keep.tile([P, 2, QUARTER], BF16, name="k_late%d" % c) for c in range(2)]
+        nc.vector.tensor_copy(k_bf[0][:, :, 2], k_raw[2][:].indirect(offsets[:, 0:32]))
         for t in range(2, PACK):
-            nc.vector.tensor_copy(k_late[:, t - 2, :], k_raw[t][:].indirect(offsets[:, 32:64]))
-            nc.vector.tensor_copy(k_bf[:, 0:HALF, t], k_raw[t][:].indirect(offsets[:, 0:32]))
-        nc.scalar.copy(k_bf[:, HALF:N, 2:4], k_late[:].rearrange("p t n -> p n t"))
+            for c in range(2):
+                nc.vector.tensor_copy(k_late[c][:, t - 2, :], k_raw[t][:].indirect(offsets[:, 32 + 16 * c : 48 + 16 * c]))
+        nc.vector.tensor_copy(k_bf[0][:, :, 3], k_raw[3][:].indirect(offsets[:, 0:32]))
+        for c in range(2):
+            nc.scalar.copy(k_bf[1][:, c * QUARTER : (c + 1) * QUARTER, 2:4], k_late[c][:].rearrange("p t n -> p n t"))
         scores = [bank(h, [P, HALF], "scores") for h in range(2)]
-        for c in range(4):
+        for c in (2, 3, 0, 1):
             s = slice(c * QUARTER, (c + 1) * QUARTER)
-            nc.vector.quantize_mx(k_codes[:, s].bitcast(FP8X4), k_scales[:, s], k_bf[:, s, :].rearrange("p n t -> p (n t)"))
-            nc.tensor.matmul_mx(scores[c // 2][:, (c % 2) * QUARTER : (c % 2 + 1) * QUARTER],
-                                lhsT=q_codes[:].bitcast(FP8X4), lhsT_scale=q_scales[:],
+            within = slice((c % 2) * QUARTER, (c % 2 + 1) * QUARTER)
+            nc.vector.quantize_mx(k_codes[:, s].bitcast(FP8X4), k_scales[:, s], k_bf[c // 2][:, within, :].rearrange("p n t -> p (n t)"))
+            nc.tensor.matmul_mx(scores[c // 2][:, within], lhsT=q_codes[:].bitcast(FP8X4), lhsT_scale=q_scales[:],
                                 rhs=k_codes[:, s].bitcast(FP8X4), rhs_scale=k_scales[:, s], start=True, stop=True)
 
-        for h in range(2):
+        for h in (1, 0):
             s = slice(h * HALF, (h + 1) * HALF)
             nc.vector.tensor_tensor(logits[:, s], scores[h][:], ks_got[:, s], MULT)
         tops = keep.tile([P, 2], F32, name="tops")
-        nc.vector.tensor_reduce(tops[:, 0:1], logits[:, 0:HALF], AX, MAX)
         nc.vector.tensor_reduce(tops[:, 1:2], logits[:, HALF : N + 1], AX, MAX)
+        nc.vector.tensor_reduce(tops[:, 0:1], logits[:, 0:HALF], AX, MAX)
         m_neg = keep.tile([P, 1], F32, name="m_neg")
         nc.gpsimd.tensor_scalar(m_neg[:], tops[:, 0:1], tops[:, 1:2], -1.0, MAX, MULT)
-        p = keep.tile([P, 2, PACK, P], F32, name="p")
+        p = [keep.tile([P, PACK, P], F32, name="p%d" % g) for g in range(2)]
         sums = keep.tile([P, 3], F32, name="sums")
         for g in range(2):
-            nc.scalar.activation(p[:, g].rearrange("q t s -> q s t"),
+            nc.scalar.activation(p[g][:].rearrange("q t s -> q s t"),
                                  logits[:, g * HALF : (g + 1) * HALF].rearrange("q (s t) -> q s t", t=PACK),
                                  EXP, bias=m_neg[:], accum_out=sums[:, g : g + 1])
         nc.scalar.activation(sums[:, 2:3], sink_col[:], EXP, bias=m_neg[:])
@@ -130,19 +134,19 @@ def tile_attend_x_ks_sink_topk_kernel(tc, qT, kT, vT, ks, vs, sink, offs, out):
         total = keep.tile([P, 1], F32, name="total")
         nc.scalar.activation(terms[:], sums[:], IDENTITY, accum_out=total[:])
 
-        v_got = [keep.tile([P, N], BF16, name="v_got%d" % j) for j in range(DV // P)]
+        v_got = [slot([P, N], BF16, "v_got0", "k_raw1"), keep.tile([P, N], BF16, name="v_got1")]
         for j in range(DV // P):
             for g in range(2):
                 nc.vector.tensor_copy(v_got[j][:, g * HALF : (g + 1) * HALF], v_raw[j][:].indirect(offsets[:, g * 32 : (g + 1) * 32]))
 
-        v_bf = keep.tile([P, 2, DV, PACK], BF16, name="v_bf", align_bytes=64)
+        v_bf = [keep.tile([P, DV, PACK], BF16, name="v_bf%d" % g, align_bytes=64) for g in range(2)]
         for j in range(DV // P):
             words = v_got[j][:].bitcast(F32)
             for g in range(2):
                 turned = bank(4 + 2 * j + g, [P, 2, P], "v_turned")
                 for u in range(2):
                     nc.tensor.transpose(turned[:, u, :], words[:, g * 256 + u : (g + 1) * 256 : 2], ident[:])
-                dest = v_bf[:, g, j * P : (j + 1) * P, :].rearrange("s e t -> s (e t)").bitcast(F32)
+                dest = v_bf[g][:, j * P : (j + 1) * P, :].rearrange("s e t -> s (e t)").bitcast(F32)
                 nc.scalar.copy(dest.rearrange("s (e u) -> s e u", u=2), turned[:].rearrange("s u e -> s e u"))
 
         w_bf = reuse.tile([P, 2, NQ, PACK], BF16, name="w_bf", offset=0, align_bytes=64)
@@ -153,14 +157,12 @@ def tile_attend_x_ks_sink_topk_kernel(tc, qT, kT, vT, ks, vs, sink, offs, out):
         for g in range(2):
             turned = bank(2 + g, [P, PACK, NQ], "p_turned")
             for t in range(PACK):
-                nc.tensor.transpose(turned[:, t, :], p[:, g, t, :], ident[:])
+                nc.tensor.transpose(turned[:, t, :], p[g][:, t, :], ident[:])
             nc.vector.tensor_tensor(w_bf[:, g], turned[:].rearrange("s t q -> s q t"),
                                     vs_col[:, g, :].unsqueeze(1).to_broadcast([P, NQ, PACK]), MULT)
-            if g == 0:
-                nc.vector.quantize_mx(v_codes[:, 0].bitcast(FP8X4), v_scales[:, 0], v_bf[:, 0].rearrange("p e t -> p (e t)"))
-        nc.vector.quantize_mx(w_codes[:, 0].bitcast(FP8X4), w_scales[:, 0], w_bf[:, 0].rearrange("p e t -> p (e t)"))
-        nc.vector.quantize_mx(v_codes[:, 1].bitcast(FP8X4), v_scales[:, 1], v_bf[:, 1].rearrange("p e t -> p (e t)"))
-        nc.vector.quantize_mx(w_codes[:, 1].bitcast(FP8X4), w_scales[:, 1], w_bf[:, 1].rearrange("p e t -> p (e t)"))
+        for g in range(2):
+            nc.vector.quantize_mx(w_codes[:, g].bitcast(FP8X4), w_scales[:, g], w_bf[:, g].rearrange("p q t -> p (q t)"))
+            nc.vector.quantize_mx(v_codes[:, g].bitcast(FP8X4), v_scales[:, g], v_bf[g][:].rearrange("p e t -> p (e t)"))
         inv = reuse.tile([P, 1], F32, name="inv", offset=5120, align_bytes=64)
         nc.vector.reciprocal(inv[:], total[:])
         acc = bank(0, [P, DV], "acc")

@@ -52,8 +52,9 @@ def tile_attend_x_ks_sink_topk_kernel(tc, qT, kT, vT, ks, vs, sink, offs, out):
         nc.vector.memset(vs_pool[0 : P - 1, :], 0.0)
         offsets = keep.tile([P, N // 16], U16, name="offsets")
         nc.sync.dma_start(offsets[:], offs)
-        sink_col = keep.tile([P, 1], F32, name="sink_col")
-        nc.sync.dma_start(sink_col[:], sink.rearrange("b q o -> (b q) o"))
+        logits = slot([P, N + 1], F32, "logits", "logits")
+        sink_col = logits[:, N : N + 1]
+        nc.sync.dma_start(sink_col, sink.rearrange("b q o -> (b q) o"))
         for t in range(PACK):
             nc.sync.dma_start(k_raw[t][:], k_rows[:, t, :])
         for j in range(DV // P):
@@ -77,11 +78,8 @@ def tile_attend_x_ks_sink_topk_kernel(tc, qT, kT, vT, ks, vs, sink, offs, out):
         q_codes = keep.tile([P, NQ], U32, name="q_codes", align_bytes=64)
         q_scales = keep.tile([P, NQ], U8, name="q_scales", align_bytes=64)
         nc.vector.quantize_mx(q_codes[:].bitcast(FP8X4), q_scales[:], q_bf[:].rearrange("p q t -> p (q t)"))
-        logits = keep.tile([P, N + 1], F32, name="logits")
-        nc.vector.tensor_copy(logits[:, N : N + 1], sink_col[:])
 
         k_bf = [keep.tile([P, HALF, PACK], BF16, name="k_bf%d" % h, align_bytes=64) for h in range(2)]
-        k_codes = keep.tile([P, N], U32, name="k_codes", align_bytes=64)
         k_scales = keep.tile([P, N], U8, name="k_scales", align_bytes=64)
         k_got = keep.tile([P, 2, N], F32, name="k_got")
         vs_got = keep.tile([P, N], F32, name="vs_got")
@@ -99,7 +97,7 @@ def tile_attend_x_ks_sink_topk_kernel(tc, qT, kT, vT, ks, vs, sink, offs, out):
                 nc.tensor.transpose(turned[:, t, :], vs_got[:, g * HALF + t : (g + 1) * HALF : PACK], ident[:])
             nc.scalar.copy(vs_col[:, g, :], turned[:, :, P - 1])
 
-        k_late = [keep.tile([P, 2, QUARTER], BF16, name="k_late%d" % c) for c in range(2)]
+        k_late = [slot([P, 2, QUARTER], BF16, "k_late%d" % c, "k_late%d" % c) for c in range(2)]
         nc.vector.tensor_copy(k_bf[0][:, :, 2], k_raw[2][:].indirect(offsets[:, 0:32]))
         for t in range(2, PACK):
             for c in range(2):
@@ -107,29 +105,27 @@ def tile_attend_x_ks_sink_topk_kernel(tc, qT, kT, vT, ks, vs, sink, offs, out):
         nc.vector.tensor_copy(k_bf[0][:, :, 3], k_raw[3][:].indirect(offsets[:, 0:32]))
         for c in range(2):
             nc.scalar.copy(k_bf[1][:, c * QUARTER : (c + 1) * QUARTER, 2:4], k_late[c][:].rearrange("p t n -> p n t"))
-        scores = [bank(h, [P, HALF], "scores") for h in range(2)]
+        scores = [bank(c, [P, QUARTER], "scores") for c in range(4)]
         for c in (2, 3, 0, 1):
             s = slice(c * QUARTER, (c + 1) * QUARTER)
             within = slice((c % 2) * QUARTER, (c % 2 + 1) * QUARTER)
-            nc.vector.quantize_mx(k_codes[:, s].bitcast(FP8X4), k_scales[:, s], k_bf[c // 2][:, within, :].rearrange("p n t -> p (n t)"))
-            nc.tensor.matmul_mx(scores[c // 2][:, within], lhsT=q_codes[:].bitcast(FP8X4), lhsT_scale=q_scales[:],
-                                rhs=k_codes[:, s].bitcast(FP8X4), rhs_scale=k_scales[:, s], start=True, stop=True)
+            k_codes = slot([P, QUARTER], U32, "k_codes", ("k_late%d" if c < 2 else "k_codes%d") % c)
+            nc.vector.quantize_mx(k_codes[:].bitcast(FP8X4), k_scales[:, s], k_bf[c // 2][:, within, :].rearrange("p n t -> p (n t)"))
+            nc.tensor.matmul_mx(scores[c][:], lhsT=q_codes[:].bitcast(FP8X4), lhsT_scale=q_scales[:],
+                                rhs=k_codes[:].bitcast(FP8X4), rhs_scale=k_scales[:, s], start=True, stop=True)
 
-        for h in (1, 0):
-            s = slice(h * HALF, (h + 1) * HALF)
-            nc.vector.tensor_tensor(logits[:, s], scores[h][:], ks_got[:, s], MULT)
-        tops = keep.tile([P, 2], F32, name="tops")
-        nc.vector.tensor_reduce(tops[:, 1:2], logits[:, HALF : N + 1], AX, MAX)
-        nc.vector.tensor_reduce(tops[:, 0:1], logits[:, 0:HALF], AX, MAX)
+        for c in (2, 3, 0, 1):
+            s = slice(c * QUARTER, (c + 1) * QUARTER)
+            nc.vector.tensor_tensor(logits[:, s], scores[c][:], ks_got[:, s], MULT)
         m_neg = keep.tile([P, 1], F32, name="m_neg")
-        nc.gpsimd.tensor_scalar(m_neg[:], tops[:, 0:1], tops[:, 1:2], -1.0, MAX, MULT)
+        nc.vector.tensor_reduce(m_neg[:], logits[:], AX, MAX, negate=True)
         p = [keep.tile([P, PACK, P], F32, name="p%d" % g) for g in range(2)]
         sums = keep.tile([P, 3], F32, name="sums")
         for g in range(2):
             nc.scalar.activation(p[g][:].rearrange("q t s -> q s t"),
                                  logits[:, g * HALF : (g + 1) * HALF].rearrange("q (s t) -> q s t", t=PACK),
                                  EXP, bias=m_neg[:], accum_out=sums[:, g : g + 1])
-        nc.scalar.activation(sums[:, 2:3], sink_col[:], EXP, bias=m_neg[:])
+        nc.scalar.activation(sums[:, 2:3], sink_col, EXP, bias=m_neg[:])
         terms = keep.tile([P, 3], F32, name="terms")
         total = keep.tile([P, 1], F32, name="total")
         nc.scalar.activation(terms[:], sums[:], IDENTITY, accum_out=total[:])
@@ -139,14 +135,15 @@ def tile_attend_x_ks_sink_topk_kernel(tc, qT, kT, vT, ks, vs, sink, offs, out):
             for g in range(2):
                 nc.vector.tensor_copy(v_got[j][:, g * HALF : (g + 1) * HALF], v_raw[j][:].indirect(offsets[:, g * 32 : (g + 1) * 32]))
 
-        v_bf = [keep.tile([P, DV, PACK], BF16, name="v_bf%d" % g, align_bytes=64) for g in range(2)]
+        v_bf = [slot([P, DV, PACK], BF16, "v_bf0", "logits")]
+        v_last = [keep.tile([P, P, PACK], BF16, name="v_last%d" % j, align_bytes=64) for j in range(DV // P)]
         for j in range(DV // P):
             words = v_got[j][:].bitcast(F32)
             for g in range(2):
-                turned = bank(4 + 2 * j + g, [P, 2, P], "v_turned")
+                turned = bank(4 + j * (1 + g), [P, 2, P], "v_turned")
                 for u in range(2):
                     nc.tensor.transpose(turned[:, u, :], words[:, g * 256 + u : (g + 1) * 256 : 2], ident[:])
-                dest = v_bf[g][:, j * P : (j + 1) * P, :].rearrange("s e t -> s (e t)").bitcast(F32)
+                dest = (v_bf[0][:, j * P : (j + 1) * P, :] if g == 0 else v_last[j][:]).rearrange("s e t -> s (e t)").bitcast(F32)
                 nc.scalar.copy(dest.rearrange("s (e u) -> s e u", u=2), turned[:].rearrange("s u e -> s e u"))
 
         w_bf = reuse.tile([P, 2, NQ, PACK], BF16, name="w_bf", offset=0, align_bytes=64)
@@ -160,15 +157,27 @@ def tile_attend_x_ks_sink_topk_kernel(tc, qT, kT, vT, ks, vs, sink, offs, out):
                 nc.tensor.transpose(turned[:, t, :], p[g][:, t, :], ident[:])
             nc.vector.tensor_tensor(w_bf[:, g], turned[:].rearrange("s t q -> s q t"),
                                     vs_col[:, g, :].unsqueeze(1).to_broadcast([P, NQ, PACK]), MULT)
-        for g in range(2):
-            nc.vector.quantize_mx(w_codes[:, g].bitcast(FP8X4), w_scales[:, g], w_bf[:, g].rearrange("p q t -> p (q t)"))
-            nc.vector.quantize_mx(v_codes[:, g].bitcast(FP8X4), v_scales[:, g], v_bf[g][:].rearrange("p e t -> p (e t)"))
+        def quantise(codes, scales, values):
+            nc.vector.quantize_mx(codes.bitcast(FP8X4), scales, values.rearrange("p x t -> p (x t)"))
+
+        quantise(w_codes[:, 0], w_scales[:, 0], w_bf[:, 0])
+        quantise(v_codes[:, 0], v_scales[:, 0], v_bf[0][:])
+        quantise(w_codes[:, 1], w_scales[:, 1], w_bf[:, 1])
+        for j in range(DV // P):
+            e = slice(j * P, (j + 1) * P)
+            quantise(v_codes[:, 1, e], v_scales[:, 1, e], v_last[j][:])
         inv = reuse.tile([P, 1], F32, name="inv", offset=5120, align_bytes=64)
         nc.vector.reciprocal(inv[:], total[:])
-        acc = bank(0, [P, DV], "acc")
-        for g in range(2):
-            nc.tensor.matmul_mx(acc[:], lhsT=w_codes[:, g].bitcast(FP8X4), lhsT_scale=w_scales[:, g],
-                                rhs=v_codes[:, g].bitcast(FP8X4), rhs_scale=v_scales[:, g], start=(g == 0), stop=(g == 1))
-        y = keep.tile([P, DV], F32, name="y")
-        nc.scalar.activation(y[:], acc[:], COPY, scale=inv[:])
-        nc.sync.dma_start(out.rearrange("b q e -> (b q) e"), y[:])
+        y_out = out.rearrange("b q e -> (b q) e")
+        for j in range(DV // P):
+            e = slice(j * P, (j + 1) * P)
+            acc = bank(j, [P, P], "acc")
+            for g in range(2):
+                nc.tensor.matmul_mx(acc[:], lhsT=w_codes[:, g].bitcast(FP8X4), lhsT_scale=w_scales[:, g],
+                                    rhs=v_codes[:, g, e].bitcast(FP8X4), rhs_scale=v_scales[:, g, e], start=(g == 0), stop=(g == 1))
+            y = keep.tile([P, P], F32, name="y%d" % j)
+            if j == 0:
+                nc.scalar.activation(y[:], acc[:], COPY, scale=inv[:])
+            else:
+                nc.vector.tensor_scalar(y[:], acc[:], inv[:], None, MULT)
+            nc.sync.dma_start(y_out[:, e], y[:])

@@ -90,12 +90,10 @@ def tile_attend_x_ks_sink_topk_kernel(tc, qT, kT, vT, ks, vs, sink, offs, out):
         nc.vector.tensor_copy(ks_got[:], ks_pool[:].indirect(offsets[:]))
         for h in range(2):
             nc.scalar.copy(k_bf[h][:, :, 0:2], k_got[:, :, h * HALF : (h + 1) * HALF].rearrange("p t n -> p n t"))
-        vs_col = keep.tile([P, 2, PACK], F32, name="vs_col")
+        vs_turned = [bank(4 + g, [P, PACK, P], "vs_turned") for g in range(2)]
         for g in range(2):
-            turned = bank(4 + g, [P, PACK, P], "vs_turned")
             for t in range(PACK):
-                nc.tensor.transpose(turned[:, t, :], vs_got[:, g * HALF + t : (g + 1) * HALF : PACK], ident[:])
-            nc.scalar.copy(vs_col[:, g, :], turned[:, :, P - 1])
+                nc.tensor.transpose(vs_turned[g][:, t, :], vs_got[:, g * HALF + t : (g + 1) * HALF : PACK], ident[:])
 
         k_late = [slot([P, 2, QUARTER], BF16, "k_late%d" % c, "k_late%d" % c) for c in range(2)]
         nc.vector.tensor_copy(k_bf[0][:, :, 2], k_raw[2][:].indirect(offsets[:, 0:32]))
@@ -126,58 +124,66 @@ def tile_attend_x_ks_sink_topk_kernel(tc, qT, kT, vT, ks, vs, sink, offs, out):
                                  logits[:, g * HALF : (g + 1) * HALF].rearrange("q (s t) -> q s t", t=PACK),
                                  EXP, bias=m_neg[:], accum_out=sums[:, g : g + 1])
         nc.scalar.activation(sums[:, 2:3], sink_col, EXP, bias=m_neg[:])
+        vs_col = slot([P, 2, PACK], F32, "vs_col", "logits")
+        for g in range(2):
+            nc.scalar.copy(vs_col[:, g, :], vs_turned[g][:, :, P - 1])
         terms = keep.tile([P, 3], F32, name="terms")
         total = keep.tile([P, 1], F32, name="total")
         nc.scalar.activation(terms[:], sums[:], IDENTITY, accum_out=total[:])
 
         v_got = [slot([P, N], BF16, "v_got0", "k_raw1"), keep.tile([P, N], BF16, name="v_got1")]
-        for j in range(DV // P):
-            for g in range(2):
-                nc.vector.tensor_copy(v_got[j][:, g * HALF : (g + 1) * HALF], v_raw[j][:].indirect(offsets[:, g * 32 : (g + 1) * 32]))
+        nc.vector.tensor_copy(v_got[0][:, 0:P], v_raw[0][:].indirect(offsets[:, 0:8]))
+        nc.vector.tensor_copy(v_got[0][:, P:N], v_raw[0][:].indirect(offsets[:, 8:64]))
+        for g in range(2):
+            nc.vector.tensor_copy(v_got[1][:, g * HALF : (g + 1) * HALF], v_raw[1][:].indirect(offsets[:, g * 32 : (g + 1) * 32]))
 
-        v_bf = [slot([P, DV, PACK], BF16, "v_bf0", "logits")]
+        w_bf = [keep.tile([P, NQ, PACK], BF16, name="w_bf0", align_bytes=64),
+                reuse.tile([P, NQ, PACK], BF16, name="w_bf1", offset=0, align_bytes=64)]
+        w_codes = reuse.tile([P, 2, NQ], U32, name="w_codes", offset=2048, align_bytes=64)
+        v_codes = reuse.tile([P, 2, DV], U32, name="v_codes", offset=3072, align_bytes=64)
+        w_scales = keep.tile([P, 2, NQ], U8, name="w_scales", align_bytes=64)
+        v_scales = keep.tile([P, 2, DV], U8, name="v_scales", align_bytes=64)
+        p_turned = [bank(2 + g, [P, PACK, NQ], "p_turned") for g in range(2)]
+        for g in range(2):
+            for t in range(PACK):
+                nc.tensor.transpose(p_turned[g][:, t, :], p[g][:, t, :], ident[:])
+        w_planes = keep.tile([P, PACK, NQ], BF16, name="w_planes")
+        for t in range(PACK):
+            nc.scalar.activation(w_planes[:, t, :], p_turned[0][:, t, :], COPY, scale=vs_col[:, 0, t : t + 1])
+        nc.scalar.copy(w_bf[0][:], w_planes[:].rearrange("s t q -> s q t"))
+        nc.vector.tensor_tensor(w_bf[1][:], p_turned[1][:].rearrange("s t q -> s q t"),
+                                vs_col[:, 1, :].unsqueeze(1).to_broadcast([P, NQ, PACK]), MULT)
+        v_bf = [keep.tile([P, DV, PACK], BF16, name="v_bf0", align_bytes=64)]
         v_last = [keep.tile([P, P, PACK], BF16, name="v_last%d" % j, align_bytes=64) for j in range(DV // P)]
         for j in range(DV // P):
             words = v_got[j][:].bitcast(F32)
             for g in range(2):
-                turned = bank(4 + j * (1 + g), [P, 2, P], "v_turned")
+                turned = bank(4 + 2 * j + g, [P, 2, P], "v_turned")
                 for u in range(2):
                     nc.tensor.transpose(turned[:, u, :], words[:, g * 256 + u : (g + 1) * 256 : 2], ident[:])
                 dest = (v_bf[0][:, j * P : (j + 1) * P, :] if g == 0 else v_last[j][:]).rearrange("s e t -> s (e t)").bitcast(F32)
                 nc.scalar.copy(dest.rearrange("s (e u) -> s e u", u=2), turned[:].rearrange("s u e -> s e u"))
 
-        w_bf = reuse.tile([P, 2, NQ, PACK], BF16, name="w_bf", offset=0, align_bytes=64)
-        w_codes = reuse.tile([P, 2, NQ], U32, name="w_codes", offset=2048, align_bytes=64)
-        v_codes = reuse.tile([P, 2, DV], U32, name="v_codes", offset=3072, align_bytes=64)
-        w_scales = keep.tile([P, 2, NQ], U8, name="w_scales", align_bytes=64)
-        v_scales = keep.tile([P, 2, DV], U8, name="v_scales", align_bytes=64)
-        for g in range(2):
-            turned = bank(2 + g, [P, PACK, NQ], "p_turned")
-            for t in range(PACK):
-                nc.tensor.transpose(turned[:, t, :], p[g][:, t, :], ident[:])
-            nc.vector.tensor_tensor(w_bf[:, g], turned[:].rearrange("s t q -> s q t"),
-                                    vs_col[:, g, :].unsqueeze(1).to_broadcast([P, NQ, PACK]), MULT)
         def quantise(codes, scales, values):
             nc.vector.quantize_mx(codes.bitcast(FP8X4), scales, values.rearrange("p x t -> p (x t)"))
 
-        quantise(w_codes[:, 0], w_scales[:, 0], w_bf[:, 0])
+        quantise(w_codes[:, 0], w_scales[:, 0], w_bf[0][:])
         quantise(v_codes[:, 0], v_scales[:, 0], v_bf[0][:])
-        quantise(w_codes[:, 1], w_scales[:, 1], w_bf[:, 1])
+        quantise(w_codes[:, 1], w_scales[:, 1], w_bf[1][:])
         for j in range(DV // P):
             e = slice(j * P, (j + 1) * P)
             quantise(v_codes[:, 1, e], v_scales[:, 1, e], v_last[j][:])
         inv = reuse.tile([P, 1], F32, name="inv", offset=5120, align_bytes=64)
         nc.vector.reciprocal(inv[:], total[:])
         y_out = out.rearrange("b q e -> (b q) e")
-        for j in range(DV // P):
-            e = slice(j * P, (j + 1) * P)
-            acc = bank(j, [P, P], "acc")
-            for g in range(2):
-                nc.tensor.matmul_mx(acc[:], lhsT=w_codes[:, g].bitcast(FP8X4), lhsT_scale=w_scales[:, g],
+        acc = [bank(j, [P, P], "acc") for j in range(DV // P)]
+        for g in range(2):
+            for j in range(DV // P):
+                e = slice(j * P, (j + 1) * P)
+                nc.tensor.matmul_mx(acc[j][:], lhsT=w_codes[:, g].bitcast(FP8X4), lhsT_scale=w_scales[:, g],
                                     rhs=v_codes[:, g, e].bitcast(FP8X4), rhs_scale=v_scales[:, g, e], start=(g == 0), stop=(g == 1))
-            y = keep.tile([P, P], F32, name="y%d" % j)
-            if j == 0:
-                nc.scalar.activation(y[:], acc[:], COPY, scale=inv[:])
-            else:
-                nc.vector.tensor_scalar(y[:], acc[:], inv[:], None, MULT)
-            nc.sync.dma_start(y_out[:, e], y[:])
+        y = [keep.tile([P, P], F32, name="y%d" % j) for j in range(DV // P)]
+        nc.scalar.activation(y[0][:], acc[0][:], COPY, scale=inv[:])
+        nc.vector.tensor_scalar(y[1][:], acc[1][:], inv[:], None, MULT)
+        for j in range(DV // P):
+            nc.sync.dma_start(y_out[:, j * P : (j + 1) * P], y[j][:])

@@ -45,8 +45,6 @@ def tile_attend_x_ks_sink_topk_kernel(tc, qT, kT, vT, ks, vs, sink, offs, out):
         v_raw = [keep.tile([P, T], F32, name="v_raw0"), reuse.tile([P, T], F32, name="v_raw1", offset=0, align_bytes=64)]
         ks_run = keep.tile([P, RUN], F32, name="ks_run")
         nc.sync.dma_start(ks_run[:], ks[0:1, :].rearrange("o (p c) -> (o p) c", c=RUN))
-        q_raw = keep.tile([P, PACK, NQ], F32, name="q_raw")
-        nc.sync.dma_start(q_raw[:], qT.rearrange("b (p t) q -> p (b t) q", t=PACK))
         vs_pool = keep.tile([P, T], F32, name="vs_pool")
         nc.sync.dma_start(vs_pool[P - 1 : P, :], vs[0:1, :])
         nc.vector.memset(vs_pool[0 : P - 1, :], 0.0)
@@ -57,13 +55,13 @@ def tile_attend_x_ks_sink_topk_kernel(tc, qT, kT, vT, ks, vs, sink, offs, out):
         nc.sync.dma_start(sink_col, sink.rearrange("b q o -> (b q) o"))
         for t in range(PACK):
             nc.sync.dma_start(k_raw[t][:], k_rows[:, t, :])
+        q_raw = keep.tile([P, PACK, NQ], F32, name="q_raw")
+        nc.sync.dma_start(q_raw[:], qT.rearrange("b (p t) q -> p (b t) q", t=PACK))
         for j in range(DV // P):
             nc.sync.dma_start(v_raw[j][:], vT[j * P : (j + 1) * P, :])
 
         ident = keep.tile([P, P], F32, name="ident")
         make_identity(nc, ident[:])
-        warm = keep.tile([P, 1], F32, name="warm")
-        nc.scalar.activation(warm[:], ident[:, 0:1], EXP)
 
         ks_pool = keep.tile([P, T], F32, name="ks_pool")
         by_run = ks_pool[:].rearrange("r (p c) -> r p c", c=RUN)
@@ -72,12 +70,6 @@ def tile_attend_x_ks_sink_topk_kernel(tc, qT, kT, vT, ks, vs, sink, offs, out):
             for c in range(4):
                 nc.tensor.transpose(turned[:, c, :], ks_run[:, 4 * b + c : 4 * b + c + 1].to_broadcast([P, P]), ident[:])
             nc.scalar.activation(by_run[:, :, 4 * b : 4 * b + 4], turned[:].rearrange("r c p -> r p c"), COPY)
-
-        q_bf = keep.tile([P, NQ, PACK], BF16, name="q_bf", align_bytes=64)
-        nc.scalar.copy(q_bf[:], q_raw[:].rearrange("p t q -> p q t"))
-        q_codes = keep.tile([P, NQ], U32, name="q_codes", align_bytes=64)
-        q_scales = keep.tile([P, NQ], U8, name="q_scales", align_bytes=64)
-        nc.vector.quantize_mx(q_codes[:].bitcast(FP8X4), q_scales[:], q_bf[:].rearrange("p q t -> p (q t)"))
 
         k_bf = [keep.tile([P, HALF, PACK], BF16, name="k_bf%d" % h, align_bytes=64) for h in range(2)]
         k_scales = keep.tile([P, N], U8, name="k_scales", align_bytes=64)
@@ -101,16 +93,25 @@ def tile_attend_x_ks_sink_topk_kernel(tc, qT, kT, vT, ks, vs, sink, offs, out):
             for c in range(2):
                 nc.vector.tensor_copy(k_late[c][:, t - 2, :], k_raw[t][:].indirect(offsets[:, 32 + 16 * c : 48 + 16 * c]))
         nc.vector.tensor_copy(k_bf[0][:, :, 3], k_raw[3][:].indirect(offsets[:, 0:32]))
+        q_bf = keep.tile([P, NQ, PACK], BF16, name="q_bf", align_bytes=64)
+        nc.scalar.copy(q_bf[:], q_raw[:].rearrange("p t q -> p q t"))
+        q_codes = slot([P, NQ], U32, "q_codes", "k_raw3")
+        q_scales = keep.tile([P, NQ], U8, name="q_scales", align_bytes=64)
         for c in range(2):
             nc.scalar.copy(k_bf[1][:, c * QUARTER : (c + 1) * QUARTER, 2:4], k_late[c][:].rearrange("p t n -> p n t"))
         scores = [bank(c, [P, QUARTER], "scores") for c in range(4)]
+        k_codes = {}
         for c in (2, 3, 0, 1):
             s = slice(c * QUARTER, (c + 1) * QUARTER)
             within = slice((c % 2) * QUARTER, (c % 2 + 1) * QUARTER)
-            k_codes = slot([P, QUARTER], U32, "k_codes", ("k_late%d" if c < 2 else "k_codes%d") % c)
-            nc.vector.quantize_mx(k_codes[:].bitcast(FP8X4), k_scales[:, s], k_bf[c // 2][:, within, :].rearrange("p n t -> p (n t)"))
+            k_codes[c] = slot([P, QUARTER], U32, "k_codes", ("k_late%d" if c < 2 else "k_codes%d") % c)
+            nc.vector.quantize_mx(k_codes[c][:].bitcast(FP8X4), k_scales[:, s], k_bf[c // 2][:, within, :].rearrange("p n t -> p (n t)"))
+            if c == 3:
+                nc.vector.quantize_mx(q_codes[:].bitcast(FP8X4), q_scales[:], q_bf[:].rearrange("p q t -> p (q t)"))
+        for c in (2, 3, 0, 1):
+            s = slice(c * QUARTER, (c + 1) * QUARTER)
             nc.tensor.matmul_mx(scores[c][:], lhsT=q_codes[:].bitcast(FP8X4), lhsT_scale=q_scales[:],
-                                rhs=k_codes[:].bitcast(FP8X4), rhs_scale=k_scales[:, s], start=True, stop=True)
+                                rhs=k_codes[c][:].bitcast(FP8X4), rhs_scale=k_scales[:, s], start=True, stop=True)
 
         for c in (2, 3, 0, 1):
             s = slice(c * QUARTER, (c + 1) * QUARTER)

@@ -44,15 +44,15 @@ def tile_attend_x_ks_sink_topk_kernel(tc, qT, kT, vT, ks, vs, sink, offs, out):
         k_raw = [slot([P, T], F32, "k_raw%d" % t, "k_raw%d" % t) for t in range(PACK)]
         v_raw = [keep.tile([P, T], F32, name="v_raw0"), reuse.tile([P, T], F32, name="v_raw1", offset=0, align_bytes=64)]
         ks_run = keep.tile([P, RUN], F32, name="ks_run")
-        nc.sync.dma_start(ks_run[:], ks[0:1, :].rearrange("o (p c) -> (o p) c", c=RUN))
+        nc.scalar.dma_start(ks_run[:], ks[0:1, :].rearrange("o (p c) -> (o p) c", c=RUN))
         vs_pool = keep.tile([P, T], F32, name="vs_pool")
-        nc.sync.dma_start(vs_pool[P - 1 : P, :], vs[0:1, :])
+        nc.scalar.dma_start(vs_pool[P - 1 : P, :], vs[0:1, :])
         nc.vector.memset(vs_pool[0 : P - 1, :], 0.0)
         offsets = keep.tile([P, N // 16], U16, name="offsets")
         nc.sync.dma_start(offsets[:], offs)
         logits = slot([P, N + 1], F32, "logits", "logits")
         sink_col = logits[:, N : N + 1]
-        nc.sync.dma_start(sink_col, sink.rearrange("b q o -> (b q) o"))
+        nc.scalar.dma_start(sink_col, sink.rearrange("b q o -> (b q) o"))
         for t in range(PACK):
             nc.sync.dma_start(k_raw[t][:], k_rows[:, t, :])
         q_raw = keep.tile([P, PACK, NQ], F32, name="q_raw")

@@ -82,10 +82,18 @@ def tile_attend_x_ks_sink_topk_kernel(tc, qT, kT, vT, ks, vs, sink, offs, out):
         nc.vector.tensor_copy(ks_got[:], ks_pool[:].indirect(offsets[:]))
         for h in range(2):
             nc.scalar.copy(k_bf[h][:, :, 0:2], k_got[:, :, h * HALF : (h + 1) * HALF].rearrange("p t n -> p n t"))
-        vs_turned = [bank(4 + g, [P, PACK, P], "vs_turned") for g in range(2)]
+        vs_col = keep.tile([P, 2, PACK], F32, name="vs_col")
+        vs_all = [keep.tile([P, 2, P, 2], F32, name="vs_all%d" % g) for g in range(2)]
         for g in range(2):
-            for t in range(PACK):
-                nc.tensor.transpose(vs_turned[g][:, t, :], vs_got[:, g * HALF + t : (g + 1) * HALF : PACK], ident[:])
+            turned = bank(4 + g, [P, PACK, P], "vs_turned")
+            for c in range(PACK):
+                nc.tensor.transpose(turned[:, c, :], vs_got[:, g * HALF + c * P : g * HALF + (c + 1) * P], ident[:])
+            nc.scalar.copy(vs_col[:, g, :], turned[:, :, P - 1])
+        for g in range(2):
+            spread = bank(2 + g, [P, HALF], "vs_spread")
+            for c in range(PACK):
+                nc.tensor.transpose(spread[:, c * P : (c + 1) * P], vs_col[:, g, c : c + 1].to_broadcast([P, P]), ident[:])
+            nc.scalar.copy(vs_all[g][:], spread[:].rearrange("r (s u e) -> r u s e", u=2, e=2))
 
         k_late = [slot([P, 2, QUARTER], BF16, "k_late%d" % c, "k_late%d" % c) for c in range(2)]
         nc.vector.tensor_copy(k_bf[0][:, :, 2], k_raw[2][:].indirect(offsets[:, 0:32]))
@@ -118,71 +126,72 @@ def tile_attend_x_ks_sink_topk_kernel(tc, qT, kT, vT, ks, vs, sink, offs, out):
             nc.vector.tensor_tensor(logits[:, s], scores[c][:], ks_got[:, s], MULT)
         m_neg = keep.tile([P, 1], F32, name="m_neg")
         nc.vector.tensor_reduce(m_neg[:], logits[:], AX, MAX, negate=True)
-        p = [keep.tile([P, PACK, P], F32, name="p%d" % g) for g in range(2)]
+        p = [keep.tile([P, 2, P, 2], F32, name="p%d" % g) for g in range(2)]
         sums = keep.tile([P, 3], F32, name="sums")
         for g in range(2):
-            nc.scalar.activation(p[g][:].rearrange("q t s -> q s t"),
-                                 logits[:, g * HALF : (g + 1) * HALF].rearrange("q (s t) -> q s t", t=PACK),
+            nc.scalar.activation(p[g][:].rearrange("q u s e -> q s u e"),
+                                 logits[:, g * HALF : (g + 1) * HALF].rearrange("q (s u e) -> q s u e", u=2, e=2),
                                  EXP, bias=m_neg[:], accum_out=sums[:, g : g + 1])
         nc.scalar.activation(sums[:, 2:3], sink_col, EXP, bias=m_neg[:])
-        vs_col = slot([P, 2, PACK], F32, "vs_col", "logits")
-        for g in range(2):
-            nc.scalar.copy(vs_col[:, g, :], vs_turned[g][:, :, P - 1])
         terms = keep.tile([P, 3], F32, name="terms")
         total = keep.tile([P, 1], F32, name="total")
         nc.scalar.activation(terms[:], sums[:], IDENTITY, accum_out=total[:])
 
         v_got = [slot([P, N], BF16, "v_got0", "k_raw1"), keep.tile([P, N], BF16, name="v_got1")]
         nc.vector.tensor_copy(v_got[0][:, 0:P], v_raw[0][:].indirect(offsets[:, 0:8]))
-        nc.vector.tensor_copy(v_got[0][:, P:N], v_raw[0][:].indirect(offsets[:, 8:64]))
+        nc.vector.tensor_copy(v_got[0][:, P:HALF], v_raw[0][:].indirect(offsets[:, 8:32]))
+        nc.vector.tensor_copy(v_got[0][:, HALF:N], v_raw[0][:].indirect(offsets[:, 32:64]))
         for g in range(2):
             nc.vector.tensor_copy(v_got[1][:, g * HALF : (g + 1) * HALF], v_raw[1][:].indirect(offsets[:, g * 32 : (g + 1) * 32]))
 
-        w_bf = [keep.tile([P, NQ, PACK], BF16, name="w_bf0", align_bytes=64),
-                reuse.tile([P, NQ, PACK], BF16, name="w_bf1", offset=0, align_bytes=64)]
-        w_codes = reuse.tile([P, 2, NQ], U32, name="w_codes", offset=2048, align_bytes=64)
-        v_codes = reuse.tile([P, 2, DV], U32, name="v_codes", offset=3072, align_bytes=64)
-        w_scales = keep.tile([P, 2, NQ], U8, name="w_scales", align_bytes=64)
-        v_scales = keep.tile([P, 2, DV], U8, name="v_scales", align_bytes=64)
-        p_turned = [bank(2 + g, [P, PACK, NQ], "p_turned") for g in range(2)]
+        w_rows = [keep.tile([P, HALF], BF16, name="w_rows%d" % g) for g in range(2)]
         for g in range(2):
-            for t in range(PACK):
-                nc.tensor.transpose(p_turned[g][:, t, :], p[g][:, t, :], ident[:])
-        w_planes = keep.tile([P, PACK, NQ], BF16, name="w_planes")
-        for t in range(PACK):
-            nc.scalar.activation(w_planes[:, t, :], p_turned[0][:, t, :], COPY, scale=vs_col[:, 0, t : t + 1])
-        nc.scalar.copy(w_bf[0][:], w_planes[:].rearrange("s t q -> s q t"))
-        nc.vector.tensor_tensor(w_bf[1][:], p_turned[1][:].rearrange("s t q -> s q t"),
-                                vs_col[:, 1, :].unsqueeze(1).to_broadcast([P, NQ, PACK]), MULT)
-        v_bf = [keep.tile([P, DV, PACK], BF16, name="v_bf0", align_bytes=64)]
-        v_last = [keep.tile([P, P, PACK], BF16, name="v_last%d" % j, align_bytes=64) for j in range(DV // P)]
-        for j in range(DV // P):
+            nc.gpsimd.tensor_tensor(w_rows[g][:], p[g][:].rearrange("q u s e -> q (u s e)"),
+                                    vs_all[g][:].rearrange("q u s e -> q (u s e)"), MULT)
+        w_bf = keep.tile([P, 2, NQ * PACK], BF16, name="w_bf", align_bytes=64)
+        v_first = slot([P, 2, P * PACK], BF16, "v_first", "logits")
+        v_last = [keep.tile([P, P * PACK], BF16, name="v_last%d" % g, align_bytes=64) for g in range(2)]
+        w_codes = reuse.tile([P, 2, NQ], U32, name="w_codes", offset=2048, align_bytes=64)
+        v_codes = reuse.tile([P, 2, 2, P], U32, name="v_codes", offset=3072, align_bytes=64)
+        w_scales = keep.tile([P, 2, NQ], U8, name="w_scales", align_bytes=64)
+        v_scales = keep.tile([P, 2, 2, P], U8, name="v_scales", align_bytes=64)
+
+        def turn(b, first, second, dest):
+            turned = bank(b, [P, 2, P], "turned")
+            nc.tensor.transpose(turned[:, 0, :], first, ident[:])
+            nc.tensor.transpose(turned[:, 1, :], second, ident[:])
+            nc.scalar.copy(dest.bitcast(F32).rearrange("s (x u) -> s x u", u=2), turned[:].rearrange("s u x -> s x u"))
+
+        def turn_values(j, g, dest):
             words = v_got[j][:].bitcast(F32)
-            for g in range(2):
-                turned = bank(4 + 2 * j + g, [P, 2, P], "v_turned")
-                for u in range(2):
-                    nc.tensor.transpose(turned[:, u, :], words[:, g * 256 + u : (g + 1) * 256 : 2], ident[:])
-                dest = (v_bf[0][:, j * P : (j + 1) * P, :] if g == 0 else v_last[j][:]).rearrange("s e t -> s (e t)").bitcast(F32)
-                nc.scalar.copy(dest.rearrange("s (e u) -> s e u", u=2), turned[:].rearrange("s u e -> s e u"))
+            turn(4 + 2 * j + g, words[:, g * 256 : (g + 1) * 256 : 2], words[:, g * 256 + 1 : (g + 1) * 256 : 2], dest)
+
+        def turn_weights(g):
+            words = w_rows[g][:].bitcast(F32)
+            turn(2 + g, words[:, 0:P], words[:, P : 2 * P], w_bf[:, g, :])
+
+        turn_values(0, 0, v_first[:, 0, :])
+        turn_weights(0)
+        turn_values(0, 1, v_first[:, 1, :])
+        turn_weights(1)
+        for g in range(2):
+            turn_values(1, g, v_last[g][:])
 
         def quantise(codes, scales, values):
-            nc.vector.quantize_mx(codes.bitcast(FP8X4), scales, values.rearrange("p x t -> p (x t)"))
+            nc.vector.quantize_mx(codes.bitcast(FP8X4), scales, values)
 
-        quantise(w_codes[:, 0], w_scales[:, 0], w_bf[0][:])
-        quantise(v_codes[:, 0], v_scales[:, 0], v_bf[0][:])
-        quantise(w_codes[:, 1], w_scales[:, 1], w_bf[1][:])
-        for j in range(DV // P):
-            e = slice(j * P, (j + 1) * P)
-            quantise(v_codes[:, 1, e], v_scales[:, 1, e], v_last[j][:])
+        quantise(v_codes[:, 0].rearrange("s g e -> s (g e)"), v_scales[:, 0].rearrange("s g e -> s (g e)"), v_first[:].rearrange("s g x -> s (g x)"))
+        quantise(w_codes[:].rearrange("s g q -> s (g q)"), w_scales[:].rearrange("s g q -> s (g q)"), w_bf[:].rearrange("s g x -> s (g x)"))
         inv = reuse.tile([P, 1], F32, name="inv", offset=5120, align_bytes=64)
         nc.vector.reciprocal(inv[:], total[:])
+        for g in range(2):
+            quantise(v_codes[:, 1, g], v_scales[:, 1, g], v_last[g][:])
         y_out = out.rearrange("b q e -> (b q) e")
         acc = [bank(j, [P, P], "acc") for j in range(DV // P)]
-        for g in range(2):
-            for j in range(DV // P):
-                e = slice(j * P, (j + 1) * P)
+        for j in range(DV // P):
+            for g in range(2):
                 nc.tensor.matmul_mx(acc[j][:], lhsT=w_codes[:, g].bitcast(FP8X4), lhsT_scale=w_scales[:, g],
-                                    rhs=v_codes[:, g, e].bitcast(FP8X4), rhs_scale=v_scales[:, g, e], start=(g == 0), stop=(g == 1))
+                                    rhs=v_codes[:, j, g].bitcast(FP8X4), rhs_scale=v_scales[:, j, g], start=(g == 0), stop=(g == 1))
         y = [keep.tile([P, P], F32, name="y%d" % j) for j in range(DV // P)]
         nc.scalar.activation(y[0][:], acc[0][:], COPY, scale=inv[:])
         nc.vector.tensor_scalar(y[1][:], acc[1][:], inv[:], None, MULT)

@@ -121,7 +121,10 @@ def tile_attend_x_ks_sink_topk_kernel(tc, qT, kT, vT, ks, vs, sink, offs, out):
             nc.tensor.matmul_mx(scores[c][:], lhsT=q_codes[:].bitcast(FP8X4), lhsT_scale=q_scales[:],
                                 rhs=k_codes[c][:].bitcast(FP8X4), rhs_scale=k_scales[:, s], start=True, stop=True)
 
-        for c in (2, 3, 0, 1):
+        unscaled = keep.tile([P, QUARTER], F32, name="unscaled")
+        nc.scalar.copy(unscaled[:], scores[2][:])
+        nc.gpsimd.tensor_tensor(logits[:, 2 * QUARTER : 3 * QUARTER], unscaled[:], ks_got[:, 2 * QUARTER : 3 * QUARTER], MULT)
+        for c in (3, 0, 1):
             s = slice(c * QUARTER, (c + 1) * QUARTER)
             nc.vector.tensor_tensor(logits[:, s], scores[c][:], ks_got[:, s], MULT)
         m_neg = keep.tile([P, 1], F32, name="m_neg")

@@ -17,6 +17,7 @@ U16 = mybir.dt.uint16
 U8 = mybir.dt.uint8
 FP8X4 = mybir.dt.float8_e4m3fn_x4
 MULT = mybir.AluOpType.mult
+ADD = mybir.AluOpType.add
 MAX = mybir.AluOpType.max
 AX = mybir.AxisListType.X
 COPY = mybir.ActivationFunctionType.Copy
@@ -46,10 +47,13 @@ def tile_attend_x_ks_sink_topk_kernel(tc, qT, kT, vT, ks, vs, sink, offs, out):
         ks_run = keep.tile([P, RUN], F32, name="ks_run")
         nc.scalar.dma_start(ks_run[:], ks[0:1, :].rearrange("o (p c) -> (o p) c", c=RUN))
         vs_pool = keep.tile([P, T], F32, name="vs_pool")
-        nc.scalar.dma_start(vs_pool[P - 1 : P, :], vs[0:1, :])
-        nc.vector.memset(vs_pool[0 : P - 1, :], 0.0)
+        nc.scalar.dma_start(vs_pool[P - 1 : P, T // 2 : T], vs[0:1, T // 2 : T])
         offsets = keep.tile([P, N // 16], U16, name="offsets")
         nc.sync.dma_start(offsets[:], offs)
+        nc.sync.dma_start(vs_pool[63:64, 0 : T // 2], vs[0:1, 0 : T // 2])
+        nc.vector.memset(vs_pool[0:63, 0 : T // 2], 0.0)
+        nc.vector.memset(vs_pool[64:P, 0 : T // 2], 0.0)
+        nc.vector.memset(vs_pool[0 : P - 1, T // 2 : T], 0.0)
         logits = slot([P, N + 1], F32, "logits", "logits")
         sink_col = logits[:, N : N + 1]
         nc.scalar.dma_start(sink_col, sink.rearrange("b q o -> (b q) o"))
@@ -82,13 +86,15 @@ def tile_attend_x_ks_sink_topk_kernel(tc, qT, kT, vT, ks, vs, sink, offs, out):
         nc.vector.tensor_copy(ks_got[:], ks_pool[:].indirect(offsets[:]))
         for h in range(2):
             nc.scalar.copy(k_bf[h][:, :, 0:2], k_got[:, :, h * HALF : (h + 1) * HALF].rearrange("p t n -> p n t"))
+        vs_parts = keep.tile([P, 2, PACK, 2], F32, name="vs_parts")
         vs_col = keep.tile([P, 2, PACK], F32, name="vs_col")
         vs_all = [keep.tile([P, 2, P, 2], F32, name="vs_all%d" % g) for g in range(2)]
         for g in range(2):
-            turned = bank(4 + g, [P, PACK, P], "vs_turned")
+            turned = bank(g, [P, PACK, P], "vs_turned")
             for c in range(PACK):
                 nc.tensor.transpose(turned[:, c, :], vs_got[:, g * HALF + c * P : g * HALF + (c + 1) * P], ident[:])
-            nc.scalar.copy(vs_col[:, g, :], turned[:, :, P - 1])
+            nc.scalar.copy(vs_parts[:, g], turned[:, :, 63::64])
+        nc.gpsimd.tensor_tensor(vs_col[:], vs_parts[:, :, :, 0], vs_parts[:, :, :, 1], ADD)
         for g in range(2):
             spread = bank(2 + g, [P, HALF], "vs_spread")
             for c in range(PACK):
@@ -176,19 +182,21 @@ def tile_attend_x_ks_sink_topk_kernel(tc, qT, kT, vT, ks, vs, sink, offs, out):
         turn_values(0, 0, v_first[:, 0, :])
         turn_weights(0)
         turn_values(0, 1, v_first[:, 1, :])
+        turn_values(1, 0, v_last[0][:])
         turn_weights(1)
-        for g in range(2):
-            turn_values(1, g, v_last[g][:])
+        turn_values(1, 1, v_last[1][:])
 
         def quantise(codes, scales, values):
             nc.vector.quantize_mx(codes.bitcast(FP8X4), scales, values)
 
-        quantise(v_codes[:, 0].rearrange("s g e -> s (g e)"), v_scales[:, 0].rearrange("s g e -> s (g e)"), v_first[:].rearrange("s g x -> s (g x)"))
-        quantise(w_codes[:].rearrange("s g q -> s (g q)"), w_scales[:].rearrange("s g q -> s (g q)"), w_bf[:].rearrange("s g x -> s (g x)"))
+        quantise(w_codes[:, 0], w_scales[:, 0], w_bf[:, 0])
+        quantise(v_codes[:, 0, 0], v_scales[:, 0, 0], v_first[:, 0])
+        quantise(v_codes[:, 0, 1], v_scales[:, 0, 1], v_first[:, 1])
+        quantise(w_codes[:, 1], w_scales[:, 1], w_bf[:, 1])
+        quantise(v_codes[:, 1, 0], v_scales[:, 1, 0], v_last[0][:])
         inv = reuse.tile([P, 1], F32, name="inv", offset=5120, align_bytes=64)
         nc.vector.reciprocal(inv[:], total[:])
-        for g in range(2):
-            quantise(v_codes[:, 1, g], v_scales[:, 1, g], v_last[g][:])
+        quantise(v_codes[:, 1, 1], v_scales[:, 1, 1], v_last[1][:])
         y_out = out.rearrange("b q e -> (b q) e")
         acc = [bank(j, [P, P], "acc") for j in range(DV // P)]
         for j in range(DV // P):

@@ -9,6 +9,7 @@ PACK = 4
 HALF = 512
 QUARTER = 256
 RUN = T // P
+PAGE = 4096
 
 F32 = mybir.dt.float32
 BF16 = mybir.dt.bfloat16
@@ -39,11 +40,11 @@ def tile_attend_x_ks_sink_topk_kernel(tc, qT, kT, vT, ks, vs, sink, offs, out):
             return psum.tile(shape, F32, name=name, tag="bank%d" % b)
 
         def slot(shape, dtype, name, tag):
-            return keep.tile(shape, dtype, name=name, tag=tag, align_bytes=64)
+            return keep.tile(shape, dtype, name=name, tag=tag, align_bytes=PAGE if tag.startswith("k_raw") else 64)
 
         k_rows = kT.rearrange("(p t) n -> p t n", t=PACK)
         k_raw = [slot([P, T], F32, "k_raw%d" % t, "k_raw%d" % t) for t in range(PACK)]
-        v_raw = [keep.tile([P, T], F32, name="v_raw0"), reuse.tile([P, T], F32, name="v_raw1", offset=0, align_bytes=64)]
+        v_raw = [keep.tile([P, T], F32, name="v_raw0", align_bytes=PAGE), reuse.tile([P, T], F32, name="v_raw1", offset=0, align_bytes=PAGE)]
         ks_run = keep.tile([P, RUN], F32, name="ks_run")
         nc.scalar.dma_start(ks_run[:], ks[0:1, :].rearrange("o (p c) -> (o p) c", c=RUN))
         vs_pool = keep.tile([P, T], F32, name="vs_pool")

@@ -108,8 +108,8 @@ def tile_attend_x_ks_sink_topk_kernel(tc, qT, kT, vT, ks, vs, sink, offs, out):
             for c in range(2):
                 nc.vector.tensor_copy(k_late[c][:, t - 2, :], k_raw[t][:].indirect(offsets[:, 32 + 16 * c : 48 + 16 * c]))
         nc.vector.tensor_copy(k_bf[0][:, :, 3], k_raw[3][:].indirect(offsets[:, 0:32]))
-        q_bf = keep.tile([P, NQ, PACK], BF16, name="q_bf", align_bytes=64)
-        nc.scalar.copy(q_bf[:], q_raw[:].rearrange("p t q -> p q t"))
+        q_bf = reuse.tile([P, NQ, PACK], BF16, name="q_bf", offset=4 * T + 2 * QUARTER, align_bytes=64)
+        nc.gpsimd.tensor_scalar(q_bf[:], q_raw[:].rearrange("p t q -> p q t"), 1.0, 0.0, MULT, ADD)
         q_codes = slot([P, NQ], U32, "q_codes", "k_raw3")
         q_scales = keep.tile([P, NQ], U8, name="q_scales", align_bytes=64)
         for c in range(2):
@@ -119,9 +119,9 @@ def tile_attend_x_ks_sink_topk_kernel(tc, qT, kT, vT, ks, vs, sink, offs, out):
         for c in (2, 3, 0, 1):
             s = slice(c * QUARTER, (c + 1) * QUARTER)
             within = slice((c % 2) * QUARTER, (c % 2 + 1) * QUARTER)
-            k_codes[c] = slot([P, QUARTER], U32, "k_codes", ("k_late%d" if c < 2 else "k_codes%d") % c)
+            k_codes[c] = reuse.tile([P, QUARTER], U32, name="k_codes%d" % c, offset=4 * T + 4 * QUARTER * c, align_bytes=64)
             nc.vector.quantize_mx(k_codes[c][:].bitcast(FP8X4), k_scales[:, s], k_bf[c // 2][:, within, :].rearrange("p n t -> p (n t)"))
-            if c == 3:
+            if c == 2:
                 nc.vector.quantize_mx(q_codes[:].bitcast(FP8X4), q_scales[:], q_bf[:].rearrange("p q t -> p (q t)"))
         for c in (2, 3, 0, 1):
             s = slice(c * QUARTER, (c + 1) * QUARTER)

@@ -20,7 +20,9 @@ FP8X4 = mybir.dt.float8_e4m3fn_x4
 MULT = mybir.AluOpType.mult
 ADD = mybir.AluOpType.add
 MAX = mybir.AluOpType.max
+MIN = mybir.AluOpType.min
 AX = mybir.AxisListType.X
+AXY = mybir.AxisListType.XY
 COPY = mybir.ActivationFunctionType.Copy
 IDENTITY = mybir.ActivationFunctionType.Identity
 EXP = mybir.ActivationFunctionType.Exp
@@ -55,8 +57,8 @@ def tile_attend_x_ks_sink_topk_kernel(tc, qT, kT, vT, ks, vs, sink, offs, out):
         nc.vector.memset(vs_pool[0:63, 0 : T // 2], 0.0)
         nc.vector.memset(vs_pool[64:P, 0 : T // 2], 0.0)
         nc.vector.memset(vs_pool[0 : P - 1, T // 2 : T], 0.0)
-        logits = slot([P, N + 1], F32, "logits", "logits")
-        sink_col = logits[:, N : N + 1]
+        logits = slot([P, N], F32, "logits", "logits")
+        sink_col = keep.tile([P, 1], F32, name="sink_col")[:]
         nc.scalar.dma_start(sink_col, sink.rearrange("b q o -> (b q) o"))
         for t in range(PACK):
             nc.sync.dma_start(k_raw[t][:], k_rows[:, t, :])
@@ -75,6 +77,9 @@ def tile_attend_x_ks_sink_topk_kernel(tc, qT, kT, vT, ks, vs, sink, offs, out):
             for c in range(4):
                 nc.tensor.transpose(turned[:, c, :], ks_run[:, 4 * b + c : 4 * b + c + 1].to_broadcast([P, P]), ident[:])
             nc.scalar.activation(by_run[:, :, 4 * b : 4 * b + 4], turned[:].rearrange("r c p -> r p c"), COPY)
+
+        sink_neg = keep.tile([P, 1], F32, name="sink_neg")
+        nc.scalar.activation(sink_neg[:], sink_col, COPY, scale=-1.0)
 
         k_bf = [keep.tile([P, HALF, PACK], BF16, name="k_bf%d" % h, align_bytes=64) for h in range(2)]
         k_scales = keep.tile([P, N], U8, name="k_scales", align_bytes=64)
@@ -135,7 +140,10 @@ def tile_attend_x_ks_sink_topk_kernel(tc, qT, kT, vT, ks, vs, sink, offs, out):
             s = slice(c * QUARTER, (c + 1) * QUARTER)
             nc.vector.tensor_tensor(logits[:, s], scores[c][:], ks_got[:, s], MULT)
         m_neg = keep.tile([P, 1], F32, name="m_neg")
-        nc.vector.tensor_reduce(m_neg[:], logits[:], AX, MAX, negate=True)
+        m_parts = keep.tile([P, 2], F32, name="m_parts")
+        nc.vector.tensor_reduce(m_parts[:, 0:1], logits[:].rearrange("q (c s) -> q c s", s=QUARTER)[:, 0::3, :], AXY, MAX, negate=True)
+        nc.vector.tensor_reduce(m_parts[:, 1:2], logits[:, QUARTER : 3 * QUARTER], AX, MAX, negate=True)
+        nc.gpsimd.tensor_scalar(m_neg[:], m_parts[:, 0:1], m_parts[:, 1:2], sink_neg[:], MIN, MIN)
         p = [keep.tile([P, 2, P, 2], F32, name="p%d" % g) for g in range(2)]
         sums = keep.tile([P, 3], F32, name="sums")
         for g in range(2):
@@ -148,11 +156,9 @@ def tile_attend_x_ks_sink_topk_kernel(tc, qT, kT, vT, ks, vs, sink, offs, out):
         nc.scalar.activation(terms[:], sums[:], IDENTITY, accum_out=total[:])
 
         v_got = [slot([P, N], BF16, "v_got0", "k_raw1"), keep.tile([P, N], BF16, name="v_got1")]
-        nc.vector.tensor_copy(v_got[0][:, 0:P], v_raw[0][:].indirect(offsets[:, 0:8]))
-        nc.vector.tensor_copy(v_got[0][:, P:HALF], v_raw[0][:].indirect(offsets[:, 8:32]))
-        nc.vector.tensor_copy(v_got[0][:, HALF:N], v_raw[0][:].indirect(offsets[:, 32:64]))
-        for g in range(2):
-            nc.vector.tensor_copy(v_got[1][:, g * HALF : (g + 1) * HALF], v_raw[1][:].indirect(offsets[:, g * 32 : (g + 1) * 32]))
+        for j in range(DV // P):
+            for g in range(2):
+                nc.vector.tensor_copy(v_got[j][:, g * HALF : (g + 1) * HALF], v_raw[j][:].indirect(offsets[:, g * 32 : (g + 1) * 32]))
 
         w_rows = [keep.tile([P, HALF], BF16, name="w_rows%d" % g) for g in range(2)]
         for g in range(2):

@@ -21,7 +21,6 @@ MULT = mybir.AluOpType.mult
 ADD = mybir.AluOpType.add
 MAX = mybir.AluOpType.max
 MIN = mybir.AluOpType.min
-AX = mybir.AxisListType.X
 AXY = mybir.AxisListType.XY
 COPY = mybir.ActivationFunctionType.Copy
 IDENTITY = mybir.ActivationFunctionType.Identity
@@ -57,8 +56,8 @@ def tile_attend_x_ks_sink_topk_kernel(tc, qT, kT, vT, ks, vs, sink, offs, out):
         nc.vector.memset(vs_pool[0:63, 0 : T // 2], 0.0)
         nc.vector.memset(vs_pool[64:P, 0 : T // 2], 0.0)
         nc.vector.memset(vs_pool[0 : P - 1, T // 2 : T], 0.0)
-        logits = slot([P, N], F32, "logits", "logits")
-        sink_col = keep.tile([P, 1], F32, name="sink_col")[:]
+        logits = slot([P, N + QUARTER], F32, "logits", "logits")
+        sink_col = logits[:, N : N + 1]
         nc.scalar.dma_start(sink_col, sink.rearrange("b q o -> (b q) o"))
         for t in range(PACK):
             nc.sync.dma_start(k_raw[t][:], k_rows[:, t, :])
@@ -77,9 +76,6 @@ def tile_attend_x_ks_sink_topk_kernel(tc, qT, kT, vT, ks, vs, sink, offs, out):
             for c in range(4):
                 nc.tensor.transpose(turned[:, c, :], ks_run[:, 4 * b + c : 4 * b + c + 1].to_broadcast([P, P]), ident[:])
             nc.scalar.activation(by_run[:, :, 4 * b : 4 * b + 4], turned[:].rearrange("r c p -> r p c"), COPY)
-
-        sink_neg = keep.tile([P, 1], F32, name="sink_neg")
-        nc.scalar.activation(sink_neg[:], sink_col, COPY, scale=-1.0)
 
         k_bf = [keep.tile([P, HALF, PACK], BF16, name="k_bf%d" % h, align_bytes=64) for h in range(2)]
         k_scales = keep.tile([P, N], U8, name="k_scales", align_bytes=64)
@@ -110,40 +106,42 @@ def tile_attend_x_ks_sink_topk_kernel(tc, qT, kT, vT, ks, vs, sink, offs, out):
         k_late = [slot([P, 2, QUARTER], BF16, "k_late%d" % c, "k_late%d" % c) for c in range(2)]
         nc.vector.tensor_copy(k_bf[0][:, :, 2], k_raw[2][:].indirect(offsets[:, 0:32]))
         for t in range(2, PACK):
-            for c in range(2):
+            for c in (1, 0):
                 nc.vector.tensor_copy(k_late[c][:, t - 2, :], k_raw[t][:].indirect(offsets[:, 32 + 16 * c : 48 + 16 * c]))
         nc.vector.tensor_copy(k_bf[0][:, :, 3], k_raw[3][:].indirect(offsets[:, 0:32]))
         q_bf = reuse.tile([P, NQ, PACK], BF16, name="q_bf", offset=4 * T + 2 * QUARTER, align_bytes=64)
         nc.gpsimd.tensor_scalar(q_bf[:], q_raw[:].rearrange("p t q -> p q t"), 1.0, 0.0, MULT, ADD)
         q_codes = slot([P, NQ], U32, "q_codes", "k_raw3")
         q_scales = keep.tile([P, NQ], U8, name="q_scales", align_bytes=64)
-        for c in range(2):
+        for c in (1, 0):
             nc.scalar.copy(k_bf[1][:, c * QUARTER : (c + 1) * QUARTER, 2:4], k_late[c][:].rearrange("p t n -> p n t"))
         scores = [bank(c, [P, QUARTER], "scores") for c in range(4)]
         k_codes = {}
-        for c in (2, 3, 0, 1):
+        for c in (3, 2, 0, 1):
             s = slice(c * QUARTER, (c + 1) * QUARTER)
             within = slice((c % 2) * QUARTER, (c % 2 + 1) * QUARTER)
             k_codes[c] = reuse.tile([P, QUARTER], U32, name="k_codes%d" % c, offset=4 * T + 4 * QUARTER * c, align_bytes=64)
             nc.vector.quantize_mx(k_codes[c][:].bitcast(FP8X4), k_scales[:, s], k_bf[c // 2][:, within, :].rearrange("p n t -> p (n t)"))
-            if c == 2:
+            if c == 3:
                 nc.vector.quantize_mx(q_codes[:].bitcast(FP8X4), q_scales[:], q_bf[:].rearrange("p q t -> p (q t)"))
-        for c in (2, 3, 0, 1):
+        for c in (3, 2, 0, 1):
             s = slice(c * QUARTER, (c + 1) * QUARTER)
             nc.tensor.matmul_mx(scores[c][:], lhsT=q_codes[:].bitcast(FP8X4), lhsT_scale=q_scales[:],
                                 rhs=k_codes[c][:].bitcast(FP8X4), rhs_scale=k_scales[:, s], start=True, stop=True)
 
         unscaled = keep.tile([P, QUARTER], F32, name="unscaled")
-        nc.scalar.copy(unscaled[:], scores[2][:])
-        nc.gpsimd.tensor_tensor(logits[:, 2 * QUARTER : 3 * QUARTER], unscaled[:], ks_got[:, 2 * QUARTER : 3 * QUARTER], MULT)
-        for c in (3, 0, 1):
+        nc.scalar.copy(unscaled[:], scores[3][:])
+        nc.gpsimd.tensor_tensor(logits[:, 3 * QUARTER : N], unscaled[:], ks_got[:, 3 * QUARTER : N], MULT)
+        for c in (2, 0, 1):
             s = slice(c * QUARTER, (c + 1) * QUARTER)
             nc.vector.tensor_tensor(logits[:, s], scores[c][:], ks_got[:, s], MULT)
         m_neg = keep.tile([P, 1], F32, name="m_neg")
         m_parts = keep.tile([P, 2], F32, name="m_parts")
-        nc.vector.tensor_reduce(m_parts[:, 0:1], logits[:].rearrange("q (c s) -> q c s", s=QUARTER)[:, 0::3, :], AXY, MAX, negate=True)
-        nc.vector.tensor_reduce(m_parts[:, 1:2], logits[:, QUARTER : 3 * QUARTER], AX, MAX, negate=True)
-        nc.gpsimd.tensor_scalar(m_neg[:], m_parts[:, 0:1], m_parts[:, 1:2], sink_neg[:], MIN, MIN)
+        even = logits[:, 0:N].rearrange("q (h s) -> q h s", h=2)[:, :, 0:QUARTER]
+        odd = logits[:, QUARTER : N + QUARTER].rearrange("q (h s) -> q h s", h=2)[:, :, 0 : QUARTER + 1]
+        nc.vector.tensor_reduce(m_parts[:, 0:1], even, AXY, MAX, negate=True)
+        nc.vector.tensor_reduce(m_parts[:, 1:2], odd, AXY, MAX, negate=True)
+        nc.gpsimd.tensor_scalar(m_neg[:], m_parts[:, 0:1], m_parts[:, 1:2], None, MIN)
         p = [keep.tile([P, 2, P, 2], F32, name="p%d" % g) for g in range(2)]
         sums = keep.tile([P, 3], F32, name="sums")
         for g in range(2):
@@ -197,17 +195,16 @@ def tile_attend_x_ks_sink_topk_kernel(tc, qT, kT, vT, ks, vs, sink, offs, out):
             nc.vector.quantize_mx(codes.bitcast(FP8X4), scales, values)
 
         quantise(w_codes[:, 0], w_scales[:, 0], w_bf[:, 0])
-        quantise(v_codes[:, 0, 0], v_scales[:, 0, 0], v_first[:, 0])
-        quantise(v_codes[:, 0, 1], v_scales[:, 0, 1], v_first[:, 1])
-        quantise(w_codes[:, 1], w_scales[:, 1], w_bf[:, 1])
+        quantise(v_codes[:, 0].rearrange("s g e -> s (g e)"), v_scales[:, 0].rearrange("s g e -> s (g e)"), v_first[:].rearrange("s g e -> s (g e)"))
         quantise(v_codes[:, 1, 0], v_scales[:, 1, 0], v_last[0][:])
         inv = reuse.tile([P, 1], F32, name="inv", offset=5120, align_bytes=64)
         nc.vector.reciprocal(inv[:], total[:])
+        quantise(w_codes[:, 1], w_scales[:, 1], w_bf[:, 1])
         quantise(v_codes[:, 1, 1], v_scales[:, 1, 1], v_last[1][:])
         y_out = out.rearrange("b q e -> (b q) e")
         acc = [bank(j, [P, P], "acc") for j in range(DV // P)]
-        for j in range(DV // P):
-            for g in range(2):
+        for g in range(2):
+            for j in range(DV // P):
                 nc.tensor.matmul_mx(acc[j][:], lhsT=w_codes[:, g].bitcast(FP8X4), lhsT_scale=w_scales[:, g],
                                     rhs=v_codes[:, j, g].bitcast(FP8X4), rhs_scale=v_scales[:, j, g], start=(g == 0), stop=(g == 1))
         y = [keep.tile([P, P], F32, name="y%d" % j) for j in range(DV // P)]

@@ -10,6 +10,7 @@ HALF = 512
 QUARTER = 256
 RUN = T // P
 PAGE = 4096
+LANES = 16
 
 F32 = mybir.dt.float32
 BF16 = mybir.dt.bfloat16
@@ -21,9 +22,8 @@ MULT = mybir.AluOpType.mult
 ADD = mybir.AluOpType.add
 MAX = mybir.AluOpType.max
 MIN = mybir.AluOpType.min
-AXY = mybir.AxisListType.XY
+AX = mybir.AxisListType.X
 COPY = mybir.ActivationFunctionType.Copy
-IDENTITY = mybir.ActivationFunctionType.Identity
 EXP = mybir.ActivationFunctionType.Exp
 
 FLOPS = 2 * NQ * N * (D + DV)
@@ -40,31 +40,31 @@ def tile_attend_x_ks_sink_topk_kernel(tc, qT, kT, vT, ks, vs, sink, offs, out):
         def bank(b, shape, name):
             return psum.tile(shape, F32, name=name, tag="bank%d" % b)
 
-        def slot(shape, dtype, name, tag):
-            return keep.tile(shape, dtype, name=name, tag=tag, align_bytes=PAGE if tag.startswith("k_raw") else 64)
-
         k_rows = kT.rearrange("(p t) n -> p t n", t=PACK)
-        k_raw = [slot([P, T], F32, "k_raw%d" % t, "k_raw%d" % t) for t in range(PACK)]
-        v_raw = [keep.tile([P, T], F32, name="v_raw0", align_bytes=PAGE), reuse.tile([P, T], F32, name="v_raw1", offset=0, align_bytes=PAGE)]
+        k_raw = [keep.tile([P, T], F32, name="k_raw%d" % t, align_bytes=PAGE) for t in range(PACK)]
+        v_raw = [reuse.tile([P, T], F32, name="v_raw%d" % j, offset=4 * T * j, align_bytes=PAGE) for j in range(DV // P)]
         ks_run = keep.tile([P, RUN], F32, name="ks_run")
         nc.scalar.dma_start(ks_run[:], ks[0:1, :].rearrange("o (p c) -> (o p) c", c=RUN))
         vs_pool = keep.tile([P, T], F32, name="vs_pool")
         nc.scalar.dma_start(vs_pool[P - 1 : P, T // 2 : T], vs[0:1, T // 2 : T])
-        offsets = keep.tile([P, N // 16], U16, name="offsets")
+        offsets = keep.tile([P, N // LANES], U16, name="offsets")
         nc.sync.dma_start(offsets[:], offs)
         nc.sync.dma_start(vs_pool[63:64, 0 : T // 2], vs[0:1, 0 : T // 2])
         nc.vector.memset(vs_pool[0:63, 0 : T // 2], 0.0)
         nc.vector.memset(vs_pool[64:P, 0 : T // 2], 0.0)
         nc.vector.memset(vs_pool[0 : P - 1, T // 2 : T], 0.0)
-        logits = slot([P, N + QUARTER], F32, "logits", "logits")
-        sink_col = logits[:, N : N + 1]
+        logits_b = keep.tile([P, HALF + 8], F32, name="logits_b")
+        sink_col = logits_b[:, HALF : HALF + 1]
         nc.scalar.dma_start(sink_col, sink.rearrange("b q o -> (b q) o"))
-        for t in range(PACK):
-            nc.sync.dma_start(k_raw[t][:], k_rows[:, t, :])
         q_raw = keep.tile([P, PACK, NQ], F32, name="q_raw")
         nc.sync.dma_start(q_raw[:], qT.rearrange("b (p t) q -> p (b t) q", t=PACK))
+        for t in range(PACK):
+            nc.sync.dma_start(k_raw[t][:], k_rows[:, t, :])
         for j in range(DV // P):
             nc.sync.dma_start(v_raw[j][:], vT[j * P : (j + 1) * P, :])
+
+        def listed(pool, first, count):
+            return pool[:].indirect(offsets[:, first // LANES : (first + count) // LANES])
 
         ident = keep.tile([P, P], F32, name="ident")
         make_identity(nc, ident[:])
@@ -77,138 +77,137 @@ def tile_attend_x_ks_sink_topk_kernel(tc, qT, kT, vT, ks, vs, sink, offs, out):
                 nc.tensor.transpose(turned[:, c, :], ks_run[:, 4 * b + c : 4 * b + c + 1].to_broadcast([P, P]), ident[:])
             nc.scalar.activation(by_run[:, :, 4 * b : 4 * b + 4], turned[:].rearrange("r c p -> r p c"), COPY)
 
-        k_bf = [keep.tile([P, HALF, PACK], BF16, name="k_bf%d" % h, align_bytes=64) for h in range(2)]
-        k_scales = keep.tile([P, N], U8, name="k_scales", align_bytes=64)
-        k_got = keep.tile([P, 2, N], F32, name="k_got")
+        ks_got = keep.tile([P, N], F32, name="ks_got")
+        nc.scalar.activation(ks_got[:], listed(ks_pool, 0, N), COPY)
+
+        ks_dealt = keep.tile([P, N // QUARTER, PACK, QUARTER // PACK], F32, name="ks_dealt")
+        nc.vector.tensor_copy(ks_dealt[:], ks_got[:].rearrange("q (c s t) -> q c t s", t=PACK, c=N // QUARTER))
+
         vs_got = keep.tile([P, N], F32, name="vs_got")
-        nc.vector.tensor_copy(vs_got[:], vs_pool[:].indirect(offsets[:]))
-        for t in range(2):
-            nc.vector.tensor_copy(k_got[:, t, :], k_raw[t][:].indirect(offsets[:]))
-        ks_got = slot([P, N], F32, "ks_got", "k_raw1")
-        nc.vector.tensor_copy(ks_got[:], ks_pool[:].indirect(offsets[:]))
-        for h in range(2):
-            nc.scalar.copy(k_bf[h][:, :, 0:2], k_got[:, :, h * HALF : (h + 1) * HALF].rearrange("p t n -> p n t"))
-        vs_parts = keep.tile([P, 2, PACK, 2], F32, name="vs_parts")
-        vs_col = keep.tile([P, 2, PACK], F32, name="vs_col")
-        vs_all = [keep.tile([P, 2, P, 2], F32, name="vs_all%d" % g) for g in range(2)]
+        nc.vector.tensor_copy(vs_got[:], listed(vs_pool, 0, N))
+        vs_col = [reuse.tile([P, PACK], F32, name="vs_col%d" % g, offset=8 * T + 4096 + 2048 * g, align_bytes=64) for g in range(2)]
         for g in range(2):
-            turned = bank(g, [P, PACK, P], "vs_turned")
-            for c in range(PACK):
-                nc.tensor.transpose(turned[:, c, :], vs_got[:, g * HALF + c * P : g * HALF + (c + 1) * P], ident[:])
-            nc.scalar.copy(vs_parts[:, g], turned[:, :, 63::64])
-        nc.gpsimd.tensor_tensor(vs_col[:], vs_parts[:, :, :, 0], vs_parts[:, :, :, 1], ADD)
-        for g in range(2):
-            spread = bank(2 + g, [P, HALF], "vs_spread")
-            for c in range(PACK):
-                nc.tensor.transpose(spread[:, c * P : (c + 1) * P], vs_col[:, g, c : c + 1].to_broadcast([P, P]), ident[:])
-            nc.scalar.copy(vs_all[g][:], spread[:].rearrange("r (s u e) -> r u s e", u=2, e=2))
+            turned = bank(2 + g, [P, PACK, P], "vs_turned")
+            for t in range(PACK):
+                nc.tensor.transpose(turned[:, t, :], vs_got[:, g * HALF + t : (g + 1) * HALF : PACK], ident[:])
+            nc.vector.tensor_reduce(vs_col[g][:], turned[:, :, 63::64], AX, ADD)
 
-        k_late = [slot([P, 2, QUARTER], BF16, "k_late%d" % c, "k_late%d" % c) for c in range(2)]
-        nc.vector.tensor_copy(k_bf[0][:, :, 2], k_raw[2][:].indirect(offsets[:, 0:32]))
-        for t in range(2, PACK):
-            for c in (1, 0):
-                nc.vector.tensor_copy(k_late[c][:, t - 2, :], k_raw[t][:].indirect(offsets[:, 32 + 16 * c : 48 + 16 * c]))
-        nc.vector.tensor_copy(k_bf[0][:, :, 3], k_raw[3][:].indirect(offsets[:, 0:32]))
-        q_bf = reuse.tile([P, NQ, PACK], BF16, name="q_bf", offset=4 * T + 2 * QUARTER, align_bytes=64)
-        nc.gpsimd.tensor_scalar(q_bf[:], q_raw[:].rearrange("p t q -> p q t"), 1.0, 0.0, MULT, ADD)
-        q_codes = slot([P, NQ], U32, "q_codes", "k_raw3")
+        k_first = keep.tile([P, HALF, PACK], BF16, name="k_first", align_bytes=64)
+        k_bf = [k_first[:, 0:QUARTER, :], k_first[:, QUARTER:HALF, :]]
+        k_bf.extend(reuse.tile([P, QUARTER, PACK], BF16, name="k_bf%d" % c, offset=8 * T + 2048 * (c - 2), align_bytes=64)[:] for c in (2, 3))
+        k_got = [[keep.tile([P, 2, QUARTER], BF16, name="k_got%d%d" % (pair, h)) for h in range(2)] for pair in range(2)]
+        for t in range(PACK):
+            nc.vector.tensor_copy(k_first[:, :, t], listed(k_raw[t], 0, HALF))
+            for h in range(2):
+                nc.scalar.activation(k_got[t // 2][h][:, t % 2, :], listed(k_raw[t], HALF + h * QUARTER, QUARTER), COPY)
+            if t % 2 == 1:
+                for h in range(2):
+                    nc.scalar.copy(k_bf[2 + h][:, :, t - 1 : t + 1], k_got[t // 2][h][:].rearrange("p t n -> p n t"))
+
+        q_bf = keep.tile([P, NQ, PACK], BF16, name="q_bf", align_bytes=64)
+        nc.vector.tensor_copy(q_bf[:], q_raw[:].rearrange("p t q -> p q t"))
+        q_codes = keep.tile([P, NQ], U32, name="q_codes", align_bytes=64)
         q_scales = keep.tile([P, NQ], U8, name="q_scales", align_bytes=64)
-        for c in (1, 0):
-            nc.scalar.copy(k_bf[1][:, c * QUARTER : (c + 1) * QUARTER, 2:4], k_late[c][:].rearrange("p t n -> p n t"))
-        scores = [bank(c, [P, QUARTER], "scores") for c in range(4)]
-        k_codes = {}
-        for c in (3, 2, 0, 1):
-            s = slice(c * QUARTER, (c + 1) * QUARTER)
-            within = slice((c % 2) * QUARTER, (c % 2 + 1) * QUARTER)
-            k_codes[c] = reuse.tile([P, QUARTER], U32, name="k_codes%d" % c, offset=4 * T + 4 * QUARTER * c, align_bytes=64)
-            nc.vector.quantize_mx(k_codes[c][:].bitcast(FP8X4), k_scales[:, s], k_bf[c // 2][:, within, :].rearrange("p n t -> p (n t)"))
-            if c == 3:
-                nc.vector.quantize_mx(q_codes[:].bitcast(FP8X4), q_scales[:], q_bf[:].rearrange("p q t -> p (q t)"))
-        for c in (3, 2, 0, 1):
-            s = slice(c * QUARTER, (c + 1) * QUARTER)
-            nc.tensor.matmul_mx(scores[c][:], lhsT=q_codes[:].bitcast(FP8X4), lhsT_scale=q_scales[:],
-                                rhs=k_codes[c][:].bitcast(FP8X4), rhs_scale=k_scales[:, s], start=True, stop=True)
-
-        unscaled = keep.tile([P, QUARTER], F32, name="unscaled")
-        nc.scalar.copy(unscaled[:], scores[3][:])
-        nc.gpsimd.tensor_tensor(logits[:, 3 * QUARTER : N], unscaled[:], ks_got[:, 3 * QUARTER : N], MULT)
-        for c in (2, 0, 1):
-            s = slice(c * QUARTER, (c + 1) * QUARTER)
-            nc.vector.tensor_tensor(logits[:, s], scores[c][:], ks_got[:, s], MULT)
-        m_neg = keep.tile([P, 1], F32, name="m_neg")
-        m_parts = keep.tile([P, 2], F32, name="m_parts")
-        even = logits[:, 0:N].rearrange("q (h s) -> q h s", h=2)[:, :, 0:QUARTER]
-        odd = logits[:, QUARTER : N + QUARTER].rearrange("q (h s) -> q h s", h=2)[:, :, 0 : QUARTER + 1]
-        nc.vector.tensor_reduce(m_parts[:, 0:1], even, AXY, MAX, negate=True)
-        nc.vector.tensor_reduce(m_parts[:, 1:2], odd, AXY, MAX, negate=True)
-        nc.gpsimd.tensor_scalar(m_neg[:], m_parts[:, 0:1], m_parts[:, 1:2], None, MIN)
-        p = [keep.tile([P, 2, P, 2], F32, name="p%d" % g) for g in range(2)]
-        sums = keep.tile([P, 3], F32, name="sums")
-        for g in range(2):
-            nc.scalar.activation(p[g][:].rearrange("q u s e -> q s u e"),
-                                 logits[:, g * HALF : (g + 1) * HALF].rearrange("q (s u e) -> q s u e", u=2, e=2),
-                                 EXP, bias=m_neg[:], accum_out=sums[:, g : g + 1])
-        nc.scalar.activation(sums[:, 2:3], sink_col, EXP, bias=m_neg[:])
-        terms = keep.tile([P, 3], F32, name="terms")
-        total = keep.tile([P, 1], F32, name="total")
-        nc.scalar.activation(terms[:], sums[:], IDENTITY, accum_out=total[:])
-
-        v_got = [slot([P, N], BF16, "v_got0", "k_raw1"), keep.tile([P, N], BF16, name="v_got1")]
-        for j in range(DV // P):
-            for g in range(2):
-                nc.vector.tensor_copy(v_got[j][:, g * HALF : (g + 1) * HALF], v_raw[j][:].indirect(offsets[:, g * 32 : (g + 1) * 32]))
-
-        w_rows = [keep.tile([P, HALF], BF16, name="w_rows%d" % g) for g in range(2)]
-        for g in range(2):
-            nc.gpsimd.tensor_tensor(w_rows[g][:], p[g][:].rearrange("q u s e -> q (u s e)"),
-                                    vs_all[g][:].rearrange("q u s e -> q (u s e)"), MULT)
-        w_bf = keep.tile([P, 2, NQ * PACK], BF16, name="w_bf", align_bytes=64)
-        v_first = slot([P, 2, P * PACK], BF16, "v_first", "logits")
-        v_last = [keep.tile([P, P * PACK], BF16, name="v_last%d" % g, align_bytes=64) for g in range(2)]
-        w_codes = reuse.tile([P, 2, NQ], U32, name="w_codes", offset=2048, align_bytes=64)
-        v_codes = reuse.tile([P, 2, 2, P], U32, name="v_codes", offset=3072, align_bytes=64)
-        w_scales = keep.tile([P, 2, NQ], U8, name="w_scales", align_bytes=64)
-        v_scales = keep.tile([P, 2, 2, P], U8, name="v_scales", align_bytes=64)
-
-        def turn(b, first, second, dest):
-            turned = bank(b, [P, 2, P], "turned")
-            nc.tensor.transpose(turned[:, 0, :], first, ident[:])
-            nc.tensor.transpose(turned[:, 1, :], second, ident[:])
-            nc.scalar.copy(dest.bitcast(F32).rearrange("s (x u) -> s x u", u=2), turned[:].rearrange("s u x -> s x u"))
-
-        def turn_values(j, g, dest):
-            words = v_got[j][:].bitcast(F32)
-            turn(4 + 2 * j + g, words[:, g * 256 : (g + 1) * 256 : 2], words[:, g * 256 + 1 : (g + 1) * 256 : 2], dest)
-
-        def turn_weights(g):
-            words = w_rows[g][:].bitcast(F32)
-            turn(2 + g, words[:, 0:P], words[:, P : 2 * P], w_bf[:, g, :])
-
-        turn_values(0, 0, v_first[:, 0, :])
-        turn_weights(0)
-        turn_values(0, 1, v_first[:, 1, :])
-        turn_values(1, 0, v_last[0][:])
-        turn_weights(1)
-        turn_values(1, 1, v_last[1][:])
 
         def quantise(codes, scales, values):
             nc.vector.quantize_mx(codes.bitcast(FP8X4), scales, values)
 
-        quantise(w_codes[:, 0], w_scales[:, 0], w_bf[:, 0])
-        quantise(v_codes[:, 0].rearrange("s g e -> s (g e)"), v_scales[:, 0].rearrange("s g e -> s (g e)"), v_first[:].rearrange("s g e -> s (g e)"))
-        quantise(v_codes[:, 1, 0], v_scales[:, 1, 0], v_last[0][:])
-        inv = reuse.tile([P, 1], F32, name="inv", offset=5120, align_bytes=64)
-        nc.vector.reciprocal(inv[:], total[:])
-        quantise(w_codes[:, 1], w_scales[:, 1], w_bf[:, 1])
-        quantise(v_codes[:, 1, 1], v_scales[:, 1, 1], v_last[1][:])
-        y_out = out.rearrange("b q e -> (b q) e")
-        acc = [bank(j, [P, P], "acc") for j in range(DV // P)]
+        quantise(q_codes[:], q_scales[:], q_bf[:].rearrange("p q t -> p (q t)"))
+        order = (0, 1, 2, 3)
+        scores = {}
+        for c in order:
+            k_codes = keep.tile([P, QUARTER], U32, name="k_codes%d" % c, align_bytes=64)
+            k_scales = keep.tile([P, QUARTER], U8, name="k_scales%d" % c, align_bytes=64)
+            quantise(k_codes[:], k_scales[:], k_bf[c].rearrange("p n t -> p (n t)"))
+            scores[c] = bank(c, [P, QUARTER], "scores")
+            nc.tensor.matmul_mx(scores[c][:], lhsT=q_codes[:].bitcast(FP8X4), lhsT_scale=q_scales[:],
+                                rhs=k_codes[:].bitcast(FP8X4), rhs_scale=k_scales[:], start=True, stop=True)
+
+        logits = [reuse.tile([P, HALF], F32, name="logits_a", offset=8 * T, align_bytes=64), logits_b]
+        unscaled = keep.tile([P, PACK, QUARTER // PACK], F32, name="unscaled")
+        for c in order:
+            place = logits[c // 2][:, (c % 2) * QUARTER : (c % 2 + 1) * QUARTER].rearrange("q (t s) -> q t s", t=PACK)
+            raw = scores[c][:].rearrange("q (s t) -> q t s", t=PACK)
+            if c == 2:
+                nc.scalar.copy(unscaled[:], raw)
+                nc.gpsimd.tensor_tensor(place, unscaled[:], ks_dealt[:, c], MULT)
+            else:
+                nc.vector.tensor_tensor(place, raw, ks_dealt[:, c], MULT)
+        m_parts = reuse.tile([P, 2], F32, name="m_parts", offset=8 * T + 2048, align_bytes=64)
         for g in range(2):
-            for j in range(DV // P):
-                nc.tensor.matmul_mx(acc[j][:], lhsT=w_codes[:, g].bitcast(FP8X4), lhsT_scale=w_scales[:, g],
-                                    rhs=v_codes[:, j, g].bitcast(FP8X4), rhs_scale=v_scales[:, j, g], start=(g == 0), stop=(g == 1))
-        y = [keep.tile([P, P], F32, name="y%d" % j) for j in range(DV // P)]
-        nc.scalar.activation(y[0][:], acc[0][:], COPY, scale=inv[:])
-        nc.vector.tensor_scalar(y[1][:], acc[1][:], inv[:], None, MULT)
+            nc.vector.tensor_reduce(m_parts[:, g : g + 1], logits[g][:, 0 : HALF + g], AX, MAX, negate=True)
+        m_neg = keep.tile([P, 1], F32, name="m_neg")
+        nc.gpsimd.tensor_scalar(m_neg[:], m_parts[:, 0:1], m_parts[:, 1:2], None, MIN)
+        v_got = [[keep.tile([P, HALF], BF16, name="v_got0%d" % g) for g in range(2)],
+                 [reuse.tile([P, HALF], BF16, name="v_got1%d" % g, offset=8 * T + 4096 + 1024 * g, align_bytes=64) for g in range(2)]]
+        nc.scalar.activation(v_got[0][0][:], listed(v_raw[0], 0, HALF), COPY)
+        nc.scalar.activation(v_got[0][1][:, 0:QUARTER], listed(v_raw[0], HALF, QUARTER), COPY)
+        nc.vector.tensor_copy(v_got[0][1][:, QUARTER:HALF], listed(v_raw[0], HALF + QUARTER, QUARTER))
+        p = [reuse.tile([P, PACK, P], F32, name="p%d" % g, offset=PAGE * g, align_bytes=64) for g in range(2)]
+        sums = reuse.tile([P, 3], F32, name="sums", offset=2 * PAGE, align_bytes=64)
+        for g in range(2):
+            nc.scalar.activation(p[g][:].rearrange("q t (h s) -> q h t s", h=2), logits[g][:, 0:HALF].rearrange("q (h t s) -> q h t s", h=2, t=PACK),
+                                 EXP, bias=m_neg[:], accum_out=sums[:, g : g + 1])
+        nc.scalar.activation(sums[:, 2:3], sink_col, EXP, bias=m_neg[:])
+        total = keep.tile([P, 1], F32, name="total")
+        nc.gpsimd.tensor_scalar(total[:], sums[:, 0:1], sums[:, 1:2], sums[:, 2:3], ADD, ADD)
+
+
+        v_first = keep.tile([P, 2, P * PACK], BF16, name="v_first", align_bytes=64)
+        v_last = [keep.tile([P, P * PACK], BF16, name="v_last%d" % g, align_bytes=64) for g in range(2)]
+
+        def turn_values(b, got, dest, copy):
+            words = got.bitcast(F32)
+            turned = bank(b, [P, 2, P], "v_turned")
+            for u in range(2):
+                nc.tensor.transpose(turned[:, u, :], words[:, u : HALF // 2 : 2], ident[:])
+            copy(dest.bitcast(F32).rearrange("s (x u) -> s x u", u=2), turned[:].rearrange("s u x -> s x u"))
+
+        for g in range(2):
+            turn_values(6 + g, v_got[0][g][:], v_first[:, g, :], nc.vector.tensor_copy)
+        w_bf = [keep.tile([P, NQ, PACK], BF16, name="w_bf0", align_bytes=64),
+                reuse.tile([P, NQ, PACK], BF16, name="w_bf1", offset=4 * T + 4096, align_bytes=64)]
+        p_turned = [bank(4 + g, [P, PACK, NQ], "p_turned") for g in range(2)]
+        for g in range(2):
+            for t in range(PACK):
+                nc.tensor.transpose(p_turned[g][:, t, :], p[g][:, t, :], ident[:])
+
+        def weigh(g):
+            nc.vector.tensor_tensor(w_bf[g][:], p_turned[g][:].rearrange("s t q -> s q t"),
+                                    vs_col[g][:].unsqueeze(1).to_broadcast([P, NQ, PACK]), MULT)
+
+        w_codes = [reuse.tile([P, NQ], U32, name="w_codes%d" % g, offset=4 * T + 512 * g, align_bytes=64) for g in range(2)]
+        w_scales = [keep.tile([P, NQ], U8, name="w_scales%d" % g, align_bytes=64) for g in range(2)]
+        first_codes = keep.tile([P, 2, P], U32, name="first_codes", align_bytes=64)
+        first_scales = keep.tile([P, 2, P], U8, name="first_scales", align_bytes=64)
+        last_codes = keep.tile([P, 2, P], U32, name="last_codes", align_bytes=64)
+        last_scales = keep.tile([P, 2, P], U8, name="last_scales", align_bytes=64)
+        quantise(first_codes[:].rearrange("s g e -> s (g e)"), first_scales[:].rearrange("s g e -> s (g e)"), v_first[:].rearrange("s g e -> s (g e)"))
+        weigh(0)
+        for g in range(2):
+            nc.vector.tensor_copy(v_got[1][g][:, 0:QUARTER], listed(v_raw[1], g * HALF, QUARTER))
+            nc.scalar.activation(v_got[1][g][:, QUARTER:HALF], listed(v_raw[1], g * HALF + QUARTER, QUARTER), COPY)
+        for g in range(2):
+            turn_values(g, v_got[1][g][:], v_last[g][:], nc.scalar.copy)
+        weigh(1)
+        quantise(w_codes[0][:], w_scales[0][:], w_bf[0][:].rearrange("s q t -> s (q t)"))
+        quantise(last_codes[:, 0], last_scales[:, 0], v_last[0][:])
+        quantise(w_codes[1][:], w_scales[1][:], w_bf[1][:].rearrange("s q t -> s (q t)"))
+        inv = reuse.tile([P, 1], F32, name="inv", offset=4 * T + 2048, align_bytes=64)
+        nc.vector.reciprocal(inv[:], total[:])
+        quantise(last_codes[:, 1], last_scales[:, 1], v_last[1][:])
+
+        y_out = out.rearrange("b q e -> (b q) e")
+        v_codes = (first_codes, last_codes)
+        v_scales = (first_scales, last_scales)
         for j in range(DV // P):
-            nc.sync.dma_start(y_out[:, j * P : (j + 1) * P], y[j][:])
+            acc = bank(2 + j, [P, P], "acc")
+            for g in range(2):
+                nc.tensor.matmul_mx(acc[:], lhsT=w_codes[g][:].bitcast(FP8X4), lhsT_scale=w_scales[g][:],
+                                    rhs=v_codes[j][:, g].bitcast(FP8X4), rhs_scale=v_scales[j][:, g], start=(g == 0), stop=(g == 1))
+            y = keep.tile([P, P], F32, name="y%d" % j)
+            if j == 0:
+                nc.scalar.activation(y[:], acc[:], COPY, scale=inv[:])
+            else:
+                nc.vector.tensor_scalar(y[:], acc[:], inv[:], None, MULT)
+            nc.sync.dma_start(y_out[:, j * P : (j + 1) * P], y[:])

@@ -56,10 +56,10 @@ def tile_attend_x_ks_sink_topk_kernel(tc, qT, kT, vT, ks, vs, sink, offs, out):
         logits_b = keep.tile([P, HALF + 8], F32, name="logits_b")
         sink_col = logits_b[:, HALF : HALF + 1]
         nc.scalar.dma_start(sink_col, sink.rearrange("b q o -> (b q) o"))
-        q_raw = keep.tile([P, PACK, NQ], F32, name="q_raw")
-        nc.sync.dma_start(q_raw[:], qT.rearrange("b (p t) q -> p (b t) q", t=PACK))
         for t in range(PACK):
             nc.sync.dma_start(k_raw[t][:], k_rows[:, t, :])
+        q_raw = keep.tile([P, PACK, NQ], F32, name="q_raw")
+        nc.sync.dma_start(q_raw[:], qT.rearrange("b (p t) q -> p (b t) q", t=PACK))
         for j in range(DV // P):
             nc.sync.dma_start(v_raw[j][:], vT[j * P : (j + 1) * P, :])
 
@@ -78,19 +78,25 @@ def tile_attend_x_ks_sink_topk_kernel(tc, qT, kT, vT, ks, vs, sink, offs, out):
             nc.scalar.activation(by_run[:, :, 4 * b : 4 * b + 4], turned[:].rearrange("r c p -> r p c"), COPY)
 
         ks_got = keep.tile([P, N], F32, name="ks_got")
-        nc.scalar.activation(ks_got[:], listed(ks_pool, 0, N), COPY)
-
-        ks_dealt = keep.tile([P, N // QUARTER, PACK, QUARTER // PACK], F32, name="ks_dealt")
-        nc.vector.tensor_copy(ks_dealt[:], ks_got[:].rearrange("q (c s t) -> q c t s", t=PACK, c=N // QUARTER))
+        nc.vector.tensor_copy(ks_got[:], listed(ks_pool, 0, N))
+        ks_a = keep.tile([P, 2, P, 2], F32, name="ks_a")
+        nc.scalar.copy(ks_a[:], ks_got[:, 0:HALF].rearrange("q (s u e) -> q u s e", u=2, e=2))
+        ks_b = reuse.tile([P, 2, PACK, QUARTER // PACK], F32, name="ks_b", offset=8 * T + 12288, align_bytes=64)
+        nc.scalar.copy(ks_b[:], ks_got[:, HALF:N].rearrange("q (h s t) -> q h t s", t=PACK, h=2))
 
         vs_got = keep.tile([P, N], F32, name="vs_got")
         nc.vector.tensor_copy(vs_got[:], listed(vs_pool, 0, N))
-        vs_col = [reuse.tile([P, PACK], F32, name="vs_col%d" % g, offset=8 * T + 4096 + 2048 * g, align_bytes=64) for g in range(2)]
+        vs_col = [keep.tile([P, PACK], F32, name="vs_col%d" % g) for g in range(2)]
         for g in range(2):
             turned = bank(2 + g, [P, PACK, P], "vs_turned")
             for t in range(PACK):
                 nc.tensor.transpose(turned[:, t, :], vs_got[:, g * HALF + t : (g + 1) * HALF : PACK], ident[:])
             nc.vector.tensor_reduce(vs_col[g][:], turned[:, :, 63::64], AX, ADD)
+        spread = bank(2, [P, PACK, P], "vs_spread")
+        for t in range(PACK):
+            nc.tensor.transpose(spread[:, t, :], vs_col[0][:, t : t + 1].to_broadcast([P, P]), ident[:])
+        vs_a = keep.tile([P, 2, P, 2], F32, name="vs_a")
+        nc.scalar.copy(vs_a[:], spread[:].rearrange("r (u e) s -> r u s e", u=2))
 
         k_first = keep.tile([P, HALF, PACK], BF16, name="k_first", align_bytes=64)
         k_bf = [k_first[:, 0:QUARTER, :], k_first[:, QUARTER:HALF, :]]
@@ -104,95 +110,105 @@ def tile_attend_x_ks_sink_topk_kernel(tc, qT, kT, vT, ks, vs, sink, offs, out):
                 for h in range(2):
                     nc.scalar.copy(k_bf[2 + h][:, :, t - 1 : t + 1], k_got[t // 2][h][:].rearrange("p t n -> p n t"))
 
-        q_bf = keep.tile([P, NQ, PACK], BF16, name="q_bf", align_bytes=64)
-        nc.vector.tensor_copy(q_bf[:], q_raw[:].rearrange("p t q -> p q t"))
+        q_bf = reuse.tile([P, NQ, PACK], BF16, name="q_bf", offset=8 * T + 4096, align_bytes=64)
+        nc.gpsimd.tensor_scalar(q_bf[:], q_raw[:].rearrange("p t q -> p q t"), 1.0, 0.0, MULT, ADD)
         q_codes = keep.tile([P, NQ], U32, name="q_codes", align_bytes=64)
         q_scales = keep.tile([P, NQ], U8, name="q_scales", align_bytes=64)
 
         def quantise(codes, scales, values):
             nc.vector.quantize_mx(codes.bitcast(FP8X4), scales, values)
 
-        quantise(q_codes[:], q_scales[:], q_bf[:].rearrange("p q t -> p (q t)"))
-        order = (0, 1, 2, 3)
-        scores = {}
-        for c in order:
-            k_codes = keep.tile([P, QUARTER], U32, name="k_codes%d" % c, align_bytes=64)
-            k_scales = keep.tile([P, QUARTER], U8, name="k_scales%d" % c, align_bytes=64)
-            quantise(k_codes[:], k_scales[:], k_bf[c].rearrange("p n t -> p (n t)"))
-            scores[c] = bank(c, [P, QUARTER], "scores")
+        k_codes = [keep.tile([P, QUARTER], U32, name="k_codes%d" % c, align_bytes=64) for c in range(4)]
+        k_scales = [keep.tile([P, QUARTER], U8, name="k_scales0", align_bytes=64)]
+        k_scales.extend(reuse.tile([P, QUARTER], U8, name="k_scales%d" % c, offset=8 * T + 4096 + QUARTER * c, align_bytes=64) for c in (1, 2, 3))
+        scores = []
+        for c in range(4):
+            if c == 1:
+                quantise(q_codes[:], q_scales[:], q_bf[:].rearrange("p q t -> p (q t)"))
+            quantise(k_codes[c][:], k_scales[c][:], k_bf[c].rearrange("p n t -> p (n t)"))
+        for c in range(4):
+            scores.append(bank(c, [P, QUARTER], "scores"))
             nc.tensor.matmul_mx(scores[c][:], lhsT=q_codes[:].bitcast(FP8X4), lhsT_scale=q_scales[:],
-                                rhs=k_codes[:].bitcast(FP8X4), rhs_scale=k_scales[:], start=True, stop=True)
+                                rhs=k_codes[c][:].bitcast(FP8X4), rhs_scale=k_scales[c][:], start=True, stop=True)
 
-        logits = [reuse.tile([P, HALF], F32, name="logits_a", offset=8 * T, align_bytes=64), logits_b]
-        unscaled = keep.tile([P, PACK, QUARTER // PACK], F32, name="unscaled")
-        for c in order:
-            place = logits[c // 2][:, (c % 2) * QUARTER : (c % 2 + 1) * QUARTER].rearrange("q (t s) -> q t s", t=PACK)
-            raw = scores[c][:].rearrange("q (s t) -> q t s", t=PACK)
-            if c == 2:
-                nc.scalar.copy(unscaled[:], raw)
-                nc.gpsimd.tensor_tensor(place, unscaled[:], ks_dealt[:, c], MULT)
-            else:
-                nc.vector.tensor_tensor(place, raw, ks_dealt[:, c], MULT)
+        logits_a = reuse.tile([P, 2, P, 2], F32, name="logits_a", offset=8 * T, align_bytes=64)
+        rows = QUARTER // PACK
+        for h in range(2):
+            place = slice(h * rows, (h + 1) * rows)
+            nc.vector.tensor_tensor(logits_a[:, :, place, :], scores[h][:].rearrange("q (s u e) -> q u s e", u=2, e=2), ks_a[:, :, place, :], MULT)
+        unscaled = keep.tile([P, PACK, rows], F32, name="unscaled")
+        dealt_b = logits_b[:, 0:HALF].rearrange("q (h t s) -> q h t s", h=2, t=PACK)
+        nc.scalar.copy(unscaled[:], scores[2][:].rearrange("q (s t) -> q t s", t=PACK))
+        nc.gpsimd.tensor_tensor(dealt_b[:, 0], unscaled[:], ks_b[:, 0], MULT)
+        nc.vector.tensor_tensor(dealt_b[:, 1], scores[3][:].rearrange("q (s t) -> q t s", t=PACK), ks_b[:, 1], MULT)
+        flat_a = logits_a[:].rearrange("q u s e -> q (u s e)")
         m_parts = reuse.tile([P, 2], F32, name="m_parts", offset=8 * T + 2048, align_bytes=64)
-        for g in range(2):
-            nc.vector.tensor_reduce(m_parts[:, g : g + 1], logits[g][:, 0 : HALF + g], AX, MAX, negate=True)
+        nc.vector.tensor_reduce(m_parts[:, 0:1], flat_a, AX, MAX, negate=True)
+        nc.vector.tensor_reduce(m_parts[:, 1:2], logits_b[:, 0 : HALF + 1], AX, MAX, negate=True)
         m_neg = keep.tile([P, 1], F32, name="m_neg")
         nc.gpsimd.tensor_scalar(m_neg[:], m_parts[:, 0:1], m_parts[:, 1:2], None, MIN)
-        v_got = [[keep.tile([P, HALF], BF16, name="v_got0%d" % g) for g in range(2)],
-                 [reuse.tile([P, HALF], BF16, name="v_got1%d" % g, offset=8 * T + 4096 + 1024 * g, align_bytes=64) for g in range(2)]]
+
+        got_at = 8 * T + 8192
+        v_got = [[reuse.tile([P, HALF], BF16, name="v_got00", offset=got_at, align_bytes=64), reuse.tile([P, HALF], BF16, name="v_got01", offset=8 * T + 12288, align_bytes=64)],
+                 [keep.tile([P, HALF], BF16, name="v_got1%d" % g) for g in range(2)]]
         nc.scalar.activation(v_got[0][0][:], listed(v_raw[0], 0, HALF), COPY)
-        nc.scalar.activation(v_got[0][1][:, 0:QUARTER], listed(v_raw[0], HALF, QUARTER), COPY)
-        nc.vector.tensor_copy(v_got[0][1][:, QUARTER:HALF], listed(v_raw[0], HALF + QUARTER, QUARTER))
-        p = [reuse.tile([P, PACK, P], F32, name="p%d" % g, offset=PAGE * g, align_bytes=64) for g in range(2)]
-        sums = reuse.tile([P, 3], F32, name="sums", offset=2 * PAGE, align_bytes=64)
-        for g in range(2):
-            nc.scalar.activation(p[g][:].rearrange("q t (h s) -> q h t s", h=2), logits[g][:, 0:HALF].rearrange("q (h t s) -> q h t s", h=2, t=PACK),
-                                 EXP, bias=m_neg[:], accum_out=sums[:, g : g + 1])
-        nc.scalar.activation(sums[:, 2:3], sink_col, EXP, bias=m_neg[:])
-        total = keep.tile([P, 1], F32, name="total")
-        nc.gpsimd.tensor_scalar(total[:], sums[:, 0:1], sums[:, 1:2], sums[:, 2:3], ADD, ADD)
-
-
+        nc.vector.tensor_copy(v_got[0][1][:], listed(v_raw[0], HALF, HALF))
         v_first = keep.tile([P, 2, P * PACK], BF16, name="v_first", align_bytes=64)
         v_last = [keep.tile([P, P * PACK], BF16, name="v_last%d" % g, align_bytes=64) for g in range(2)]
 
-        def turn_values(b, got, dest, copy):
+        def turn_pairs(b, first, second):
+            turned = bank(b, [P, 2, P], "pairs_turned")
+            nc.tensor.transpose(turned[:, 0, :], first, ident[:])
+            nc.tensor.transpose(turned[:, 1, :], second, ident[:])
+            return turned
+
+        def turn_values(b, got):
             words = got.bitcast(F32)
-            turned = bank(b, [P, 2, P], "v_turned")
-            for u in range(2):
-                nc.tensor.transpose(turned[:, u, :], words[:, u : HALF // 2 : 2], ident[:])
+            return turn_pairs(b, words[:, 0 : HALF // 2 : 2], words[:, 1 : HALF // 2 : 2])
+
+        def interleave(copy, dest, turned):
             copy(dest.bitcast(F32).rearrange("s (x u) -> s x u", u=2), turned[:].rearrange("s u x -> s x u"))
 
-        for g in range(2):
-            turn_values(6 + g, v_got[0][g][:], v_first[:, g, :], nc.vector.tensor_copy)
-        w_bf = [keep.tile([P, NQ, PACK], BF16, name="w_bf0", align_bytes=64),
-                reuse.tile([P, NQ, PACK], BF16, name="w_bf1", offset=4 * T + 4096, align_bytes=64)]
-        p_turned = [bank(4 + g, [P, PACK, NQ], "p_turned") for g in range(2)]
-        for g in range(2):
-            for t in range(PACK):
-                nc.tensor.transpose(p_turned[g][:, t, :], p[g][:, t, :], ident[:])
+        for g, copy in enumerate((nc.scalar.copy, nc.vector.tensor_copy)):
+            interleave(copy, v_first[:, g, :], turn_values(6, v_got[0][g][:]))
 
-        def weigh(g):
-            nc.vector.tensor_tensor(w_bf[g][:], p_turned[g][:].rearrange("s t q -> s q t"),
-                                    vs_col[g][:].unsqueeze(1).to_broadcast([P, NQ, PACK]), MULT)
+        p_a = reuse.tile([P, HALF], F32, name="p_a", offset=got_at - 1536, align_bytes=64)
+        sums = reuse.tile([P, 3], F32, name="sums", offset=got_at + 512, align_bytes=64)
+        p_b = reuse.tile([P, PACK, P], F32, name="p_b", offset=got_at + 576, align_bytes=64)
+        nc.scalar.activation(p_a[:], flat_a, EXP, bias=m_neg[:], accum_out=sums[:, 0:1])
+        nc.scalar.activation(p_b[:].rearrange("q t (h s) -> q h t s", h=2), dealt_b, EXP, bias=m_neg[:], accum_out=sums[:, 1:2])
+        nc.scalar.activation(sums[:, 2:3], sink_col, EXP, bias=m_neg[:])
+        w_rows = keep.tile([P, HALF], BF16, name="w_rows")
+        nc.gpsimd.tensor_tensor(w_rows[:], p_a[:], vs_a[:].rearrange("q u s e -> q (u s e)"), MULT)
+        total = keep.tile([P, 1], F32, name="total")
+        nc.gpsimd.tensor_scalar(total[:], sums[:, 0:1], sums[:, 1:2], sums[:, 2:3], ADD, ADD)
 
-        w_codes = [reuse.tile([P, NQ], U32, name="w_codes%d" % g, offset=4 * T + 512 * g, align_bytes=64) for g in range(2)]
-        w_scales = [keep.tile([P, NQ], U8, name="w_scales%d" % g, align_bytes=64) for g in range(2)]
+        p_turned = bank(5, [P, PACK, NQ], "p_turned")
+        for t in range(PACK):
+            nc.tensor.transpose(p_turned[:, t, :], p_b[:, t, :], ident[:])
+        w_words = w_rows[:].bitcast(F32)
+        w_turned = turn_pairs(4, w_words[:, 0:P], w_words[:, P : 2 * P])
+
         first_codes = keep.tile([P, 2, P], U32, name="first_codes", align_bytes=64)
         first_scales = keep.tile([P, 2, P], U8, name="first_scales", align_bytes=64)
-        last_codes = keep.tile([P, 2, P], U32, name="last_codes", align_bytes=64)
-        last_scales = keep.tile([P, 2, P], U8, name="last_scales", align_bytes=64)
         quantise(first_codes[:].rearrange("s g e -> s (g e)"), first_scales[:].rearrange("s g e -> s (g e)"), v_first[:].rearrange("s g e -> s (g e)"))
-        weigh(0)
+
         for g in range(2):
             nc.vector.tensor_copy(v_got[1][g][:, 0:QUARTER], listed(v_raw[1], g * HALF, QUARTER))
             nc.scalar.activation(v_got[1][g][:, QUARTER:HALF], listed(v_raw[1], g * HALF + QUARTER, QUARTER), COPY)
+        w_bf = [reuse.tile([P, NQ, PACK], BF16, name="w_bf%d" % g, offset=4 * T + 4096 + 1024 * g, align_bytes=64) for g in range(2)]
+        interleave(nc.scalar.copy, w_bf[0][:].rearrange("s q t -> s (q t)"), w_turned)
         for g in range(2):
-            turn_values(g, v_got[1][g][:], v_last[g][:], nc.scalar.copy)
-        weigh(1)
+            interleave(nc.scalar.copy, v_last[g][:], turn_values(g, v_got[1][g][:]))
+        nc.vector.tensor_tensor(w_bf[1][:], p_turned[:].rearrange("s t q -> s q t"), vs_col[1][:].unsqueeze(1).to_broadcast([P, NQ, PACK]), MULT)
+
+        w_codes = [keep.tile([P, NQ], U32, name="w_codes%d" % g, align_bytes=64) for g in range(2)]
+        w_scales = [keep.tile([P, NQ], U8, name="w_scales%d" % g, align_bytes=64) for g in range(2)]
+        last_codes = keep.tile([P, 2, P], U32, name="last_codes", align_bytes=64)
+        last_scales = keep.tile([P, 2, P], U8, name="last_scales", align_bytes=64)
         quantise(w_codes[0][:], w_scales[0][:], w_bf[0][:].rearrange("s q t -> s (q t)"))
-        quantise(last_codes[:, 0], last_scales[:, 0], v_last[0][:])
         quantise(w_codes[1][:], w_scales[1][:], w_bf[1][:].rearrange("s q t -> s (q t)"))
+        quantise(last_codes[:, 0], last_scales[:, 0], v_last[0][:])
         inv = reuse.tile([P, 1], F32, name="inv", offset=4 * T + 2048, align_bytes=64)
         nc.vector.reciprocal(inv[:], total[:])
         quantise(last_codes[:, 1], last_scales[:, 1], v_last[1][:])

@@ -81,8 +81,8 @@ def tile_attend_x_ks_sink_topk_kernel(tc, qT, kT, vT, ks, vs, sink, offs, out):
         nc.vector.tensor_copy(ks_got[:], listed(ks_pool, 0, N))
         ks_a = keep.tile([P, 2, P, 2], F32, name="ks_a")
         nc.scalar.copy(ks_a[:], ks_got[:, 0:HALF].rearrange("q (s u e) -> q u s e", u=2, e=2))
-        ks_b = reuse.tile([P, 2, PACK, QUARTER // PACK], F32, name="ks_b", offset=8 * T + 12288, align_bytes=64)
-        nc.scalar.copy(ks_b[:], ks_got[:, HALF:N].rearrange("q (h s t) -> q h t s", t=PACK, h=2))
+        ks_b = reuse.tile([P, PACK, P], F32, name="ks_b", offset=8 * T + 12288, align_bytes=64)
+        nc.scalar.copy(ks_b[:], ks_got[:, HALF:N].rearrange("q (s t) -> q t s", t=PACK))
 
         vs_got = keep.tile([P, N], F32, name="vs_got")
         nc.vector.tensor_copy(vs_got[:], listed(vs_pool, 0, N))
@@ -137,10 +137,10 @@ def tile_attend_x_ks_sink_topk_kernel(tc, qT, kT, vT, ks, vs, sink, offs, out):
             place = slice(h * rows, (h + 1) * rows)
             nc.vector.tensor_tensor(logits_a[:, :, place, :], scores[h][:].rearrange("q (s u e) -> q u s e", u=2, e=2), ks_a[:, :, place, :], MULT)
         unscaled = keep.tile([P, PACK, rows], F32, name="unscaled")
-        dealt_b = logits_b[:, 0:HALF].rearrange("q (h t s) -> q h t s", h=2, t=PACK)
+        dealt_b = logits_b[:, 0:HALF].rearrange("q (t s) -> q t s", t=PACK)
         nc.scalar.copy(unscaled[:], scores[2][:].rearrange("q (s t) -> q t s", t=PACK))
-        nc.gpsimd.tensor_tensor(dealt_b[:, 0], unscaled[:], ks_b[:, 0], MULT)
-        nc.vector.tensor_tensor(dealt_b[:, 1], scores[3][:].rearrange("q (s t) -> q t s", t=PACK), ks_b[:, 1], MULT)
+        nc.gpsimd.tensor_tensor(dealt_b[:, :, 0:rows], unscaled[:], ks_b[:, :, 0:rows], MULT)
+        nc.vector.tensor_tensor(dealt_b[:, :, rows:P], scores[3][:].rearrange("q (s t) -> q t s", t=PACK), ks_b[:, :, rows:P], MULT)
         flat_a = logits_a[:].rearrange("q u s e -> q (u s e)")
         m_parts = reuse.tile([P, 2], F32, name="m_parts", offset=8 * T + 2048, align_bytes=64)
         nc.vector.tensor_reduce(m_parts[:, 0:1], flat_a, AX, MAX, negate=True)
@@ -148,13 +148,12 @@ def tile_attend_x_ks_sink_topk_kernel(tc, qT, kT, vT, ks, vs, sink, offs, out):
         m_neg = keep.tile([P, 1], F32, name="m_neg")
         nc.gpsimd.tensor_scalar(m_neg[:], m_parts[:, 0:1], m_parts[:, 1:2], None, MIN)
 
-        got_at = 8 * T + 8192
-        v_got = [[reuse.tile([P, HALF], BF16, name="v_got00", offset=got_at, align_bytes=64), reuse.tile([P, HALF], BF16, name="v_got01", offset=8 * T + 12288, align_bytes=64)],
+        v_got = [[keep.tile([P, HALF], BF16, name="v_got00"), reuse.tile([P, HALF], BF16, name="v_got01", offset=8 * T + 12288, align_bytes=64)],
                  [keep.tile([P, HALF], BF16, name="v_got1%d" % g) for g in range(2)]]
         nc.scalar.activation(v_got[0][0][:], listed(v_raw[0], 0, HALF), COPY)
-        nc.vector.tensor_copy(v_got[0][1][:], listed(v_raw[0], HALF, HALF))
+        nc.vector.tensor_copy(v_got[0][1][:, 0:QUARTER], listed(v_raw[0], HALF, QUARTER))
+        nc.scalar.activation(v_got[0][1][:, QUARTER:HALF], listed(v_raw[0], HALF + QUARTER, QUARTER), COPY)
         v_first = keep.tile([P, 2, P * PACK], BF16, name="v_first", align_bytes=64)
-        v_last = [keep.tile([P, P * PACK], BF16, name="v_last%d" % g, align_bytes=64) for g in range(2)]
 
         def turn_pairs(b, first, second):
             turned = bank(b, [P, 2, P], "pairs_turned")
@@ -169,23 +168,22 @@ def tile_attend_x_ks_sink_topk_kernel(tc, qT, kT, vT, ks, vs, sink, offs, out):
         def interleave(copy, dest, turned):
             copy(dest.bitcast(F32).rearrange("s (x u) -> s x u", u=2), turned[:].rearrange("s u x -> s x u"))
 
-        for g, copy in enumerate((nc.scalar.copy, nc.vector.tensor_copy)):
-            interleave(copy, v_first[:, g, :], turn_values(6, v_got[0][g][:]))
+        for g in range(2):
+            interleave(nc.vector.tensor_copy, v_first[:, g, :], turn_values(6 + g, v_got[0][g][:]))
 
-        p_a = reuse.tile([P, HALF], F32, name="p_a", offset=got_at - 1536, align_bytes=64)
-        sums = reuse.tile([P, 3], F32, name="sums", offset=got_at + 512, align_bytes=64)
-        p_b = reuse.tile([P, PACK, P], F32, name="p_b", offset=got_at + 576, align_bytes=64)
+        p_a = reuse.tile([P, HALF], F32, name="p_a", offset=0, align_bytes=64)
+        p_b = reuse.tile([P, HALF + 8], F32, name="p_b", offset=PAGE, align_bytes=64)
+        sums = keep.tile([P, 2], F32, name="sums")
         nc.scalar.activation(p_a[:], flat_a, EXP, bias=m_neg[:], accum_out=sums[:, 0:1])
-        nc.scalar.activation(p_b[:].rearrange("q t (h s) -> q h t s", h=2), dealt_b, EXP, bias=m_neg[:], accum_out=sums[:, 1:2])
-        nc.scalar.activation(sums[:, 2:3], sink_col, EXP, bias=m_neg[:])
+        nc.scalar.activation(p_b[:, 0 : HALF + 1], logits_b[:, 0 : HALF + 1], EXP, bias=m_neg[:], accum_out=sums[:, 1:2])
         w_rows = keep.tile([P, HALF], BF16, name="w_rows")
         nc.gpsimd.tensor_tensor(w_rows[:], p_a[:], vs_a[:].rearrange("q u s e -> q (u s e)"), MULT)
         total = keep.tile([P, 1], F32, name="total")
-        nc.gpsimd.tensor_scalar(total[:], sums[:, 0:1], sums[:, 1:2], sums[:, 2:3], ADD, ADD)
+        nc.gpsimd.tensor_tensor(total[:], sums[:, 0:1], sums[:, 1:2], ADD)
 
         p_turned = bank(5, [P, PACK, NQ], "p_turned")
         for t in range(PACK):
-            nc.tensor.transpose(p_turned[:, t, :], p_b[:, t, :], ident[:])
+            nc.tensor.transpose(p_turned[:, t, :], p_b[:, t * P : (t + 1) * P], ident[:])
         w_words = w_rows[:].bitcast(F32)
         w_turned = turn_pairs(4, w_words[:, 0:P], w_words[:, P : 2 * P])
 
@@ -196,22 +194,24 @@ def tile_attend_x_ks_sink_topk_kernel(tc, qT, kT, vT, ks, vs, sink, offs, out):
         for g in range(2):
             nc.vector.tensor_copy(v_got[1][g][:, 0:QUARTER], listed(v_raw[1], g * HALF, QUARTER))
             nc.scalar.activation(v_got[1][g][:, QUARTER:HALF], listed(v_raw[1], g * HALF + QUARTER, QUARTER), COPY)
-        w_bf = [reuse.tile([P, NQ, PACK], BF16, name="w_bf%d" % g, offset=4 * T + 4096 + 1024 * g, align_bytes=64) for g in range(2)]
-        interleave(nc.scalar.copy, w_bf[0][:].rearrange("s q t -> s (q t)"), w_turned)
+        w_bf = [reuse.tile([P, NQ * PACK], BF16, name="w_bf%d" % g, offset=4 * T + 1024 * g, align_bytes=64) for g in range(2)]
+        v_last = [keep.tile([P, P * PACK], BF16, name="v_last%d" % g, align_bytes=64) for g in range(2)]
+        interleave(nc.scalar.copy, w_bf[0][:], w_turned)
         for g in range(2):
             interleave(nc.scalar.copy, v_last[g][:], turn_values(g, v_got[1][g][:]))
-        nc.vector.tensor_tensor(w_bf[1][:], p_turned[:].rearrange("s t q -> s q t"), vs_col[1][:].unsqueeze(1).to_broadcast([P, NQ, PACK]), MULT)
+        nc.vector.tensor_tensor(w_bf[1][:].rearrange("s (q t) -> s q t", t=PACK), p_turned[:].rearrange("s t q -> s q t"),
+                                vs_col[1][:].unsqueeze(1).to_broadcast([P, NQ, PACK]), MULT)
 
         w_codes = [keep.tile([P, NQ], U32, name="w_codes%d" % g, align_bytes=64) for g in range(2)]
         w_scales = [keep.tile([P, NQ], U8, name="w_scales%d" % g, align_bytes=64) for g in range(2)]
         last_codes = keep.tile([P, 2, P], U32, name="last_codes", align_bytes=64)
         last_scales = keep.tile([P, 2, P], U8, name="last_scales", align_bytes=64)
-        quantise(w_codes[0][:], w_scales[0][:], w_bf[0][:].rearrange("s q t -> s (q t)"))
-        quantise(w_codes[1][:], w_scales[1][:], w_bf[1][:].rearrange("s q t -> s (q t)"))
-        quantise(last_codes[:, 0], last_scales[:, 0], v_last[0][:])
-        inv = reuse.tile([P, 1], F32, name="inv", offset=4 * T + 2048, align_bytes=64)
+        for g in range(2):
+            quantise(w_codes[g][:], w_scales[g][:], w_bf[g][:])
+        for g in range(2):
+            quantise(last_codes[:, g], last_scales[:, g], v_last[g][:])
+        inv = reuse.tile([P, 1], F32, name="inv", offset=4 * T + 1024, align_bytes=64)
         nc.vector.reciprocal(inv[:], total[:])
-        quantise(last_codes[:, 1], last_scales[:, 1], v_last[1][:])
 
         y_out = out.rearrange("b q e -> (b q) e")
         v_codes = (first_codes, last_codes)

@@ -53,9 +53,8 @@ def tile_attend_x_ks_sink_topk_kernel(tc, qT, kT, vT, ks, vs, sink, offs, out):
         nc.vector.memset(vs_pool[0:63, 0 : T // 2], 0.0)
         nc.vector.memset(vs_pool[64:P, 0 : T // 2], 0.0)
         nc.vector.memset(vs_pool[0 : P - 1, T // 2 : T], 0.0)
-        logits_b = keep.tile([P, HALF + 8], F32, name="logits_b")
-        sink_col = logits_b[:, HALF : HALF + 1]
-        nc.scalar.dma_start(sink_col, sink.rearrange("b q o -> (b q) o"))
+        sink_in = keep.tile([P, 1], F32, name="sink_in")
+        nc.scalar.dma_start(sink_in[:], sink.rearrange("b q o -> (b q) o"))
         for t in range(PACK):
             nc.sync.dma_start(k_raw[t][:], k_rows[:, t, :])
         q_raw = keep.tile([P, PACK, NQ], F32, name="q_raw")
@@ -80,9 +79,9 @@ def tile_attend_x_ks_sink_topk_kernel(tc, qT, kT, vT, ks, vs, sink, offs, out):
         ks_got = keep.tile([P, N], F32, name="ks_got")
         nc.vector.tensor_copy(ks_got[:], listed(ks_pool, 0, N))
         ks_a = keep.tile([P, 2, P, 2], F32, name="ks_a")
-        nc.scalar.copy(ks_a[:], ks_got[:, 0:HALF].rearrange("q (s u e) -> q u s e", u=2, e=2))
-        ks_b = reuse.tile([P, PACK, P], F32, name="ks_b", offset=8 * T + 12288, align_bytes=64)
-        nc.scalar.copy(ks_b[:], ks_got[:, HALF:N].rearrange("q (s t) -> q t s", t=PACK))
+        nc.vector.tensor_copy(ks_a[:], ks_got[:, 0:HALF].rearrange("q (s u e) -> q u s e", u=2, e=2))
+        ks_b = keep.tile([P, 2, PACK, QUARTER // PACK], F32, name="ks_b")
+        nc.vector.tensor_copy(ks_b[:], ks_got[:, HALF:N].rearrange("q (h s t) -> q h t s", t=PACK, h=2))
 
         vs_got = keep.tile([P, N], F32, name="vs_got")
         nc.vector.tensor_copy(vs_got[:], listed(vs_pool, 0, N))
@@ -100,7 +99,7 @@ def tile_attend_x_ks_sink_topk_kernel(tc, qT, kT, vT, ks, vs, sink, offs, out):
 
         k_first = keep.tile([P, HALF, PACK], BF16, name="k_first", align_bytes=64)
         k_bf = [k_first[:, 0:QUARTER, :], k_first[:, QUARTER:HALF, :]]
-        k_bf.extend(reuse.tile([P, QUARTER, PACK], BF16, name="k_bf%d" % c, offset=8 * T + 2048 * (c - 2), align_bytes=64)[:] for c in (2, 3))
+        k_bf.extend(reuse.tile([P, QUARTER, PACK], BF16, name="k_bf%d" % c, offset=8 * T + 2112 * (c - 2), align_bytes=64)[:] for c in (2, 3))
         k_got = [[keep.tile([P, 2, QUARTER], BF16, name="k_got%d%d" % (pair, h)) for h in range(2)] for pair in range(2)]
         for t in range(PACK):
             nc.vector.tensor_copy(k_first[:, :, t], listed(k_raw[t], 0, HALF))
@@ -110,7 +109,7 @@ def tile_attend_x_ks_sink_topk_kernel(tc, qT, kT, vT, ks, vs, sink, offs, out):
                 for h in range(2):
                     nc.scalar.copy(k_bf[2 + h][:, :, t - 1 : t + 1], k_got[t // 2][h][:].rearrange("p t n -> p n t"))
 
-        q_bf = reuse.tile([P, NQ, PACK], BF16, name="q_bf", offset=8 * T + 4096, align_bytes=64)
+        q_bf = reuse.tile([P, NQ, PACK], BF16, name="q_bf", offset=8 * T + 8192, align_bytes=64)
         nc.gpsimd.tensor_scalar(q_bf[:], q_raw[:].rearrange("p t q -> p q t"), 1.0, 0.0, MULT, ADD)
         q_codes = keep.tile([P, NQ], U32, name="q_codes", align_bytes=64)
         q_scales = keep.tile([P, NQ], U8, name="q_scales", align_bytes=64)
@@ -120,7 +119,7 @@ def tile_attend_x_ks_sink_topk_kernel(tc, qT, kT, vT, ks, vs, sink, offs, out):
 
         k_codes = [keep.tile([P, QUARTER], U32, name="k_codes%d" % c, align_bytes=64) for c in range(4)]
         k_scales = [keep.tile([P, QUARTER], U8, name="k_scales0", align_bytes=64)]
-        k_scales.extend(reuse.tile([P, QUARTER], U8, name="k_scales%d" % c, offset=8 * T + 4096 + QUARTER * c, align_bytes=64) for c in (1, 2, 3))
+        k_scales.extend(reuse.tile([P, QUARTER], U8, name="k_scales%d" % c, offset=8 * T + 8192 + QUARTER * c, align_bytes=64) for c in (1, 2, 3))
         scores = []
         for c in range(4):
             if c == 1:
@@ -131,28 +130,27 @@ def tile_attend_x_ks_sink_topk_kernel(tc, qT, kT, vT, ks, vs, sink, offs, out):
             nc.tensor.matmul_mx(scores[c][:], lhsT=q_codes[:].bitcast(FP8X4), lhsT_scale=q_scales[:],
                                 rhs=k_codes[c][:].bitcast(FP8X4), rhs_scale=k_scales[c][:], start=True, stop=True)
 
-        logits_a = reuse.tile([P, 2, P, 2], F32, name="logits_a", offset=8 * T, align_bytes=64)
+        logits_a = reuse.tile([P, HALF + 8], F32, name="logits_a", offset=8 * T, align_bytes=64)
+        dealt_a = logits_a[:, 0:HALF].rearrange("q (u s e) -> q u s e", u=2, e=2)
         rows = QUARTER // PACK
         for h in range(2):
             place = slice(h * rows, (h + 1) * rows)
-            nc.vector.tensor_tensor(logits_a[:, :, place, :], scores[h][:].rearrange("q (s u e) -> q u s e", u=2, e=2), ks_a[:, :, place, :], MULT)
+            nc.vector.tensor_tensor(dealt_a[:, :, place, :], scores[h][:].rearrange("q (s u e) -> q u s e", u=2, e=2), ks_a[:, :, place, :], MULT)
+        nc.gpsimd.tensor_copy(logits_a[:, HALF : HALF + 1], sink_in[:])
         unscaled = keep.tile([P, PACK, rows], F32, name="unscaled")
-        dealt_b = logits_b[:, 0:HALF].rearrange("q (t s) -> q t s", t=PACK)
+        logits_b = keep.tile([P, 2, PACK, rows], F32, name="logits_b")
         nc.scalar.copy(unscaled[:], scores[2][:].rearrange("q (s t) -> q t s", t=PACK))
-        nc.gpsimd.tensor_tensor(dealt_b[:, :, 0:rows], unscaled[:], ks_b[:, :, 0:rows], MULT)
-        nc.vector.tensor_tensor(dealt_b[:, :, rows:P], scores[3][:].rearrange("q (s t) -> q t s", t=PACK), ks_b[:, :, rows:P], MULT)
-        flat_a = logits_a[:].rearrange("q u s e -> q (u s e)")
-        m_parts = reuse.tile([P, 2], F32, name="m_parts", offset=8 * T + 2048, align_bytes=64)
-        nc.vector.tensor_reduce(m_parts[:, 0:1], flat_a, AX, MAX, negate=True)
-        nc.vector.tensor_reduce(m_parts[:, 1:2], logits_b[:, 0 : HALF + 1], AX, MAX, negate=True)
+        nc.gpsimd.tensor_tensor(logits_b[:, 0], unscaled[:], ks_b[:, 0], MULT)
+        nc.vector.tensor_tensor(logits_b[:, 1], scores[3][:].rearrange("q (s t) -> q t s", t=PACK), ks_b[:, 1], MULT)
+        m_parts = reuse.tile([P, 2], F32, name="m_parts", offset=8 * T + 2112, align_bytes=64)
+        nc.vector.tensor_reduce(m_parts[:, 0:1], logits_a[:, 0 : HALF + 1], AX, MAX, negate=True)
+        nc.vector.tensor_reduce(m_parts[:, 1:2], logits_b[:].rearrange("q h t s -> q (h t s)"), AX, MAX, negate=True)
         m_neg = keep.tile([P, 1], F32, name="m_neg")
         nc.gpsimd.tensor_scalar(m_neg[:], m_parts[:, 0:1], m_parts[:, 1:2], None, MIN)
 
-        v_got = [[keep.tile([P, HALF], BF16, name="v_got00"), reuse.tile([P, HALF], BF16, name="v_got01", offset=8 * T + 12288, align_bytes=64)],
-                 [keep.tile([P, HALF], BF16, name="v_got1%d" % g) for g in range(2)]]
-        nc.scalar.activation(v_got[0][0][:], listed(v_raw[0], 0, HALF), COPY)
-        nc.vector.tensor_copy(v_got[0][1][:, 0:QUARTER], listed(v_raw[0], HALF, QUARTER))
-        nc.scalar.activation(v_got[0][1][:, QUARTER:HALF], listed(v_raw[0], HALF + QUARTER, QUARTER), COPY)
+        v_got = [[keep.tile([P, HALF], BF16, name="v_got%d%d" % (j, g)) for g in range(2)] for j in range(DV // P)]
+        for g in range(2):
+            nc.scalar.activation(v_got[0][g][:], listed(v_raw[0], g * HALF, HALF), COPY)
         v_first = keep.tile([P, 2, P * PACK], BF16, name="v_first", align_bytes=64)
 
         def turn_pairs(b, first, second):
@@ -171,25 +169,26 @@ def tile_attend_x_ks_sink_topk_kernel(tc, qT, kT, vT, ks, vs, sink, offs, out):
         for g in range(2):
             interleave(nc.vector.tensor_copy, v_first[:, g, :], turn_values(6 + g, v_got[0][g][:]))
 
-        p_a = reuse.tile([P, HALF], F32, name="p_a", offset=0, align_bytes=64)
-        p_b = reuse.tile([P, HALF + 8], F32, name="p_b", offset=PAGE, align_bytes=64)
+        p_a = reuse.tile([P, HALF + 8], F32, name="p_a", offset=0, align_bytes=64)
+        p_b = reuse.tile([P, PACK, P], F32, name="p_b", offset=PAGE, align_bytes=64)
         sums = keep.tile([P, 2], F32, name="sums")
-        nc.scalar.activation(p_a[:], flat_a, EXP, bias=m_neg[:], accum_out=sums[:, 0:1])
-        nc.scalar.activation(p_b[:, 0 : HALF + 1], logits_b[:, 0 : HALF + 1], EXP, bias=m_neg[:], accum_out=sums[:, 1:2])
+        nc.scalar.activation(p_a[:, 0 : HALF + 1], logits_a[:, 0 : HALF + 1], EXP, bias=m_neg[:], accum_out=sums[:, 0:1])
+        nc.scalar.activation(p_b[:].rearrange("q t (h s) -> q h t s", h=2), logits_b[:], EXP, bias=m_neg[:], accum_out=sums[:, 1:2])
         w_rows = keep.tile([P, HALF], BF16, name="w_rows")
-        nc.gpsimd.tensor_tensor(w_rows[:], p_a[:], vs_a[:].rearrange("q u s e -> q (u s e)"), MULT)
+        nc.gpsimd.tensor_tensor(w_rows[:], p_a[:, 0:HALF], vs_a[:].rearrange("q u s e -> q (u s e)"), MULT)
         total = keep.tile([P, 1], F32, name="total")
         nc.gpsimd.tensor_tensor(total[:], sums[:, 0:1], sums[:, 1:2], ADD)
 
         p_turned = bank(5, [P, PACK, NQ], "p_turned")
         for t in range(PACK):
-            nc.tensor.transpose(p_turned[:, t, :], p_b[:, t * P : (t + 1) * P], ident[:])
+            nc.tensor.transpose(p_turned[:, t, :], p_b[:, t, :], ident[:])
         w_words = w_rows[:].bitcast(F32)
         w_turned = turn_pairs(4, w_words[:, 0:P], w_words[:, P : 2 * P])
 
         first_codes = keep.tile([P, 2, P], U32, name="first_codes", align_bytes=64)
         first_scales = keep.tile([P, 2, P], U8, name="first_scales", align_bytes=64)
-        quantise(first_codes[:].rearrange("s g e -> s (g e)"), first_scales[:].rearrange("s g e -> s (g e)"), v_first[:].rearrange("s g e -> s (g e)"))
+        for g in range(2):
+            quantise(first_codes[:, g], first_scales[:, g], v_first[:, g])
 
         for g in range(2):
             nc.vector.tensor_copy(v_got[1][g][:, 0:QUARTER], listed(v_raw[1], g * HALF, QUARTER))

@@ -11,6 +11,7 @@ QUARTER = 256
 RUN = T // P
 PAGE = 4096
 LANES = 16
+SHARE = 320
 
 F32 = mybir.dt.float32
 BF16 = mybir.dt.bfloat16
@@ -100,7 +101,7 @@ def tile_attend_x_ks_sink_topk_kernel(tc, qT, kT, vT, ks, vs, sink, offs, out):
         k_first = keep.tile([P, HALF, PACK], BF16, name="k_first", align_bytes=64)
         k_bf = [k_first[:, 0:QUARTER, :], k_first[:, QUARTER:HALF, :]]
         k_bf.extend(reuse.tile([P, QUARTER, PACK], BF16, name="k_bf%d" % c, offset=8 * T + 2112 * (c - 2), align_bytes=64)[:] for c in (2, 3))
-        k_got = [[keep.tile([P, 2, QUARTER], BF16, name="k_got%d%d" % (pair, h)) for h in range(2)] for pair in range(2)]
+        k_got = [[keep.tile([P, 2, QUARTER], F32, name="k_got%d%d" % (pair, h)) for h in range(2)] for pair in range(2)]
         for t in range(PACK):
             nc.vector.tensor_copy(k_first[:, :, t], listed(k_raw[t], 0, HALF))
             for h in range(2):
@@ -148,9 +149,12 @@ def tile_attend_x_ks_sink_topk_kernel(tc, qT, kT, vT, ks, vs, sink, offs, out):
         m_neg = keep.tile([P, 1], F32, name="m_neg")
         nc.gpsimd.tensor_scalar(m_neg[:], m_parts[:, 0:1], m_parts[:, 1:2], None, MIN)
 
-        v_got = [[keep.tile([P, HALF], BF16, name="v_got%d%d" % (j, g)) for g in range(2)] for j in range(DV // P)]
-        for g in range(2):
-            nc.scalar.activation(v_got[0][g][:], listed(v_raw[0], g * HALF, HALF), COPY)
+        got_at = 8 * T + 12288
+        v_got = [[reuse.tile([P, HALF], BF16, name="v_got00", offset=got_at, align_bytes=64), keep.tile([P, HALF], BF16, name="v_got01")],
+                 [keep.tile([P, HALF], BF16, name="v_got1%d" % g) for g in range(2)]]
+        nc.scalar.activation(v_got[0][0][:], listed(v_raw[0], 0, HALF), COPY)
+        nc.vector.tensor_copy(v_got[0][1][:, 0 : HALF - P], listed(v_raw[0], HALF, HALF - P))
+        nc.scalar.activation(v_got[0][1][:, HALF - P : HALF], listed(v_raw[0], N - P, P), COPY)
         v_first = keep.tile([P, 2, P * PACK], BF16, name="v_first", align_bytes=64)
 
         def turn_pairs(b, first, second):
@@ -169,8 +173,8 @@ def tile_attend_x_ks_sink_topk_kernel(tc, qT, kT, vT, ks, vs, sink, offs, out):
         for g in range(2):
             interleave(nc.vector.tensor_copy, v_first[:, g, :], turn_values(6 + g, v_got[0][g][:]))
 
-        p_a = reuse.tile([P, HALF + 8], F32, name="p_a", offset=0, align_bytes=64)
-        p_b = reuse.tile([P, PACK, P], F32, name="p_b", offset=PAGE, align_bytes=64)
+        p_a = reuse.tile([P, HALF + 16], F32, name="p_a", offset=got_at - 1600, align_bytes=64)
+        p_b = reuse.tile([P, PACK, P], F32, name="p_b", offset=got_at + 512, align_bytes=64)
         sums = keep.tile([P, 2], F32, name="sums")
         nc.scalar.activation(p_a[:, 0 : HALF + 1], logits_a[:, 0 : HALF + 1], EXP, bias=m_neg[:], accum_out=sums[:, 0:1])
         nc.scalar.activation(p_b[:].rearrange("q t (h s) -> q h t s", h=2), logits_b[:], EXP, bias=m_neg[:], accum_out=sums[:, 1:2])
@@ -191,8 +195,8 @@ def tile_attend_x_ks_sink_topk_kernel(tc, qT, kT, vT, ks, vs, sink, offs, out):
             quantise(first_codes[:, g], first_scales[:, g], v_first[:, g])
 
         for g in range(2):
-            nc.vector.tensor_copy(v_got[1][g][:, 0:QUARTER], listed(v_raw[1], g * HALF, QUARTER))
-            nc.scalar.activation(v_got[1][g][:, QUARTER:HALF], listed(v_raw[1], g * HALF + QUARTER, QUARTER), COPY)
+            nc.vector.tensor_copy(v_got[1][g][:, 0:SHARE], listed(v_raw[1], g * HALF, SHARE))
+            nc.scalar.activation(v_got[1][g][:, SHARE:HALF], listed(v_raw[1], g * HALF + SHARE, HALF - SHARE), COPY)
         w_bf = [reuse.tile([P, NQ * PACK], BF16, name="w_bf%d" % g, offset=4 * T + 1024 * g, align_bytes=64) for g in range(2)]
         v_last = [keep.tile([P, P * PACK], BF16, name="v_last%d" % g, align_bytes=64) for g in range(2)]
         interleave(nc.scalar.copy, w_bf[0][:], w_turned)

@@ -11,7 +11,7 @@ QUARTER = 256
 RUN = T // P
 PAGE = 4096
 LANES = 16
-SHARE = 320
+SHARE = 288
 
 F32 = mybir.dt.float32
 BF16 = mybir.dt.bfloat16
@@ -48,15 +48,16 @@ def tile_attend_x_ks_sink_topk_kernel(tc, qT, kT, vT, ks, vs, sink, offs, out):
         nc.scalar.dma_start(ks_run[:], ks[0:1, :].rearrange("o (p c) -> (o p) c", c=RUN))
         vs_pool = keep.tile([P, T], F32, name="vs_pool")
         nc.scalar.dma_start(vs_pool[P - 1 : P, T // 2 : T], vs[0:1, T // 2 : T])
+        nc.sync.dma_start(vs_pool[63:64, 0 : T // 2], vs[0:1, 0 : T // 2])
+        nc.sync.dma_start(k_raw[0][:], k_rows[:, 0, :])
         offsets = keep.tile([P, N // LANES], U16, name="offsets")
         nc.sync.dma_start(offsets[:], offs)
-        nc.sync.dma_start(vs_pool[63:64, 0 : T // 2], vs[0:1, 0 : T // 2])
         nc.vector.memset(vs_pool[0:63, 0 : T // 2], 0.0)
         nc.vector.memset(vs_pool[64:P, 0 : T // 2], 0.0)
         nc.vector.memset(vs_pool[0 : P - 1, T // 2 : T], 0.0)
         sink_in = keep.tile([P, 1], F32, name="sink_in")
         nc.scalar.dma_start(sink_in[:], sink.rearrange("b q o -> (b q) o"))
-        for t in range(PACK):
+        for t in range(1, PACK):
             nc.sync.dma_start(k_raw[t][:], k_rows[:, t, :])
         q_raw = keep.tile([P, PACK, NQ], F32, name="q_raw")
         nc.sync.dma_start(q_raw[:], qT.rearrange("b (p t) q -> p (b t) q", t=PACK))
@@ -155,7 +156,8 @@ def tile_attend_x_ks_sink_topk_kernel(tc, qT, kT, vT, ks, vs, sink, offs, out):
         nc.scalar.activation(v_got[0][0][:], listed(v_raw[0], 0, HALF), COPY)
         nc.vector.tensor_copy(v_got[0][1][:, 0 : HALF - P], listed(v_raw[0], HALF, HALF - P))
         nc.scalar.activation(v_got[0][1][:, HALF - P : HALF], listed(v_raw[0], N - P, P), COPY)
-        v_first = keep.tile([P, 2, P * PACK], BF16, name="v_first", align_bytes=64)
+        v_first = [reuse.tile([P, P * PACK], BF16, name="v_first0", offset=8 * T + 20480, align_bytes=64),
+                   reuse.tile([P, P * PACK], BF16, name="v_first1", offset=8 * T + 20480 + 512, align_bytes=64)]
 
         def turn_pairs(b, first, second):
             turned = bank(b, [P, 2, P], "pairs_turned")
@@ -170,29 +172,28 @@ def tile_attend_x_ks_sink_topk_kernel(tc, qT, kT, vT, ks, vs, sink, offs, out):
         def interleave(copy, dest, turned):
             copy(dest.bitcast(F32).rearrange("s (x u) -> s x u", u=2), turned[:].rearrange("s u x -> s x u"))
 
-        for g in range(2):
-            interleave(nc.vector.tensor_copy, v_first[:, g, :], turn_values(6 + g, v_got[0][g][:]))
+        first_turned = [turn_values(6 + g, v_got[0][g][:]) for g in range(2)]
+        interleave(nc.vector.tensor_copy, v_first[0][:], first_turned[0])
+
+        v_codes = [[keep.tile([P, P], U32, name="v_codes00", align_bytes=64), reuse.tile([P, P], U32, name="v_codes01", offset=4 * T + 2048, align_bytes=64)],
+                   [keep.tile([P, P], U32, name="v_codes1%d" % g, align_bytes=64) for g in range(2)]]
+        v_scales = [[keep.tile([P, P], U8, name="v_scales%d%d" % (j, g), align_bytes=64) for g in range(2)] for j in range(DV // P)]
+        quantise(v_codes[0][0][:], v_scales[0][0][:], v_first[0][:])
+        interleave(nc.vector.tensor_copy, v_first[1][:], first_turned[1])
 
         p_a = reuse.tile([P, HALF + 16], F32, name="p_a", offset=got_at - 1600, align_bytes=64)
         p_b = reuse.tile([P, PACK, P], F32, name="p_b", offset=got_at + 512, align_bytes=64)
         sums = keep.tile([P, 2], F32, name="sums")
         nc.scalar.activation(p_a[:, 0 : HALF + 1], logits_a[:, 0 : HALF + 1], EXP, bias=m_neg[:], accum_out=sums[:, 0:1])
         nc.scalar.activation(p_b[:].rearrange("q t (h s) -> q h t s", h=2), logits_b[:], EXP, bias=m_neg[:], accum_out=sums[:, 1:2])
-        w_rows = keep.tile([P, HALF], BF16, name="w_rows")
+        w_rows = reuse.tile([P, HALF], BF16, name="w_rows", offset=8 * T + 20480 - 512, align_bytes=64)
         nc.gpsimd.tensor_tensor(w_rows[:], p_a[:, 0:HALF], vs_a[:].rearrange("q u s e -> q (u s e)"), MULT)
-        total = keep.tile([P, 1], F32, name="total")
-        nc.gpsimd.tensor_tensor(total[:], sums[:, 0:1], sums[:, 1:2], ADD)
 
         p_turned = bank(5, [P, PACK, NQ], "p_turned")
         for t in range(PACK):
             nc.tensor.transpose(p_turned[:, t, :], p_b[:, t, :], ident[:])
         w_words = w_rows[:].bitcast(F32)
         w_turned = turn_pairs(4, w_words[:, 0:P], w_words[:, P : 2 * P])
-
-        first_codes = keep.tile([P, 2, P], U32, name="first_codes", align_bytes=64)
-        first_scales = keep.tile([P, 2, P], U8, name="first_scales", align_bytes=64)
-        for g in range(2):
-            quantise(first_codes[:, g], first_scales[:, g], v_first[:, g])
 
         for g in range(2):
             nc.vector.tensor_copy(v_got[1][g][:, 0:SHARE], listed(v_raw[1], g * HALF, SHARE))
@@ -207,23 +208,22 @@ def tile_attend_x_ks_sink_topk_kernel(tc, qT, kT, vT, ks, vs, sink, offs, out):
 
         w_codes = [keep.tile([P, NQ], U32, name="w_codes%d" % g, align_bytes=64) for g in range(2)]
         w_scales = [keep.tile([P, NQ], U8, name="w_scales%d" % g, align_bytes=64) for g in range(2)]
-        last_codes = keep.tile([P, 2, P], U32, name="last_codes", align_bytes=64)
-        last_scales = keep.tile([P, 2, P], U8, name="last_scales", align_bytes=64)
+        quantise(v_codes[0][1][:], v_scales[0][1][:], v_first[1][:])
+        total = reuse.tile([P, 1], F32, name="total", offset=4 * T + 8192, align_bytes=64)
+        nc.vector.tensor_reduce(total[:], sums[:], AX, ADD)
         for g in range(2):
             quantise(w_codes[g][:], w_scales[g][:], w_bf[g][:])
         for g in range(2):
-            quantise(last_codes[:, g], last_scales[:, g], v_last[g][:])
+            quantise(v_codes[1][g][:], v_scales[1][g][:], v_last[g][:])
         inv = reuse.tile([P, 1], F32, name="inv", offset=4 * T + 1024, align_bytes=64)
         nc.vector.reciprocal(inv[:], total[:])
 
         y_out = out.rearrange("b q e -> (b q) e")
-        v_codes = (first_codes, last_codes)
-        v_scales = (first_scales, last_scales)
         for j in range(DV // P):
             acc = bank(2 + j, [P, P], "acc")
             for g in range(2):
                 nc.tensor.matmul_mx(acc[:], lhsT=w_codes[g][:].bitcast(FP8X4), lhsT_scale=w_scales[g][:],
-                                    rhs=v_codes[j][:, g].bitcast(FP8X4), rhs_scale=v_scales[j][:, g], start=(g == 0), stop=(g == 1))
+                                    rhs=v_codes[j][g][:].bitcast(FP8X4), rhs_scale=v_scales[j][g][:], start=(g == 0), stop=(g == 1))
             y = keep.tile([P, P], F32, name="y%d" % j)
             if j == 0:
                 nc.scalar.activation(y[:], acc[:], COPY, scale=inv[:])

@@ -22,7 +22,6 @@ FP8X4 = mybir.dt.float8_e4m3fn_x4
 MULT = mybir.AluOpType.mult
 ADD = mybir.AluOpType.add
 MAX = mybir.AluOpType.max
-MIN = mybir.AluOpType.min
 AX = mybir.AxisListType.X
 COPY = mybir.ActivationFunctionType.Copy
 EXP = mybir.ActivationFunctionType.Exp
@@ -55,8 +54,8 @@ def tile_attend_x_ks_sink_topk_kernel(tc, qT, kT, vT, ks, vs, sink, offs, out):
         nc.vector.memset(vs_pool[0:63, 0 : T // 2], 0.0)
         nc.vector.memset(vs_pool[64:P, 0 : T // 2], 0.0)
         nc.vector.memset(vs_pool[0 : P - 1, T // 2 : T], 0.0)
-        sink_in = keep.tile([P, 1], F32, name="sink_in")
-        nc.scalar.dma_start(sink_in[:], sink.rearrange("b q o -> (b q) o"))
+        logits = keep.tile([P, N + 16], F32, name="logits")
+        nc.scalar.dma_start(logits[:, 7:8], sink.rearrange("b q o -> (b q) o"))
         for t in range(1, PACK):
             nc.sync.dma_start(k_raw[t][:], k_rows[:, t, :])
         q_raw = keep.tile([P, PACK, NQ], F32, name="q_raw")
@@ -78,12 +77,11 @@ def tile_attend_x_ks_sink_topk_kernel(tc, qT, kT, vT, ks, vs, sink, offs, out):
                 nc.tensor.transpose(turned[:, c, :], ks_run[:, 4 * b + c : 4 * b + c + 1].to_broadcast([P, P]), ident[:])
             nc.scalar.activation(by_run[:, :, 4 * b : 4 * b + 4], turned[:].rearrange("r c p -> r p c"), COPY)
 
+        rows = QUARTER // PACK
         ks_got = keep.tile([P, N], F32, name="ks_got")
         nc.vector.tensor_copy(ks_got[:], listed(ks_pool, 0, N))
-        ks_a = keep.tile([P, 2, P, 2], F32, name="ks_a")
-        nc.vector.tensor_copy(ks_a[:], ks_got[:, 0:HALF].rearrange("q (s u e) -> q u s e", u=2, e=2))
-        ks_b = keep.tile([P, 2, PACK, QUARTER // PACK], F32, name="ks_b")
-        nc.vector.tensor_copy(ks_b[:], ks_got[:, HALF:N].rearrange("q (h s t) -> q h t s", t=PACK, h=2))
+        ks_dealt = keep.tile([P, 4, PACK, rows], F32, name="ks_dealt")
+        nc.vector.tensor_copy(ks_dealt[:], ks_got[:].rearrange("q (c s t) -> q c t s", t=PACK, c=4))
 
         vs_got = keep.tile([P, N], F32, name="vs_got")
         nc.vector.tensor_copy(vs_got[:], listed(vs_pool, 0, N))
@@ -93,25 +91,18 @@ def tile_attend_x_ks_sink_topk_kernel(tc, qT, kT, vT, ks, vs, sink, offs, out):
             for t in range(PACK):
                 nc.tensor.transpose(turned[:, t, :], vs_got[:, g * HALF + t : (g + 1) * HALF : PACK], ident[:])
             nc.vector.tensor_reduce(vs_col[g][:], turned[:, :, 63::64], AX, ADD)
-        spread = bank(2, [P, PACK, P], "vs_spread")
-        for t in range(PACK):
-            nc.tensor.transpose(spread[:, t, :], vs_col[0][:, t : t + 1].to_broadcast([P, P]), ident[:])
-        vs_a = keep.tile([P, 2, P, 2], F32, name="vs_a")
-        nc.scalar.copy(vs_a[:], spread[:].rearrange("r (u e) s -> r u s e", u=2))
 
-        k_first = keep.tile([P, HALF, PACK], BF16, name="k_first", align_bytes=64)
-        k_bf = [k_first[:, 0:QUARTER, :], k_first[:, QUARTER:HALF, :]]
-        k_bf.extend(reuse.tile([P, QUARTER, PACK], BF16, name="k_bf%d" % c, offset=8 * T + 2112 * (c - 2), align_bytes=64)[:] for c in (2, 3))
-        k_got = [[keep.tile([P, 2, QUARTER], F32, name="k_got%d%d" % (pair, h)) for h in range(2)] for pair in range(2)]
+        pieces = [(0, QUARTER), (QUARTER, QUARTER), (HALF, QUARTER), (HALF + QUARTER, P), (N - P, P)]
+        k_bf = [keep.tile([P, count, PACK], BF16, name="k_bf%d" % i, align_bytes=64) for i, (first, count) in enumerate(pieces)]
+        k_got = [keep.tile([P, 2, QUARTER], BF16, name="k_got%d" % pair) for pair in range(2)]
         for t in range(PACK):
-            nc.vector.tensor_copy(k_first[:, :, t], listed(k_raw[t], 0, HALF))
-            for h in range(2):
-                nc.scalar.activation(k_got[t // 2][h][:, t % 2, :], listed(k_raw[t], HALF + h * QUARTER, QUARTER), COPY)
+            nc.vector.tensor_copy(k_got[t // 2][:, t % 2, :], listed(k_raw[t], 0, QUARTER))
             if t % 2 == 1:
-                for h in range(2):
-                    nc.scalar.copy(k_bf[2 + h][:, :, t - 1 : t + 1], k_got[t // 2][h][:].rearrange("p t n -> p n t"))
+                nc.vector.tensor_copy(k_bf[0][:, :, t - 1 : t + 1], k_got[t // 2][:].rearrange("p t n -> p n t"))
+            for i in range(1, len(pieces)):
+                nc.scalar.activation(k_bf[i][:, :, t], listed(k_raw[t], *pieces[i]), COPY)
 
-        q_bf = reuse.tile([P, NQ, PACK], BF16, name="q_bf", offset=8 * T + 8192, align_bytes=64)
+        q_bf = reuse.tile([P, NQ, PACK], BF16, name="q_bf", offset=8 * T, align_bytes=64)
         nc.gpsimd.tensor_scalar(q_bf[:], q_raw[:].rearrange("p t q -> p q t"), 1.0, 0.0, MULT, ADD)
         q_codes = keep.tile([P, NQ], U32, name="q_codes", align_bytes=64)
         q_scales = keep.tile([P, NQ], U8, name="q_scales", align_bytes=64)
@@ -119,114 +110,93 @@ def tile_attend_x_ks_sink_topk_kernel(tc, qT, kT, vT, ks, vs, sink, offs, out):
         def quantise(codes, scales, values):
             nc.vector.quantize_mx(codes.bitcast(FP8X4), scales, values)
 
-        k_codes = [keep.tile([P, QUARTER], U32, name="k_codes%d" % c, align_bytes=64) for c in range(4)]
-        k_scales = [keep.tile([P, QUARTER], U8, name="k_scales0", align_bytes=64)]
-        k_scales.extend(reuse.tile([P, QUARTER], U8, name="k_scales%d" % c, offset=8 * T + 8192 + QUARTER * c, align_bytes=64) for c in (1, 2, 3))
-        scores = []
-        for c in range(4):
-            if c == 1:
+        k_codes = [keep.tile([P, count], U32, name="k_codes%d" % i, align_bytes=64) for i, (first, count) in enumerate(pieces)]
+        k_scales = [keep.tile([P, count], U8, name="k_scales%d" % i, align_bytes=64) if i == 1 else
+                    reuse.tile([P, count], U8, name="k_scales%d" % i, offset=8 * T + first, align_bytes=64) for i, (first, count) in enumerate(pieces)]
+        scores = [bank(c, [P, QUARTER], "scores") for c in range(4)]
+        for i in (1, 0, 2, 3, 4):
+            quantise(k_codes[i][:], k_scales[i][:], k_bf[i][:].rearrange("p n t -> p (n t)"))
+            if i == 1:
                 quantise(q_codes[:], q_scales[:], q_bf[:].rearrange("p q t -> p (q t)"))
-            quantise(k_codes[c][:], k_scales[c][:], k_bf[c].rearrange("p n t -> p (n t)"))
-        for c in range(4):
-            scores.append(bank(c, [P, QUARTER], "scores"))
-            nc.tensor.matmul_mx(scores[c][:], lhsT=q_codes[:].bitcast(FP8X4), lhsT_scale=q_scales[:],
-                                rhs=k_codes[c][:].bitcast(FP8X4), rhs_scale=k_scales[c][:], start=True, stop=True)
+            first, count = pieces[i]
+            nc.tensor.matmul_mx(scores[first // QUARTER][:, first % QUARTER : first % QUARTER + count],
+                                lhsT=q_codes[:].bitcast(FP8X4), lhsT_scale=q_scales[:],
+                                rhs=k_codes[i][:].bitcast(FP8X4), rhs_scale=k_scales[i][:], start=True, stop=True)
 
-        logits_a = reuse.tile([P, HALF + 8], F32, name="logits_a", offset=8 * T, align_bytes=64)
-        dealt_a = logits_a[:, 0:HALF].rearrange("q (u s e) -> q u s e", u=2, e=2)
-        rows = QUARTER // PACK
-        for h in range(2):
-            place = slice(h * rows, (h + 1) * rows)
-            nc.vector.tensor_tensor(dealt_a[:, :, place, :], scores[h][:].rearrange("q (s u e) -> q u s e", u=2, e=2), ks_a[:, :, place, :], MULT)
-        nc.gpsimd.tensor_copy(logits_a[:, HALF : HALF + 1], sink_in[:])
+        dealt = logits[:, 8 : 8 + N].rearrange("q (h g t s) -> q g h t s", h=2, g=2, t=PACK)
         unscaled = keep.tile([P, PACK, rows], F32, name="unscaled")
-        logits_b = keep.tile([P, 2, PACK, rows], F32, name="logits_b")
-        nc.scalar.copy(unscaled[:], scores[2][:].rearrange("q (s t) -> q t s", t=PACK))
-        nc.gpsimd.tensor_tensor(logits_b[:, 0], unscaled[:], ks_b[:, 0], MULT)
-        nc.vector.tensor_tensor(logits_b[:, 1], scores[3][:].rearrange("q (s t) -> q t s", t=PACK), ks_b[:, 1], MULT)
-        m_parts = reuse.tile([P, 2], F32, name="m_parts", offset=8 * T + 2112, align_bytes=64)
-        nc.vector.tensor_reduce(m_parts[:, 0:1], logits_a[:, 0 : HALF + 1], AX, MAX, negate=True)
-        nc.vector.tensor_reduce(m_parts[:, 1:2], logits_b[:].rearrange("q h t s -> q (h t s)"), AX, MAX, negate=True)
+        nc.scalar.copy(unscaled[:], scores[1][:].rearrange("q (s t) -> q t s", t=PACK))
+        nc.gpsimd.tensor_tensor(dealt[:, 0, 1], unscaled[:], ks_dealt[:, 1], MULT)
+        for c in (0, 2, 3):
+            nc.vector.tensor_tensor(dealt[:, c // 2, c % 2], scores[c][:].rearrange("q (s t) -> q t s", t=PACK), ks_dealt[:, c], MULT)
+            if c == 2:
+                nc.vector.tensor_reduce(logits[:, N + 8 : N + 9], logits[:, 7 : 8 + HALF], AX, MAX)
         m_neg = keep.tile([P, 1], F32, name="m_neg")
-        nc.gpsimd.tensor_scalar(m_neg[:], m_parts[:, 0:1], m_parts[:, 1:2], None, MIN)
+        nc.vector.tensor_reduce(m_neg[:], logits[:, 8 + HALF : N + 9], AX, MAX, negate=True)
 
-        got_at = 8 * T + 12288
-        v_got = [[reuse.tile([P, HALF], BF16, name="v_got00", offset=got_at, align_bytes=64), keep.tile([P, HALF], BF16, name="v_got01")],
-                 [keep.tile([P, HALF], BF16, name="v_got1%d" % g) for g in range(2)]]
-        nc.scalar.activation(v_got[0][0][:], listed(v_raw[0], 0, HALF), COPY)
-        nc.vector.tensor_copy(v_got[0][1][:, 0 : HALF - P], listed(v_raw[0], HALF, HALF - P))
-        nc.scalar.activation(v_got[0][1][:, HALF - P : HALF], listed(v_raw[0], N - P, P), COPY)
-        v_first = [reuse.tile([P, P * PACK], BF16, name="v_first0", offset=8 * T + 20480, align_bytes=64),
-                   reuse.tile([P, P * PACK], BF16, name="v_first1", offset=8 * T + 20480 + 512, align_bytes=64)]
+        p = [keep.tile([P, PACK, P], F32, name="p%d" % g) for g in range(2)]
+        sums = keep.tile([P, 3], F32, name="sums")
+        for g in range(2):
+            nc.scalar.activation(p[g][:].rearrange("q t (h s) -> q h t s", h=2), dealt[:, g], EXP, bias=m_neg[:], accum_out=sums[:, g : g + 1])
+        nc.scalar.activation(sums[:, 2:3], logits[:, 7:8], EXP, bias=m_neg[:])
 
-        def turn_pairs(b, first, second):
-            turned = bank(b, [P, 2, P], "pairs_turned")
-            nc.tensor.transpose(turned[:, 0, :], first, ident[:])
-            nc.tensor.transpose(turned[:, 1, :], second, ident[:])
-            return turned
+        v_got = [[keep.tile([P, HALF], BF16, name="v_got%d%d" % (j, g)) for g in range(2)] for j in range(2)]
+        nc.vector.tensor_copy(v_got[0][0][:], listed(v_raw[0], 0, HALF))
+        nc.vector.tensor_copy(v_got[0][1][:, 0:P], listed(v_raw[0], HALF, P))
+        nc.scalar.activation(v_got[0][1][:, P:HALF], listed(v_raw[0], HALF + P, HALF - P), COPY)
 
         def turn_values(b, got):
             words = got.bitcast(F32)
-            return turn_pairs(b, words[:, 0 : HALF // 2 : 2], words[:, 1 : HALF // 2 : 2])
+            turned = bank(b, [P, 2, P], "pairs_turned")
+            for u in range(2):
+                nc.tensor.transpose(turned[:, u, :], words[:, u : HALF // 2 : 2], ident[:])
+            return turned
 
-        def interleave(copy, dest, turned):
-            copy(dest.bitcast(F32).rearrange("s (x u) -> s x u", u=2), turned[:].rearrange("s u x -> s x u"))
+        def interleave(dest, turned):
+            nc.scalar.copy(dest.bitcast(F32).rearrange("s (x u) -> s x u", u=2), turned[:].rearrange("s u x -> s x u"))
 
-        first_turned = [turn_values(6 + g, v_got[0][g][:]) for g in range(2)]
-        interleave(nc.vector.tensor_copy, v_first[0][:], first_turned[0])
-
-        v_codes = [[keep.tile([P, P], U32, name="v_codes00", align_bytes=64), reuse.tile([P, P], U32, name="v_codes01", offset=4 * T + 2048, align_bytes=64)],
+        w_bf = [keep.tile([P, NQ * PACK], BF16, name="w_bf%d" % g, align_bytes=64) for g in range(2)]
+        v_bf = [[reuse.tile([P, P * PACK], BF16, name="v_bf0%d" % g, offset=1024 * g, align_bytes=64) for g in range(2)],
+                [keep.tile([P, P * PACK], BF16, name="v_bf1%d" % g, align_bytes=64) for g in range(2)]]
+        w_codes = [keep.tile([P, NQ], U32, name="w_codes%d" % g, align_bytes=64) for g in range(2)]
+        w_scales = [keep.tile([P, NQ], U8, name="w_scales%d" % g, align_bytes=64) for g in range(2)]
+        v_codes = [[reuse.tile([P, P], U32, name="v_codes0%d" % g, offset=4 * T + 512 * g, align_bytes=64) for g in range(2)],
                    [keep.tile([P, P], U32, name="v_codes1%d" % g, align_bytes=64) for g in range(2)]]
-        v_scales = [[keep.tile([P, P], U8, name="v_scales%d%d" % (j, g), align_bytes=64) for g in range(2)] for j in range(DV // P)]
-        quantise(v_codes[0][0][:], v_scales[0][0][:], v_first[0][:])
-        interleave(nc.vector.tensor_copy, v_first[1][:], first_turned[1])
-
-        p_a = reuse.tile([P, HALF + 16], F32, name="p_a", offset=got_at - 1600, align_bytes=64)
-        p_b = reuse.tile([P, PACK, P], F32, name="p_b", offset=got_at + 512, align_bytes=64)
-        sums = keep.tile([P, 2], F32, name="sums")
-        nc.scalar.activation(p_a[:, 0 : HALF + 1], logits_a[:, 0 : HALF + 1], EXP, bias=m_neg[:], accum_out=sums[:, 0:1])
-        nc.scalar.activation(p_b[:].rearrange("q t (h s) -> q h t s", h=2), logits_b[:], EXP, bias=m_neg[:], accum_out=sums[:, 1:2])
-        w_rows = reuse.tile([P, HALF], BF16, name="w_rows", offset=8 * T + 20480 - 512, align_bytes=64)
-        nc.gpsimd.tensor_tensor(w_rows[:], p_a[:, 0:HALF], vs_a[:].rearrange("q u s e -> q (u s e)"), MULT)
-
-        p_turned = bank(5, [P, PACK, NQ], "p_turned")
-        for t in range(PACK):
-            nc.tensor.transpose(p_turned[:, t, :], p_b[:, t, :], ident[:])
-        w_words = w_rows[:].bitcast(F32)
-        w_turned = turn_pairs(4, w_words[:, 0:P], w_words[:, P : 2 * P])
+        v_scales = [[keep.tile([P, P], U8, name="v_scales%d%d" % (j, g), align_bytes=64) for g in range(2)] for j in range(2)]
+        for g in range(2):
+            p_turned = bank(4 + g, [P, PACK, NQ], "p_turned")
+            for t in range(PACK):
+                nc.tensor.transpose(p_turned[:, t, :], p[g][:, t, :], ident[:])
+            nc.vector.tensor_tensor(w_bf[g][:].rearrange("s (q t) -> s q t", t=PACK), p_turned[:].rearrange("s t q -> s q t"),
+                                    vs_col[g][:].unsqueeze(1).to_broadcast([P, NQ, PACK]), MULT)
+        for g in range(2):
+            interleave(v_bf[0][g][:], turn_values(4 + 2 * g, v_got[0][g][:]))
+        for g in range(2):
+            quantise(w_codes[g][:], w_scales[g][:], w_bf[g][:])
 
         for g in range(2):
             nc.vector.tensor_copy(v_got[1][g][:, 0:SHARE], listed(v_raw[1], g * HALF, SHARE))
             nc.scalar.activation(v_got[1][g][:, SHARE:HALF], listed(v_raw[1], g * HALF + SHARE, HALF - SHARE), COPY)
-        w_bf = [reuse.tile([P, NQ * PACK], BF16, name="w_bf%d" % g, offset=4 * T + 1024 * g, align_bytes=64) for g in range(2)]
-        v_last = [keep.tile([P, P * PACK], BF16, name="v_last%d" % g, align_bytes=64) for g in range(2)]
-        interleave(nc.scalar.copy, w_bf[0][:], w_turned)
         for g in range(2):
-            interleave(nc.scalar.copy, v_last[g][:], turn_values(g, v_got[1][g][:]))
-        nc.vector.tensor_tensor(w_bf[1][:].rearrange("s (q t) -> s q t", t=PACK), p_turned[:].rearrange("s t q -> s q t"),
-                                vs_col[1][:].unsqueeze(1).to_broadcast([P, NQ, PACK]), MULT)
-
-        w_codes = [keep.tile([P, NQ], U32, name="w_codes%d" % g, align_bytes=64) for g in range(2)]
-        w_scales = [keep.tile([P, NQ], U8, name="w_scales%d" % g, align_bytes=64) for g in range(2)]
-        quantise(v_codes[0][1][:], v_scales[0][1][:], v_first[1][:])
-        total = reuse.tile([P, 1], F32, name="total", offset=4 * T + 8192, align_bytes=64)
+            interleave(v_bf[1][g][:], turn_values(g, v_got[1][g][:]))
+        total = reuse.tile([P, 1], F32, name="total", offset=4 * T + 1024, align_bytes=64)
         nc.vector.tensor_reduce(total[:], sums[:], AX, ADD)
         for g in range(2):
-            quantise(w_codes[g][:], w_scales[g][:], w_bf[g][:])
-        for g in range(2):
-            quantise(v_codes[1][g][:], v_scales[1][g][:], v_last[g][:])
-        inv = reuse.tile([P, 1], F32, name="inv", offset=4 * T + 1024, align_bytes=64)
+            quantise(v_codes[0][g][:], v_scales[0][g][:], v_bf[0][g][:])
+        inv = keep.tile([P, 1], F32, name="inv")
         nc.vector.reciprocal(inv[:], total[:])
+        for g in range(2):
+            quantise(v_codes[1][g][:], v_scales[1][g][:], v_bf[1][g][:])
 
         y_out = out.rearrange("b q e -> (b q) e")
+        y = [keep.tile([P, P], F32, name="y%d" % j) for j in range(2)]
         for j in range(DV // P):
             acc = bank(2 + j, [P, P], "acc")
             for g in range(2):
                 nc.tensor.matmul_mx(acc[:], lhsT=w_codes[g][:].bitcast(FP8X4), lhsT_scale=w_scales[g][:],
                                     rhs=v_codes[j][g][:].bitcast(FP8X4), rhs_scale=v_scales[j][g][:], start=(g == 0), stop=(g == 1))
-            y = keep.tile([P, P], F32, name="y%d" % j)
             if j == 0:
-                nc.scalar.activation(y[:], acc[:], COPY, scale=inv[:])
+                nc.scalar.activation(y[j][:], acc[:], COPY, scale=inv[:])
             else:
-                nc.vector.tensor_scalar(y[:], acc[:], inv[:], None, MULT)
-            nc.sync.dma_start(y_out[:, j * P : (j + 1) * P], y[:])
+                nc.vector.tensor_scalar(y[j][:], acc[:], inv[:], None, MULT)
+            nc.sync.dma_start(y_out[:, j * P : (j + 1) * P], y[j][:])

@@ -92,15 +92,13 @@ def tile_attend_x_ks_sink_topk_kernel(tc, qT, kT, vT, ks, vs, sink, offs, out):
                 nc.tensor.transpose(turned[:, t, :], vs_got[:, g * HALF + t : (g + 1) * HALF : PACK], ident[:])
             nc.vector.tensor_reduce(vs_col[g][:], turned[:, :, 63::64], AX, ADD)
 
-        pieces = [(0, QUARTER), (QUARTER, QUARTER), (HALF, QUARTER), (HALF + QUARTER, P), (N - P, P)]
-        k_bf = [keep.tile([P, count, PACK], BF16, name="k_bf%d" % i, align_bytes=64) for i, (first, count) in enumerate(pieces)]
-        k_got = [keep.tile([P, 2, QUARTER], BF16, name="k_got%d" % pair) for pair in range(2)]
+        k_first = keep.tile([P, HALF, PACK], BF16, name="k_first", align_bytes=64)
+        k_bf = [k_first[:, 0:QUARTER, :], k_first[:, QUARTER:HALF, :]]
+        k_bf.extend(keep.tile([P, QUARTER, PACK], BF16, name="k_bf%d" % c, align_bytes=64)[:] for c in (2, 3))
         for t in range(PACK):
-            nc.vector.tensor_copy(k_got[t // 2][:, t % 2, :], listed(k_raw[t], 0, QUARTER))
-            if t % 2 == 1:
-                nc.vector.tensor_copy(k_bf[0][:, :, t - 1 : t + 1], k_got[t // 2][:].rearrange("p t n -> p n t"))
-            for i in range(1, len(pieces)):
-                nc.scalar.activation(k_bf[i][:, :, t], listed(k_raw[t], *pieces[i]), COPY)
+            nc.vector.tensor_copy(k_first[:, :, t], listed(k_raw[t], 0, HALF))
+            for c in (2, 3):
+                nc.scalar.activation(k_bf[c][:, :, t], listed(k_raw[t], c * QUARTER, QUARTER), COPY)
 
         q_bf = reuse.tile([P, NQ, PACK], BF16, name="q_bf", offset=8 * T, align_bytes=64)
         nc.gpsimd.tensor_scalar(q_bf[:], q_raw[:].rearrange("p t q -> p q t"), 1.0, 0.0, MULT, ADD)
@@ -110,29 +108,25 @@ def tile_attend_x_ks_sink_topk_kernel(tc, qT, kT, vT, ks, vs, sink, offs, out):
         def quantise(codes, scales, values):
             nc.vector.quantize_mx(codes.bitcast(FP8X4), scales, values)
 
-        k_codes = [keep.tile([P, count], U32, name="k_codes%d" % i, align_bytes=64) for i, (first, count) in enumerate(pieces)]
-        k_scales = [keep.tile([P, count], U8, name="k_scales%d" % i, align_bytes=64) if i == 1 else
-                    reuse.tile([P, count], U8, name="k_scales%d" % i, offset=8 * T + first, align_bytes=64) for i, (first, count) in enumerate(pieces)]
+        k_codes = [keep.tile([P, QUARTER], U32, name="k_codes%d" % c, align_bytes=64) for c in range(4)]
+        k_scales = [keep.tile([P, QUARTER], U8, name="k_scales2", align_bytes=64) if c == 2 else
+                    reuse.tile([P, QUARTER], U8, name="k_scales%d" % c, offset=8 * T + QUARTER * c, align_bytes=64) for c in range(4)]
         scores = [bank(c, [P, QUARTER], "scores") for c in range(4)]
-        for i in (1, 0, 2, 3, 4):
-            quantise(k_codes[i][:], k_scales[i][:], k_bf[i][:].rearrange("p n t -> p (n t)"))
-            if i == 1:
-                quantise(q_codes[:], q_scales[:], q_bf[:].rearrange("p q t -> p (q t)"))
-            first, count = pieces[i]
-            nc.tensor.matmul_mx(scores[first // QUARTER][:, first % QUARTER : first % QUARTER + count],
-                                lhsT=q_codes[:].bitcast(FP8X4), lhsT_scale=q_scales[:],
-                                rhs=k_codes[i][:].bitcast(FP8X4), rhs_scale=k_scales[i][:], start=True, stop=True)
-
-        dealt = logits[:, 8 : 8 + N].rearrange("q (h g t s) -> q g h t s", h=2, g=2, t=PACK)
-        unscaled = keep.tile([P, PACK, rows], F32, name="unscaled")
-        nc.scalar.copy(unscaled[:], scores[1][:].rearrange("q (s t) -> q t s", t=PACK))
-        nc.gpsimd.tensor_tensor(dealt[:, 0, 1], unscaled[:], ks_dealt[:, 1], MULT)
-        for c in (0, 2, 3):
-            nc.vector.tensor_tensor(dealt[:, c // 2, c % 2], scores[c][:].rearrange("q (s t) -> q t s", t=PACK), ks_dealt[:, c], MULT)
+        for c in (2, 0, 1, 3):
+            quantise(k_codes[c][:], k_scales[c][:], k_bf[c].rearrange("p n t -> p (n t)"))
             if c == 2:
-                nc.vector.tensor_reduce(logits[:, N + 8 : N + 9], logits[:, 7 : 8 + HALF], AX, MAX)
+                quantise(q_codes[:], q_scales[:], q_bf[:].rearrange("p q t -> p (q t)"))
+            nc.tensor.matmul_mx(scores[c][:], lhsT=q_codes[:].bitcast(FP8X4), lhsT_scale=q_scales[:],
+                                rhs=k_codes[c][:].bitcast(FP8X4), rhs_scale=k_scales[c][:], start=True, stop=True)
+
+        dealt = logits[:, 8 : 8 + N].rearrange("q (g h t s) -> q g h t s", h=2, g=2, t=PACK)
+        unscaled = keep.tile([P, PACK, rows], F32, name="unscaled")
+        nc.scalar.copy(unscaled[:], scores[2][:].rearrange("q (s t) -> q t s", t=PACK))
+        nc.gpsimd.tensor_tensor(dealt[:, 1, 0], unscaled[:], ks_dealt[:, 2], MULT)
+        for c in (0, 1, 3):
+            nc.vector.tensor_tensor(dealt[:, c // 2, c % 2], scores[c][:].rearrange("q (s t) -> q t s", t=PACK), ks_dealt[:, c], MULT)
         m_neg = keep.tile([P, 1], F32, name="m_neg")
-        nc.vector.tensor_reduce(m_neg[:], logits[:, 8 + HALF : N + 9], AX, MAX, negate=True)
+        nc.vector.tensor_reduce(m_neg[:], logits[:, 7 : 8 + N], AX, MAX, negate=True)
 
         p = [keep.tile([P, PACK, P], F32, name="p%d" % g) for g in range(2)]
         sums = keep.tile([P, 3], F32, name="sums")
@@ -140,10 +134,12 @@ def tile_attend_x_ks_sink_topk_kernel(tc, qT, kT, vT, ks, vs, sink, offs, out):
             nc.scalar.activation(p[g][:].rearrange("q t (h s) -> q h t s", h=2), dealt[:, g], EXP, bias=m_neg[:], accum_out=sums[:, g : g + 1])
         nc.scalar.activation(sums[:, 2:3], logits[:, 7:8], EXP, bias=m_neg[:])
 
-        v_got = [[keep.tile([P, HALF], BF16, name="v_got%d%d" % (j, g)) for g in range(2)] for j in range(2)]
-        nc.vector.tensor_copy(v_got[0][0][:], listed(v_raw[0], 0, HALF))
-        nc.vector.tensor_copy(v_got[0][1][:, 0:P], listed(v_raw[0], HALF, P))
-        nc.scalar.activation(v_got[0][1][:, P:HALF], listed(v_raw[0], HALF + P, HALF - P), COPY)
+        v_first = keep.tile([P, N], BF16, name="v_first")
+        v_got = [[v_first[:, 0:HALF], v_first[:, HALF:N]], [keep.tile([P, HALF], BF16, name="v_got1%d" % g)[:] for g in range(2)]]
+        side = HALF - P // 2
+        nc.vector.tensor_copy(v_first[:, 0:side], listed(v_raw[0], 0, side))
+        nc.vector.tensor_copy(v_first[:, N - side : N], listed(v_raw[0], N - side, side))
+        nc.scalar.activation(v_first[:, side : N - side], listed(v_raw[0], side, P), COPY)
 
         def turn_values(b, got):
             words = got.bitcast(F32)
@@ -155,34 +151,40 @@ def tile_attend_x_ks_sink_topk_kernel(tc, qT, kT, vT, ks, vs, sink, offs, out):
         def interleave(dest, turned):
             nc.scalar.copy(dest.bitcast(F32).rearrange("s (x u) -> s x u", u=2), turned[:].rearrange("s u x -> s x u"))
 
-        w_bf = [keep.tile([P, NQ * PACK], BF16, name="w_bf%d" % g, align_bytes=64) for g in range(2)]
-        v_bf = [[reuse.tile([P, P * PACK], BF16, name="v_bf0%d" % g, offset=1024 * g, align_bytes=64) for g in range(2)],
+        w_bf = [keep.tile([P, NQ * PACK], BF16, name="w_bf0", align_bytes=64), reuse.tile([P, NQ * PACK], BF16, name="w_bf1", offset=4 * T + 4096, align_bytes=64)]
+        v_bf = [[keep.tile([P, P * PACK], BF16, name="v_bf00", align_bytes=64), reuse.tile([P, P * PACK], BF16, name="v_bf01", offset=4 * T + 2048, align_bytes=64)],
                 [keep.tile([P, P * PACK], BF16, name="v_bf1%d" % g, align_bytes=64) for g in range(2)]]
         w_codes = [keep.tile([P, NQ], U32, name="w_codes%d" % g, align_bytes=64) for g in range(2)]
         w_scales = [keep.tile([P, NQ], U8, name="w_scales%d" % g, align_bytes=64) for g in range(2)]
         v_codes = [[reuse.tile([P, P], U32, name="v_codes0%d" % g, offset=4 * T + 512 * g, align_bytes=64) for g in range(2)],
                    [keep.tile([P, P], U32, name="v_codes1%d" % g, align_bytes=64) for g in range(2)]]
         v_scales = [[keep.tile([P, P], U8, name="v_scales%d%d" % (j, g), align_bytes=64) for g in range(2)] for j in range(2)]
+        p_turned = [bank(4 + g, [P, PACK, NQ], "p_turned") for g in range(2)]
         for g in range(2):
-            p_turned = bank(4 + g, [P, PACK, NQ], "p_turned")
             for t in range(PACK):
-                nc.tensor.transpose(p_turned[:, t, :], p[g][:, t, :], ident[:])
-            nc.vector.tensor_tensor(w_bf[g][:].rearrange("s (q t) -> s q t", t=PACK), p_turned[:].rearrange("s t q -> s q t"),
+                nc.tensor.transpose(p_turned[g][:, t, :], p[g][:, t, :], ident[:])
+
+        def weigh(g):
+            nc.vector.tensor_tensor(w_bf[g][:].rearrange("s (q t) -> s q t", t=PACK), p_turned[g][:].rearrange("s t q -> s q t"),
                                     vs_col[g][:].unsqueeze(1).to_broadcast([P, NQ, PACK]), MULT)
-        for g in range(2):
-            interleave(v_bf[0][g][:], turn_values(4 + 2 * g, v_got[0][g][:]))
-        for g in range(2):
-            quantise(w_codes[g][:], w_scales[g][:], w_bf[g][:])
+
+        weigh(0)
+        first_turned = [turn_values(6 + g, v_got[0][g]) for g in range(2)]
+        interleave(v_bf[0][0][:], first_turned[0])
+        quantise(w_codes[0][:], w_scales[0][:], w_bf[0][:])
 
         for g in range(2):
             nc.vector.tensor_copy(v_got[1][g][:, 0:SHARE], listed(v_raw[1], g * HALF, SHARE))
             nc.scalar.activation(v_got[1][g][:, SHARE:HALF], listed(v_raw[1], g * HALF + SHARE, HALF - SHARE), COPY)
+        interleave(v_bf[0][1][:], first_turned[1])
         for g in range(2):
-            interleave(v_bf[1][g][:], turn_values(g, v_got[1][g][:]))
-        total = reuse.tile([P, 1], F32, name="total", offset=4 * T + 1024, align_bytes=64)
+            interleave(v_bf[1][g][:], turn_values(g, v_got[1][g]))
+        weigh(1)
+        quantise(v_codes[0][0][:], v_scales[0][0][:], v_bf[0][0][:])
+        total = keep.tile([P, 1], F32, name="total")
         nc.vector.tensor_reduce(total[:], sums[:], AX, ADD)
-        for g in range(2):
-            quantise(v_codes[0][g][:], v_scales[0][g][:], v_bf[0][g][:])
+        quantise(v_codes[0][1][:], v_scales[0][1][:], v_bf[0][1][:])
+        quantise(w_codes[1][:], w_scales[1][:], w_bf[1][:])
         inv = keep.tile([P, 1], F32, name="inv")
         nc.vector.reciprocal(inv[:], total[:])
         for g in range(2):

@@ -11,7 +11,7 @@ QUARTER = 256
 RUN = T // P
 PAGE = 4096
 LANES = 16
-SHARE = 288
+SHARE = 256
 
 F32 = mybir.dt.float32
 BF16 = mybir.dt.bfloat16
@@ -54,8 +54,9 @@ def tile_attend_x_ks_sink_topk_kernel(tc, qT, kT, vT, ks, vs, sink, offs, out):
         nc.vector.memset(vs_pool[0:63, 0 : T // 2], 0.0)
         nc.vector.memset(vs_pool[64:P, 0 : T // 2], 0.0)
         nc.vector.memset(vs_pool[0 : P - 1, T // 2 : T], 0.0)
-        logits = keep.tile([P, N + 16], F32, name="logits")
-        nc.scalar.dma_start(logits[:, 7:8], sink.rearrange("b q o -> (b q) o"))
+        sink_row = keep.tile([P, NQ], F32, name="sink_row")
+        nc.scalar.dma_start(sink_row[P - 1 : P, :], sink.rearrange("b q o -> b (q o)"))
+        nc.gpsimd.memset(sink_row[0 : P - 1, :], 0.0)
         for t in range(1, PACK):
             nc.sync.dma_start(k_raw[t][:], k_rows[:, t, :])
         q_raw = keep.tile([P, PACK, NQ], F32, name="q_raw")
@@ -91,6 +92,11 @@ def tile_attend_x_ks_sink_topk_kernel(tc, qT, kT, vT, ks, vs, sink, offs, out):
             for t in range(PACK):
                 nc.tensor.transpose(turned[:, t, :], vs_got[:, g * HALF + t : (g + 1) * HALF : PACK], ident[:])
             nc.vector.tensor_reduce(vs_col[g][:], turned[:, :, 63::64], AX, ADD)
+
+        logits = keep.tile([P, N + 16], F32, name="logits")
+        turned = bank(3, [P, P], "sink_turned")
+        nc.tensor.transpose(turned[:], sink_row[:], ident[:])
+        nc.vector.tensor_copy(logits[:, 7:8], turned[:, P - 1 : P])
 
         k_first = keep.tile([P, HALF, PACK], BF16, name="k_first", align_bytes=64)
         k_bf = [k_first[:, 0:QUARTER, :], k_first[:, QUARTER:HALF, :]]

from contextlib import ExitStack

import concourse.mybir as mybir
from concourse.masks import make_identity

D, T, N, DV, NQ = 512, 4096, 1024, 256, 128
P = 128
PACK = 4
HALF = 512
QUARTER = 256
RUN = T // P
PAGE = 4096
LANES = 16
SHARE = 256

F32 = mybir.dt.float32
BF16 = mybir.dt.bfloat16
U32 = mybir.dt.uint32
U16 = mybir.dt.uint16
U8 = mybir.dt.uint8
FP8X4 = mybir.dt.float8_e4m3fn_x4
MULT = mybir.AluOpType.mult
ADD = mybir.AluOpType.add
MAX = mybir.AluOpType.max
AX = mybir.AxisListType.X
COPY = mybir.ActivationFunctionType.Copy
EXP = mybir.ActivationFunctionType.Exp

FLOPS = 2 * NQ * N * (D + DV)
BYTES = 4 * (D * T + DV * T + D * NQ + 2 * T + NQ + NQ * DV) + 2 * 128 * 64


def tile_attend_x_ks_sink_topk_kernel(tc, qT, kT, vT, ks, vs, sink, offs, out):
    nc = tc.nc
    with ExitStack() as ctx:
        keep = ctx.enter_context(tc.tile_pool(name="keep", bufs=1))
        reuse = ctx.enter_context(tc.tile_pool(name="reuse", bufs=1))
        psum = ctx.enter_context(tc.psum_pool(name="psum", bufs=1))

        def bank(b, shape, name):
            return psum.tile(shape, F32, name=name, tag="bank%d" % b)

        k_rows = kT.rearrange("(p t) n -> p t n", t=PACK)
        k_raw = [keep.tile([P, T], F32, name="k_raw%d" % t, align_bytes=PAGE) for t in range(PACK)]
        v_raw = [reuse.tile([P, T], F32, name="v_raw%d" % j, offset=4 * T * j, align_bytes=PAGE) for j in range(DV // P)]
        ks_run = keep.tile([P, RUN], F32, name="ks_run")
        nc.scalar.dma_start(ks_run[:], ks[0:1, :].rearrange("o (p c) -> (o p) c", c=RUN))
        vs_pool = keep.tile([P, T], F32, name="vs_pool")
        nc.scalar.dma_start(vs_pool[P - 1 : P, T // 2 : T], vs[0:1, T // 2 : T])
        nc.sync.dma_start(vs_pool[63:64, 0 : T // 2], vs[0:1, 0 : T // 2])
        nc.sync.dma_start(k_raw[0][:], k_rows[:, 0, :])
        offsets = keep.tile([P, N // LANES], U16, name="offsets")
        nc.sync.dma_start(offsets[:], offs)
        nc.vector.memset(vs_pool[0:63, 0 : T // 2], 0.0)
        nc.vector.memset(vs_pool[64:P, 0 : T // 2], 0.0)
        nc.vector.memset(vs_pool[0 : P - 1, T // 2 : T], 0.0)
        sink_row = keep.tile([P, NQ], F32, name="sink_row")
        nc.scalar.dma_start(sink_row[P - 1 : P, :], sink.rearrange("b q o -> b (q o)"))
        nc.gpsimd.memset(sink_row[0 : P - 1, :], 0.0)
        for t in range(1, PACK):
            nc.sync.dma_start(k_raw[t][:], k_rows[:, t, :])
        q_raw = keep.tile([P, PACK, NQ], F32, name="q_raw")
        nc.sync.dma_start(q_raw[:], qT.rearrange("b (p t) q -> p (b t) q", t=PACK))
        for j in range(DV // P):
            nc.sync.dma_start(v_raw[j][:], vT[j * P : (j + 1) * P, :])

        def listed(pool, first, count):
            return pool[:].indirect(offsets[:, first // LANES : (first + count) // LANES])

        ident = keep.tile([P, P], F32, name="ident")
        make_identity(nc, ident[:])

        ks_pool = keep.tile([P, T], F32, name="ks_pool")
        by_run = ks_pool[:].rearrange("r (p c) -> r p c", c=RUN)
        for b in range(RUN // 4):
            turned = bank(b % 4, [P, 4, P], "spread")
            for c in range(4):
                nc.tensor.transpose(turned[:, c, :], ks_run[:, 4 * b + c : 4 * b + c + 1].to_broadcast([P, P]), ident[:])
            nc.scalar.activation(by_run[:, :, 4 * b : 4 * b + 4], turned[:].rearrange("r c p -> r p c"), COPY)

        rows = QUARTER // PACK
        ks_got = keep.tile([P, N], F32, name="ks_got")
        nc.vector.tensor_copy(ks_got[:], listed(ks_pool, 0, N))
        ks_dealt = keep.tile([P, 4, PACK, rows], F32, name="ks_dealt")
        nc.vector.tensor_copy(ks_dealt[:], ks_got[:].rearrange("q (c s t) -> q c t s", t=PACK, c=4))

        vs_got = keep.tile([P, N], F32, name="vs_got")
        nc.vector.tensor_copy(vs_got[:], listed(vs_pool, 0, N))
        vs_col = [keep.tile([P, PACK], F32, name="vs_col%d" % g) for g in range(2)]
        for g in range(2):
            turned = bank(2 + g, [P, PACK, P], "vs_turned")
            for t in range(PACK):
                nc.tensor.transpose(turned[:, t, :], vs_got[:, g * HALF + t : (g + 1) * HALF : PACK], ident[:])
            nc.vector.tensor_reduce(vs_col[g][:], turned[:, :, 63::64], AX, ADD)

        logits = keep.tile([P, N + 16], F32, name="logits")
        turned = bank(3, [P, P], "sink_turned")
        nc.tensor.transpose(turned[:], sink_row[:], ident[:])
        nc.vector.tensor_copy(logits[:, 7:8], turned[:, P - 1 : P])

        k_first = keep.tile([P, HALF, PACK], BF16, name="k_first", align_bytes=64)
        k_bf = [k_first[:, 0:QUARTER, :], k_first[:, QUARTER:HALF, :]]
        k_bf.extend(keep.tile([P, QUARTER, PACK], BF16, name="k_bf%d" % c, align_bytes=64)[:] for c in (2, 3))
        for t in range(PACK):
            nc.vector.tensor_copy(k_first[:, :, t], listed(k_raw[t], 0, HALF))
            for c in (2, 3):
                nc.scalar.activation(k_bf[c][:, :, t], listed(k_raw[t], c * QUARTER, QUARTER), COPY)

        q_bf = reuse.tile([P, NQ, PACK], BF16, name="q_bf", offset=8 * T, align_bytes=64)
        nc.gpsimd.tensor_scalar(q_bf[:], q_raw[:].rearrange("p t q -> p q t"), 1.0, 0.0, MULT, ADD)
        q_codes = keep.tile([P, NQ], U32, name="q_codes", align_bytes=64)
        q_scales = keep.tile([P, NQ], U8, name="q_scales", align_bytes=64)

        def quantise(codes, scales, values):
            nc.vector.quantize_mx(codes.bitcast(FP8X4), scales, values)

        k_codes = [keep.tile([P, QUARTER], U32, name="k_codes%d" % c, align_bytes=64) for c in range(4)]
        k_scales = [keep.tile([P, QUARTER], U8, name="k_scales2", align_bytes=64) if c == 2 else
                    reuse.tile([P, QUARTER], U8, name="k_scales%d" % c, offset=8 * T + QUARTER * c, align_bytes=64) for c in range(4)]
        scores = [bank(c, [P, QUARTER], "scores") for c in range(4)]
        for c in (2, 0, 1, 3):
            quantise(k_codes[c][:], k_scales[c][:], k_bf[c].rearrange("p n t -> p (n t)"))
            if c == 2:
                quantise(q_codes[:], q_scales[:], q_bf[:].rearrange("p q t -> p (q t)"))
            nc.tensor.matmul_mx(scores[c][:], lhsT=q_codes[:].bitcast(FP8X4), lhsT_scale=q_scales[:],
                                rhs=k_codes[c][:].bitcast(FP8X4), rhs_scale=k_scales[c][:], start=True, stop=True)

        dealt = logits[:, 8 : 8 + N].rearrange("q (g h t s) -> q g h t s", h=2, g=2, t=PACK)
        unscaled = keep.tile([P, PACK, rows], F32, name="unscaled")
        nc.scalar.copy(unscaled[:], scores[2][:].rearrange("q (s t) -> q t s", t=PACK))
        nc.gpsimd.tensor_tensor(dealt[:, 1, 0], unscaled[:], ks_dealt[:, 2], MULT)
        for c in (0, 1, 3):
            nc.vector.tensor_tensor(dealt[:, c // 2, c % 2], scores[c][:].rearrange("q (s t) -> q t s", t=PACK), ks_dealt[:, c], MULT)
        m_neg = keep.tile([P, 1], F32, name="m_neg")
        nc.vector.tensor_reduce(m_neg[:], logits[:, 7 : 8 + N], AX, MAX, negate=True)

        p = [keep.tile([P, PACK, P], F32, name="p%d" % g) for g in range(2)]
        sums = keep.tile([P, 3], F32, name="sums")
        for g in range(2):
            nc.scalar.activation(p[g][:].rearrange("q t (h s) -> q h t s", h=2), dealt[:, g], EXP, bias=m_neg[:], accum_out=sums[:, g : g + 1])
        nc.scalar.activation(sums[:, 2:3], logits[:, 7:8], EXP, bias=m_neg[:])

        v_first = keep.tile([P, N], BF16, name="v_first")
        v_got = [[v_first[:, 0:HALF], v_first[:, HALF:N]], [keep.tile([P, HALF], BF16, name="v_got1%d" % g)[:] for g in range(2)]]
        side = HALF - P // 2
        nc.vector.tensor_copy(v_first[:, 0:side], listed(v_raw[0], 0, side))
        nc.vector.tensor_copy(v_first[:, N - side : N], listed(v_raw[0], N - side, side))
        nc.scalar.activation(v_first[:, side : N - side], listed(v_raw[0], side, P), COPY)

        def turn_values(b, got):
            words = got.bitcast(F32)
            turned = bank(b, [P, 2, P], "pairs_turned")
            for u in range(2):
                nc.tensor.transpose(turned[:, u, :], words[:, u : HALF // 2 : 2], ident[:])
            return turned

        def interleave(dest, turned):
            nc.scalar.copy(dest.bitcast(F32).rearrange("s (x u) -> s x u", u=2), turned[:].rearrange("s u x -> s x u"))

        w_bf = [keep.tile([P, NQ * PACK], BF16, name="w_bf0", align_bytes=64), reuse.tile([P, NQ * PACK], BF16, name="w_bf1", offset=4 * T + 4096, align_bytes=64)]
        v_bf = [[keep.tile([P, P * PACK], BF16, name="v_bf00", align_bytes=64), reuse.tile([P, P * PACK], BF16, name="v_bf01", offset=4 * T + 2048, align_bytes=64)],
                [keep.tile([P, P * PACK], BF16, name="v_bf1%d" % g, align_bytes=64) for g in range(2)]]
        w_codes = [keep.tile([P, NQ], U32, name="w_codes%d" % g, align_bytes=64) for g in range(2)]
        w_scales = [keep.tile([P, NQ], U8, name="w_scales%d" % g, align_bytes=64) for g in range(2)]
        v_codes = [[reuse.tile([P, P], U32, name="v_codes0%d" % g, offset=4 * T + 512 * g, align_bytes=64) for g in range(2)],
                   [keep.tile([P, P], U32, name="v_codes1%d" % g, align_bytes=64) for g in range(2)]]
        v_scales = [[keep.tile([P, P], U8, name="v_scales%d%d" % (j, g), align_bytes=64) for g in range(2)] for j in range(2)]
        p_turned = [bank(4 + g, [P, PACK, NQ], "p_turned") for g in range(2)]
        for g in range(2):
            for t in range(PACK):
                nc.tensor.transpose(p_turned[g][:, t, :], p[g][:, t, :], ident[:])

        def weigh(g):
            nc.vector.tensor_tensor(w_bf[g][:].rearrange("s (q t) -> s q t", t=PACK), p_turned[g][:].rearrange("s t q -> s q t"),
                                    vs_col[g][:].unsqueeze(1).to_broadcast([P, NQ, PACK]), MULT)

        weigh(0)
        first_turned = [turn_values(6 + g, v_got[0][g]) for g in range(2)]
        interleave(v_bf[0][0][:], first_turned[0])
        quantise(w_codes[0][:], w_scales[0][:], w_bf[0][:])

        for g in range(2):
            nc.vector.tensor_copy(v_got[1][g][:, 0:SHARE], listed(v_raw[1], g * HALF, SHARE))
            nc.scalar.activation(v_got[1][g][:, SHARE:HALF], listed(v_raw[1], g * HALF + SHARE, HALF - SHARE), COPY)
        interleave(v_bf[0][1][:], first_turned[1])
        for g in range(2):
            interleave(v_bf[1][g][:], turn_values(g, v_got[1][g]))
        weigh(1)
        quantise(v_codes[0][0][:], v_scales[0][0][:], v_bf[0][0][:])
        total = keep.tile([P, 1], F32, name="total")
        nc.vector.tensor_reduce(total[:], sums[:], AX, ADD)
        quantise(v_codes[0][1][:], v_scales[0][1][:], v_bf[0][1][:])
        quantise(w_codes[1][:], w_scales[1][:], w_bf[1][:])
        inv = keep.tile([P, 1], F32, name="inv")
        nc.vector.reciprocal(inv[:], total[:])
        for g in range(2):
            quantise(v_codes[1][g][:], v_scales[1][g][:], v_bf[1][g][:])

        y_out = out.rearrange("b q e -> (b q) e")
        y = [keep.tile([P, P], F32, name="y%d" % j) for j in range(2)]
        for j in range(DV // P):
            acc = bank(2 + j, [P, P], "acc")
            for g in range(2):
                nc.tensor.matmul_mx(acc[:], lhsT=w_codes[g][:].bitcast(FP8X4), lhsT_scale=w_scales[g][:],
                                    rhs=v_codes[j][g][:].bitcast(FP8X4), rhs_scale=v_scales[j][g][:], start=(g == 0), stop=(g == 1))
            if j == 0:
                nc.scalar.activation(y[j][:], acc[:], COPY, scale=inv[:])
            else:
                nc.vector.tensor_scalar(y[j][:], acc[:], inv[:], None, MULT)
            nc.sync.dma_start(y_out[:, j * P : (j + 1) * P], y[j][:])
